import numpy as np
import ml_dtypes


def mxq(x, axis, fmt="e4m3"):
    dtype, down = {"e4m3": (ml_dtypes.float8_e4m3fn, 7), "e5m2": (ml_dtypes.float8_e5m2, 14)}[fmt]
    v = np.moveaxis(np.asarray(x, np.float32).astype(ml_dtypes.bfloat16).astype(np.float64), axis, -1)
    blocks = v.reshape(v.shape[:-1] + (-1, 32))
    amax = np.abs(blocks).max(-1, keepdims=True)
    byte = np.maximum(np.where(amax > 0, np.frexp(amax)[1] - 1 + 127, 0) - down, 1)
    scale = np.exp2(byte - 127.0)
    codes = (blocks / scale).astype(np.float32).astype(dtype).astype(np.float64)
    return np.moveaxis((codes * scale).reshape(v.shape), -1, axis)


WIDE = False


def mx_kscale(k):
    if not WIDE:
        return np.ones(k)
    levels = np.array([18, -18])
    if k % 512:
        return np.exp2(np.random.permutation(np.resize(levels, k // 32))).repeat(32)
    a = np.empty((k // 512, 16))
    for p in range(k // 512):
        a[p, :8] = np.random.permutation(np.resize(levels, 8))
        for g in range(8):
            far = levels[np.abs(levels - a[p, g]) >= 10]
            a[p, g + 8] = far[np.random.randint(len(far))]
    return np.exp2(a.ravel()).repeat(32)


def f64(x):
    return np.asarray(x).astype(np.float64)


def striped(idx):
    return np.tile(np.asarray(idx).reshape(-1, 16).T, (8, 1)).astype(np.uint16)


def unstriped(offs):
    return offs[:16].T.reshape(-1).astype(np.int64)


def setup_inputs():
    n = np.random.standard_normal
    uni = np.random.uniform
    idx = np.random.permutation(2048)[:512]
    f_d = mx_kscale(512)
    f_r = mx_kscale(512)
    return {
        "q1": (0.5 * n((512, 512)) * f_d[:, None] * f_r[None, :]).astype(np.float32),
        "q2": (0.5 * n((512, 512)) * f_d[:, None] * f_r[None, :]).astype(np.float32),
        "kT": (n((512, 2048)) / np.sqrt(512) / f_d[:, None]).astype(np.float32),
        "dp1": (n((512, 512))).astype(np.float32),
        "dp2": (n((512, 512))).astype(np.float32),
        "us": (uni(0.75, 1.3, (512, 1)) / f_r[:, None]).astype(np.float32),
        "ts": np.tile(uni(0.75, 1.3, 2048), (128, 1)).astype(np.float32),
        "w1": (uni(0.75, 1.3, (512, 1)) / np.sqrt(512)).astype(np.float32),
        "w2": (uni(0.75, 1.3, (512, 1)) / np.sqrt(512)).astype(np.float32),
        "offs": striped(idx),
    }


def reference(q1, q2, kT, dp1, dp2, us, ts, w1, w2, offs):
    idx = unstriped(offs)
    kT_i = f64(kT)[:, idx]
    ts_i = f64(ts)[:1][:, idx]
    q_kT_i = mxq(kT_i, 0, "e4m3")
    a1 = mxq(f64(q1), 0, "e4m3").T @ q_kT_i
    z1 = f64(us) * ts_i * a1
    m1 = (z1).max(-1, keepdims=True)
    e1 = np.exp(z1 - m1)
    t1 = (e1).sum(-1, keepdims=True)
    p1 = e1 / t1
    c1 = (p1 * f64(dp1)).sum(-1, keepdims=True)
    g1 = f64(w1) * f64(us) * ts_i * p1 * (f64(dp1) - c1)
    a2 = mxq(f64(q2), 0, "e4m3").T @ q_kT_i
    z2 = f64(us) * ts_i * a2
    m2 = (z2).max(-1, keepdims=True)
    e2 = np.exp(z2 - m2)
    t2 = (e2).sum(-1, keepdims=True)
    p2 = e2 / t2
    c2 = (p2 * f64(dp2)).sum(-1, keepdims=True)
    g2 = f64(w2) * f64(us) * ts_i * p2 * (f64(dp2) - c2)
    k1 = mxq(f64(q1), 1, "e4m3") @ mxq(g1, 0, "e5m2")
    k2 = mxq(f64(q2), 1, "e4m3") @ mxq(g2, 0, "e5m2")
    dk = k1 + k2
    out = np.zeros((512, 2048))
    out[:, idx] = dk
    return out

@@ -1,0 +1,266 @@
+from contextlib import ExitStack
+
+import concourse.mybir as mybir
+from concourse.masks import make_identity
+
+F32 = mybir.dt.float32
+BF16 = mybir.dt.bfloat16
+U32 = mybir.dt.uint32
+U16 = mybir.dt.uint16
+U8 = mybir.dt.uint8
+E4M3 = mybir.dt.float8_e4m3fn_x4
+E5M2 = mybir.dt.float8_e5m2_x4
+ALU = mybir.AluOpType
+ACT = mybir.ActivationFunctionType
+
+P = 128
+PACK = 4
+D = 512
+R = 512
+SLOTS = 512
+TOKENS = 2048
+HALF = SLOTS // 2
+RUN = TOKENS // P
+FLOPS = 4 * 2 * D * R * SLOTS
+H_ON_GPSIMD = False
+
+
+def tile_attend_ggqa_sm_k_kernel(tc, q1, q2, kT, dp1, dp2, us, ts, w1, w2, offs, out):
+    nc = tc.nc
+    with ExitStack() as ctx:
+        keep = ctx.enter_context(tc.tile_pool(name="keep", bufs=1))
+        ring = ctx.enter_context(tc.tile_pool(name="ring", bufs=3))
+        psum = ctx.enter_context(tc.psum_pool(name="psum", bufs=1))
+
+        def held(shape, dtype, name):
+            return keep.tile(shape, dtype, name=name, align_bytes=64)
+
+        offsets = keep.tile([P, SLOTS // 16], U16, name="offsets")
+        nc.sync.dma_start(offsets[:], offs)
+
+        q_raw = [held([P, PACK, R], F32, f"q_raw{h}") for h in range(2)]
+        dp_sb = [held([P, PACK, SLOTS], F32, f"dp_sb{h}") for h in range(2)]
+        k_raw = [held([P, TOKENS], F32, f"k_raw{j}") for j in range(PACK)]
+        us_sb = held([P, PACK], F32, "us_sb")
+        w_sb = [held([P, PACK], F32, f"w_sb{h}") for h in range(2)]
+        ts_win = held([P, TOKENS], F32, "ts_win")
+        ident = held([P, P], F32, "ident")
+
+        make_identity(nc, ident[:])
+        warm = held([P, 1], F32, "warm")
+        warm_out = held([P, 1], F32, "warm_out")
+        nc.vector.memset(warm[:], 0.0)
+        nc.scalar.activation(warm_out[:], warm[:], ACT.Exp)
+
+        ts_runs = held([P, RUN], F32, "ts_runs")
+        nc.sync.dma_start(ts_runs[:], ts[0:1, :].rearrange("o (p c) -> p (o c)", c=RUN))
+        nc.sync.dma_start(q_raw[0][:], q1.rearrange("(p j) r -> p j r", j=PACK))
+        k_planes = kT.rearrange("(p j) t -> j p t", j=PACK)
+        for j in range(PACK):
+            nc.sync.dma_start(k_raw[j][:], k_planes[j])
+        nc.sync.dma_start(us_sb[:], us.rearrange("(s t) o -> s (t o)", t=PACK))
+        for h, w in enumerate((w1, w2)):
+            nc.sync.dma_start(w_sb[h][:], w.rearrange("(s t) o -> s (t o)", t=PACK))
+        nc.sync.dma_start(q_raw[1][:], q2.rearrange("(p j) r -> p j r", j=PACK))
+        for h, dp in enumerate((dp1, dp2)):
+            nc.sync.dma_start(dp_sb[h][:], dp.rearrange("(s t) i -> s t i", t=PACK))
+
+        windows = [held([P, TOKENS], F32, f"window{j}") for j in range(PACK)]
+        for j in range(PACK):
+            (nc.vector if j < 2 else nc.gpsimd).memset(windows[j][:], 0.0)
+
+        for g in range(RUN // PACK):
+            bank = psum.tile([P, PACK, P], F32, name="spread", tag="scores", bufs=3)
+            for c in range(PACK):
+                nc.tensor.transpose(bank[:, c, :], ts_runs[:, PACK * g + c : PACK * g + c + 1].to_broadcast([P, P]), ident[:])
+            copy = nc.scalar.copy if g % 2 == 0 else nc.vector.tensor_copy
+            copy(ts_win[:].rearrange("m (p c) -> m p c", c=RUN)[:, :, PACK * g : PACK * (g + 1)], bank[:].rearrange("m c p -> m p c"))
+
+        def quantise(source, fmt, codes, scales):
+            nc.vector.quantize_mx(out=codes.bitcast(fmt), scales=scales, in_=source)
+
+        q_woven = [held([P, R, PACK], BF16, f"q_woven{h}") for h in range(2)]
+        qd_codes = [held([P, R], U32, f"qd_codes{h}") for h in range(2)]
+        qd_scales = [held([P, R], U8, f"qd_scales{h}") for h in range(2)]
+        qr_woven = [held([P, PACK, P, PACK], BF16, f"qr_woven{h}") for h in range(2)]
+        qr_codes = [held([P, D], U32, f"qr_codes{h}") for h in range(2)]
+        qr_scales = [held([P, D], U8, f"qr_scales{h}") for h in range(2)]
+
+        def weave_queries(h, copy):
+            copy(q_woven[h][:].rearrange("p (c i) j -> p c j i", i=4),
+                 q_raw[h][:].rearrange("p j (c i) -> p c j i", i=4))
+
+        def quantise_queries_along_d(h):
+            quantise(q_woven[h][:].rearrange("p r j -> p (r j)"), E4M3, qd_codes[h][:], qd_scales[h][:])
+
+        def turn_queries(h):
+            words = q_woven[h][:].rearrange("p r j -> p (r j)").bitcast(F32)
+            for u in range(2):
+                bank = psum.tile([P, PACK, P], F32, name="turned", tag="turned", bufs=2)
+                for t in range(PACK):
+                    nc.tensor.transpose(bank[:, t, :], words[:, 2 * t + u :: 2 * PACK], ident[:])
+                halves = bank[:].rearrange("s t p -> s (t p)").bitcast(BF16)
+                nc.scalar.copy(qr_woven[h][:, 2 * u : 2 * u + 2, :, :],
+                               halves.rearrange("s (t p e) -> s e p t", t=PACK, e=2))
+
+        def quantise_queries_along_r(h):
+            quantise(qr_woven[h][:].rearrange("s j p t -> s (j p t)"), E4M3, qr_codes[h][:], qr_scales[h][:])
+
+        weave_queries(0, nc.scalar.copy)
+        quantise_queries_along_d(0)
+        turn_queries(0)
+
+        ts_slots = held([P, SLOTS], F32, "ts_slots")
+        nc.vector.tensor_copy(ts_slots[:], ts_win[:].indirect(offsets[:]))
+        ts_turned = psum.tile([P, PACK, P], F32, name="ts_turned", tag="scores", bufs=3)
+        for b in range(PACK):
+            nc.tensor.transpose(ts_turned[:, b, :], ts_slots[:, b * P : (b + 1) * P], ident[:])
+        ts_cols = held([P, PACK], F32, "ts_cols")
+        nc.scalar.copy(ts_cols[:], ts_turned[:, :, 0])
+        ts_rows = psum.tile([P, SLOTS], F32, name="ts_rows")
+        for b in range(PACK):
+            nc.tensor.transpose(ts_rows[:, b * P : (b + 1) * P], ts_cols[:, b : b + 1].to_broadcast([P, P]), ident[:])
+
+        k_woven = [held([P, HALF, PACK], BF16, f"k_woven{a}") for a in range(2)]
+        k_codes = [held([P, HALF], U32, f"k_codes{a}") for a in range(2)]
+        k_scales = [held([P, HALF], U8, f"k_scales{a}") for a in range(2)]
+        cols = HALF // 16
+        for j in range(PACK):
+            for a in range(2):
+                nc.vector.tensor_copy(k_woven[a][:, :, j], k_raw[j][:].indirect(offsets[:, a * cols : (a + 1) * cols]))
+            if j == 1:
+                quantise_queries_along_r(0)
+        for a in range(2):
+            quantise(k_woven[a][:].rearrange("p i j -> p (i j)"), E4M3, k_codes[a][:], k_scales[a][:])
+
+        neg_us = held([P, PACK], F32, "neg_us")
+        nc.vector.tensor_scalar(neg_us[:], us_sb[:], -1.0, None, ALU.mult)
+        gate = [held([P, PACK], F32, f"gate{h}") for h in range(2)]
+        neg_gate = [held([P, PACK], F32, f"neg_gate{h}") for h in range(2)]
+        for h in range(2):
+            nc.vector.tensor_tensor(gate[h][:], w_sb[h][:], us_sb[:], ALU.mult)
+            nc.vector.tensor_tensor(neg_gate[h][:], w_sb[h][:], neg_us[:], ALU.mult)
+
+        scaled = [[held([P, PACK, P], F32, f"scaled{h}_{b}") for b in range(PACK)] for h in range(2)]
+
+        def score_block(h, b, on_vector):
+            a, c = divmod(b, 2)
+            bank = psum.tile([P, R], F32, name="scores", tag="scores", bufs=3)
+            nc.tensor.matmul_mx(out=bank[:], lhsT=k_codes[a][:, c * P : (c + 1) * P].bitcast(E4M3),
+                                lhsT_scale=k_scales[a][:, c * P : (c + 1) * P],
+                                rhs=qd_codes[h][:].bitcast(E4M3), rhs_scale=qd_scales[h][:], start=True, stop=True)
+            dealt = bank[:].rearrange("i (s t) -> i t s", t=PACK)
+            if on_vector:
+                nc.vector.tensor_scalar(scaled[h][b][:], dealt, ts_cols[:, b : b + 1], None, ALU.mult)
+            else:
+                nc.scalar.activation(scaled[h][b][:], dealt, ACT.Copy, scale=ts_cols[:, b : b + 1])
+
+        grad = [held([P, PACK, SLOTS], F32, f"grad{h}") for h in range(2)]
+        g_woven = [[held([P, HALF, PACK], BF16, f"g_woven{h}_{a}") for a in range(2)] for h in range(2)]
+        g_codes = [held([P, SLOTS], U32, f"g_codes{h}") for h in range(2)]
+        g_scales = [held([P, SLOTS], U8, f"g_scales{h}") for h in range(2)]
+        state = {}
+
+        def column(name):
+            return ring.tile([P, 1], F32, name=name, tag=name, bufs=4)
+
+        def stage_max(h, t):
+            rows = psum.tile([P, SLOTS], F32, name="rows", tag="rows", bufs=2)
+            for b in range(PACK):
+                nc.tensor.transpose(rows[:, b * P : (b + 1) * P], scaled[h][b][:, t, :], ident[:])
+            neg_z = ring.tile([P, SLOTS], F32, name="neg_z")
+            neg_max = column("neg_max")
+            nc.vector.tensor_scalar(neg_z[:], rows[:], neg_us[:, t : t + 1], None, ALU.mult, ALU.min, accum_out=neg_max[:])
+            e = ring.tile([P, SLOTS], F32, name="e", bufs=4)
+            total = column("total")
+            nc.scalar.activation(e[:], neg_z[:], ACT.Exp, bias=neg_max[:], scale=-1.0, accum_out=total[:])
+            state[h, t] = (e, total)
+
+        def stage_inverse(h, t):
+            e, total = state[h, t]
+            inv = column("inv")
+            nc.vector.reciprocal(inv[:], total[:])
+            state[h, t] = (e, inv)
+
+        def stage_factors(h, t):
+            e, inv = state[h, t]
+            mean_factor = column("mean_factor")
+            nc.vector.tensor_scalar(mean_factor[:], inv[:], neg_gate[h][:, t : t + 1], inv[:], ALU.mult, ALU.mult)
+            coef = column("coef")
+            nc.scalar.activation(coef[:], inv[:], ACT.Copy, scale=gate[h][:, t : t + 1])
+            state[h, t] = (e, mean_factor, coef)
+
+        def stage_mean(h, t):
+            e, mean_factor, coef = state[h, t]
+            products = ring.tile([P, SLOTS], F32, name="products", bufs=2)
+            shift = column("shift")
+            nc.vector.scalar_tensor_tensor(products[:], e[:], mean_factor[:], dp_sb[h][:, t, :], ALU.mult, ALU.mult,
+                                           accum_out=shift[:])
+            centred = ring.tile([P, SLOTS], F32, name="centred")
+            nc.scalar.activation(centred[:], dp_sb[h][:, t, :], ACT.Identity, bias=shift[:], scale=coef[:])
+            state[h, t] = (e, centred)
+
+        def stage_grad(h, t):
+            e, centred = state[h, t]
+            engine = nc.gpsimd if H_ON_GPSIMD and (h, t) != (1, PACK - 1) else nc.vector
+            engine.tensor_tensor(grad[h][:, t, :], centred[:], e[:], ALU.mult)
+
+        def finish_head(h):
+            for a in range(2):
+                slots = slice(a * HALF, (a + 1) * HALF)
+                factors = ts_rows[:, slots].rearrange("p (c i) -> p c i", i=4).unsqueeze(2).to_broadcast([P, HALF // 4, PACK, 4])
+                nc.vector.tensor_tensor(g_woven[h][a][:].rearrange("p (c i) t -> p c t i", i=4),
+                                        grad[h][:, :, slots].rearrange("p t (c i) -> p c t i", i=4), factors, ALU.mult)
+            for a in range(2):
+                slots = slice(a * HALF, (a + 1) * HALF)
+                quantise(g_woven[h][a][:].rearrange("p i t -> p (i t)"), E5M2, g_codes[h][:, slots], g_scales[h][:, slots])
+
+        sums = {}
+
+        def key_gradient_pass(j, h):
+            feats = slice(j * P, (j + 1) * P)
+            nc.tensor.matmul_mx(out=sums[j][:], lhsT=qr_codes[h][:, feats].bitcast(E4M3), lhsT_scale=qr_scales[h][:, feats],
+                                rhs=g_codes[h][:].bitcast(E5M2), rhs_scale=g_scales[h][:], start=(h == 0), stop=(h == 1))
+
+        for b in range(PACK):
+            score_block(0, b, False)
+        weave_queries(1, nc.vector.tensor_copy)
+        quantise_queries_along_d(1)
+
+        tiles = [(h, t) for h in range(2) for t in range(PACK)]
+        last = len(tiles)
+        for n in range(last + 2):
+            if 1 <= n <= last:
+                stage_inverse(*tiles[n - 1])
+            if n < last:
+                stage_max(*tiles[n])
+            if 1 <= n <= last:
+                stage_factors(*tiles[n - 1])
+            if n < PACK:
+                score_block(1, n, False)
+            if 2 <= n <= last:
+                stage_grad(*tiles[n - 2])
+            if 1 <= n <= last:
+                stage_mean(*tiles[n - 1])
+            if n == PACK:
+                turn_queries(1)
+            if n == last:
+                quantise_queries_along_r(1)
+                finish_head(0)
+                for j in range(2):
+                    sums[j] = psum.tile([P, SLOTS], F32, name="sums", tag="turned", bufs=2)
+                    key_gradient_pass(j, 0)
+            if n == last + 1:
+                stage_grad(*tiles[n - 2])
+        finish_head(1)
+
+        out_planes = out.rearrange("(p j) c -> j p c", j=PACK)
+        for j in range(PACK):
+            if j >= 2:
+                sums[j] = psum.tile([P, SLOTS], F32, name="late_sums", tag="scores", bufs=3)
+                key_gradient_pass(j, 0)
+            key_gradient_pass(j, 1)
+            dk = held([P, SLOTS], F32, f"dk{j}")
+            nc.scalar.copy(dk[:], sums[j][:])
+            nc.vector.tensor_copy(windows[j][:].indirect(offsets[:]), dk[:])
+            nc.sync.dma_start(out_planes[j], windows[j][:])

@@ -6,6 +6,7 @@ from concourse.masks import make_identity
 F32 = mybir.dt.float32
 BF16 = mybir.dt.bfloat16
 U32 = mybir.dt.uint32
+I32 = mybir.dt.int32
 U16 = mybir.dt.uint16
 U8 = mybir.dt.uint8
 E4M3 = mybir.dt.float8_e4m3fn_x4
@@ -22,7 +23,6 @@ TOKENS = 2048
 HALF = SLOTS // 2
 RUN = TOKENS // P
 FLOPS = 4 * 2 * D * R * SLOTS
-H_ON_GPSIMD = False
 
 
 def tile_attend_ggqa_sm_k_kernel(tc, q1, q2, kT, dp1, dp2, us, ts, w1, w2, offs, out):
@@ -58,16 +58,16 @@ def tile_attend_ggqa_sm_k_kernel(tc, q1, q2, kT, dp1, dp2, us, ts, w1, w2, offs,
         k_planes = kT.rearrange("(p j) t -> j p t", j=PACK)
         for j in range(PACK):
             nc.sync.dma_start(k_raw[j][:], k_planes[j])
-        nc.sync.dma_start(us_sb[:], us.rearrange("(s t) o -> s (t o)", t=PACK))
+        nc.scalar.dma_start(us_sb[:], us.rearrange("(s t) o -> s (t o)", t=PACK))
         for h, w in enumerate((w1, w2)):
-            nc.sync.dma_start(w_sb[h][:], w.rearrange("(s t) o -> s (t o)", t=PACK))
+            nc.scalar.dma_start(w_sb[h][:], w.rearrange("(s t) o -> s (t o)", t=PACK))
         nc.sync.dma_start(q_raw[1][:], q2.rearrange("(p j) r -> p j r", j=PACK))
         for h, dp in enumerate((dp1, dp2)):
             nc.sync.dma_start(dp_sb[h][:], dp.rearrange("(s t) i -> s t i", t=PACK))
 
-        windows = [held([P, TOKENS], F32, f"window{j}") for j in range(PACK)]
-        for j in range(PACK):
-            (nc.vector if j < 2 else nc.gpsimd).memset(windows[j][:], 0.0)
+        windows = [held([P, TOKENS], F32, f"window{j}") for j in range(PACK - 1)]
+        for j in range(PACK - 1):
+            nc.vector.memset(windows[j][:].bitcast(I32), 0)
 
         for g in range(RUN // PACK):
             bank = psum.tile([P, PACK, P], F32, name="spread", tag="scores", bufs=3)
@@ -82,7 +82,7 @@ def tile_attend_ggqa_sm_k_kernel(tc, q1, q2, kT, dp1, dp2, us, ts, w1, w2, offs,
         q_woven = [held([P, R, PACK], BF16, f"q_woven{h}") for h in range(2)]
         qd_codes = [held([P, R], U32, f"qd_codes{h}") for h in range(2)]
         qd_scales = [held([P, R], U8, f"qd_scales{h}") for h in range(2)]
-        qr_woven = [held([P, PACK, P, PACK], BF16, f"qr_woven{h}") for h in range(2)]
+        qr_woven = [[held([P, 2, P, PACK], BF16, f"qr_woven{h}_{u}") for u in range(2)] for h in range(2)]
         qr_codes = [held([P, D], U32, f"qr_codes{h}") for h in range(2)]
         qr_scales = [held([P, D], U8, f"qr_scales{h}") for h in range(2)]
 
@@ -93,22 +93,22 @@ def tile_attend_ggqa_sm_k_kernel(tc, q1, q2, kT, dp1, dp2, us, ts, w1, w2, offs,
         def quantise_queries_along_d(h):
             quantise(q_woven[h][:].rearrange("p r j -> p (r j)"), E4M3, qd_codes[h][:], qd_scales[h][:])
 
-        def turn_queries(h):
+        def turn_queries(h, u, tag="turned"):
             words = q_woven[h][:].rearrange("p r j -> p (r j)").bitcast(F32)
-            for u in range(2):
-                bank = psum.tile([P, PACK, P], F32, name="turned", tag="turned", bufs=2)
-                for t in range(PACK):
-                    nc.tensor.transpose(bank[:, t, :], words[:, 2 * t + u :: 2 * PACK], ident[:])
-                halves = bank[:].rearrange("s t p -> s (t p)").bitcast(BF16)
-                nc.scalar.copy(qr_woven[h][:, 2 * u : 2 * u + 2, :, :],
-                               halves.rearrange("s (t p e) -> s e p t", t=PACK, e=2))
+            bank = psum.tile([P, PACK, P], F32, name="turned", tag=tag, bufs=2)
+            for t in range(PACK):
+                nc.tensor.transpose(bank[:, t, :], words[:, 2 * t + u :: 2 * PACK], ident[:])
+            halves = bank[:].rearrange("s t p -> s (t p)").bitcast(BF16)
+            nc.scalar.copy(qr_woven[h][u][:], halves.rearrange("s (t p e) -> s e p t", t=PACK, e=2))
 
-        def quantise_queries_along_r(h):
-            quantise(qr_woven[h][:].rearrange("s j p t -> s (j p t)"), E4M3, qr_codes[h][:], qr_scales[h][:])
+        def quantise_queries_along_r(h, u):
+            feats = slice(2 * u * P, 2 * (u + 1) * P)
+            quantise(qr_woven[h][u][:].rearrange("s e p t -> s (e p t)"), E4M3, qr_codes[h][:, feats], qr_scales[h][:, feats])
 
         weave_queries(0, nc.scalar.copy)
         quantise_queries_along_d(0)
-        turn_queries(0)
+        for u in range(2):
+            turn_queries(0, u)
 
         ts_slots = held([P, SLOTS], F32, "ts_slots")
         nc.vector.tensor_copy(ts_slots[:], ts_win[:].indirect(offsets[:]))
@@ -129,17 +129,15 @@ def tile_attend_ggqa_sm_k_kernel(tc, q1, q2, kT, dp1, dp2, us, ts, w1, w2, offs,
             for a in range(2):
                 nc.vector.tensor_copy(k_woven[a][:, :, j], k_raw[j][:].indirect(offsets[:, a * cols : (a + 1) * cols]))
             if j == 1:
-                quantise_queries_along_r(0)
+                quantise_queries_along_r(0, 0)
         for a in range(2):
             quantise(k_woven[a][:].rearrange("p i j -> p (i j)"), E4M3, k_codes[a][:], k_scales[a][:])
 
         neg_us = held([P, PACK], F32, "neg_us")
-        nc.vector.tensor_scalar(neg_us[:], us_sb[:], -1.0, None, ALU.mult)
-        gate = [held([P, PACK], F32, f"gate{h}") for h in range(2)]
+        nc.gpsimd.tensor_scalar(neg_us[:], us_sb[:], -1.0, 0.0, ALU.mult, ALU.add)
         neg_gate = [held([P, PACK], F32, f"neg_gate{h}") for h in range(2)]
         for h in range(2):
-            nc.vector.tensor_tensor(gate[h][:], w_sb[h][:], us_sb[:], ALU.mult)
-            nc.vector.tensor_tensor(neg_gate[h][:], w_sb[h][:], neg_us[:], ALU.mult)
+            nc.gpsimd.tensor_tensor(neg_gate[h][:], w_sb[h][:], (us_sb, neg_us)[h][:], ALU.mult)
 
         scaled = [[held([P, PACK, P], F32, f"scaled{h}_{b}") for b in range(PACK)] for h in range(2)]
 
@@ -159,10 +157,11 @@ def tile_attend_ggqa_sm_k_kernel(tc, q1, q2, kT, dp1, dp2, us, ts, w1, w2, offs,
         g_woven = [[held([P, HALF, PACK], BF16, f"g_woven{h}_{a}") for a in range(2)] for h in range(2)]
         g_codes = [held([P, SLOTS], U32, f"g_codes{h}") for h in range(2)]
         g_scales = [held([P, SLOTS], U8, f"g_scales{h}") for h in range(2)]
+        mean_part = held([P, PACK, SLOTS], F32, "mean_part")
         state = {}
 
         def column(name):
-            return ring.tile([P, 1], F32, name=name, tag=name, bufs=4)
+            return ring.tile([P, 1], F32, name=name, tag=name, bufs=8)
 
         def stage_max(h, t):
             rows = psum.tile([P, SLOTS], F32, name="rows", tag="rows", bufs=2)
@@ -171,7 +170,7 @@ def tile_attend_ggqa_sm_k_kernel(tc, q1, q2, kT, dp1, dp2, us, ts, w1, w2, offs,
             neg_z = ring.tile([P, SLOTS], F32, name="neg_z")
             neg_max = column("neg_max")
             nc.vector.tensor_scalar(neg_z[:], rows[:], neg_us[:, t : t + 1], None, ALU.mult, ALU.min, accum_out=neg_max[:])
-            e = ring.tile([P, SLOTS], F32, name="e", bufs=4)
+            e = ring.tile([P, SLOTS], F32, name="e", bufs=6)
             total = column("total")
             nc.scalar.activation(e[:], neg_z[:], ACT.Exp, bias=neg_max[:], scale=-1.0, accum_out=total[:])
             state[h, t] = (e, total)
@@ -184,26 +183,56 @@ def tile_attend_ggqa_sm_k_kernel(tc, q1, q2, kT, dp1, dp2, us, ts, w1, w2, offs,
 
         def stage_factors(h, t):
             e, inv = state[h, t]
-            mean_factor = column("mean_factor")
-            nc.vector.tensor_scalar(mean_factor[:], inv[:], neg_gate[h][:, t : t + 1], inv[:], ALU.mult, ALU.mult)
-            coef = column("coef")
-            nc.scalar.activation(coef[:], inv[:], ACT.Copy, scale=gate[h][:, t : t + 1])
-            state[h, t] = (e, mean_factor, coef)
+            neg_coef = column("neg_coef")
+            nc.vector.tensor_scalar(neg_coef[:], inv[:], neg_gate[h][:, t : t + 1], None, ALU.mult)
+            state[h, t] = (e, inv, neg_coef)
 
         def stage_mean(h, t):
-            e, mean_factor, coef = state[h, t]
-            products = ring.tile([P, SLOTS], F32, name="products", bufs=2)
+            e, inv, neg_coef = state[h, t]
+            products = ring.tile([P, SLOTS], F32, name="products") if h == 1 else grad[0][:, t, :]
+            row_sum = column("row_sum")
+            nc.vector.scalar_tensor_tensor(products[:], e[:], neg_coef[:], dp_sb[h][:, t, :], ALU.mult, ALU.mult,
+                                           accum_out=row_sum[:])
             shift = column("shift")
-            nc.vector.scalar_tensor_tensor(products[:], e[:], mean_factor[:], dp_sb[h][:, t, :], ALU.mult, ALU.mult,
-                                           accum_out=shift[:])
-            centred = ring.tile([P, SLOTS], F32, name="centred")
-            nc.scalar.activation(centred[:], dp_sb[h][:, t, :], ACT.Identity, bias=shift[:], scale=coef[:])
-            state[h, t] = (e, centred)
+            if (h, t) == (1, PACK - 1):
+                nc.vector.tensor_scalar(shift[:], row_sum[:], inv[:], None, ALU.mult)
+            elif h == 1:
+                nc.scalar.activation(shift[:], row_sum[:], ACT.Copy, scale=inv[:])
+            else:
+                nc.vector.tensor_scalar(shift[:], row_sum[:], inv[:], -1.0, ALU.mult, ALU.mult)
+            state[h, t] = (e, products, shift)
 
         def stage_grad(h, t):
-            e, centred = state[h, t]
-            engine = nc.gpsimd if H_ON_GPSIMD and (h, t) != (1, PACK - 1) else nc.vector
-            engine.tensor_tensor(grad[h][:, t, :], centred[:], e[:], ALU.mult)
+            e, products, shift = state[h, t]
+            if h == 1:
+                nc.vector.scalar_tensor_tensor(grad[h][:, t, :], e[:], shift[:], products[:], ALU.mult, ALU.subtract)
+            else:
+                nc.scalar.activation(mean_part[:, t, :], e[:], ACT.Copy, scale=shift[:])
+
+        g_turned = [held([P, 2, P, 2], BF16, f"g_turned{b}") for b in range(PACK)]
+
+        def turn_gradient(h, b):
+            bank = psum.tile([P, PACK, P], F32, name="grad_turned", tag="scores", bufs=3)
+            for t in range(PACK):
+                for first, part in ((True, grad[h]), (False, mean_part)):
+                    nc.tensor.matmul(bank[:, t, :], part[:, t, b * P : (b + 1) * P], ident[:], start=first, stop=not first,
+                                     is_transpose=True)
+            nc.scalar.activation(g_turned[b][:], bank[:].rearrange("i (u e) s -> i u s e", e=2), ACT.Copy,
+                                 scale=ts_cols[:, b : b + 1])
+
+        def return_gradient(h, a):
+            bank = psum.tile([P, 2, HALF], F32, name="grad_back", tag="turned", bufs=2)
+            for c in range(2):
+                words = g_turned[2 * a + c][:].rearrange("i u s e -> i (u s e)").bitcast(F32)
+                for u in range(2):
+                    nc.tensor.transpose(bank[:, u, c * P : (c + 1) * P], words[:, u * P : (u + 1) * P], ident[:])
+            target = g_woven[h][a][:].rearrange("s i t -> s (i t)").bitcast(F32).rearrange("s (i u) -> s i u", u=2)
+            nc.scalar.copy(target, bank[:].rearrange("s u i -> s i u"))
+
+        def quantise_gradient(h):
+            for a in range(2):
+                slots = slice(a * HALF, (a + 1) * HALF)
+                quantise(g_woven[h][a][:].rearrange("p i t -> p (i t)"), E5M2, g_codes[h][:, slots], g_scales[h][:, slots])
 
         def finish_head(h):
             for a in range(2):
@@ -211,9 +240,7 @@ def tile_attend_ggqa_sm_k_kernel(tc, q1, q2, kT, dp1, dp2, us, ts, w1, w2, offs,
                 factors = ts_rows[:, slots].rearrange("p (c i) -> p c i", i=4).unsqueeze(2).to_broadcast([P, HALF // 4, PACK, 4])
                 nc.vector.tensor_tensor(g_woven[h][a][:].rearrange("p (c i) t -> p c t i", i=4),
                                         grad[h][:, :, slots].rearrange("p t (c i) -> p c t i", i=4), factors, ALU.mult)
-            for a in range(2):
-                slots = slice(a * HALF, (a + 1) * HALF)
-                quantise(g_woven[h][a][:].rearrange("p i t -> p (i t)"), E5M2, g_codes[h][:, slots], g_scales[h][:, slots])
+            quantise_gradient(h)
 
         sums = {}
 
@@ -224,6 +251,7 @@ def tile_attend_ggqa_sm_k_kernel(tc, q1, q2, kT, dp1, dp2, us, ts, w1, w2, offs,
 
         for b in range(PACK):
             score_block(0, b, False)
+        quantise_queries_along_r(0, 1)
         weave_queries(1, nc.vector.tensor_copy)
         quantise_queries_along_d(1)
 
@@ -238,27 +266,40 @@ def tile_attend_ggqa_sm_k_kernel(tc, q1, q2, kT, dp1, dp2, us, ts, w1, w2, offs,
                 stage_factors(*tiles[n - 1])
             if n < PACK:
                 score_block(1, n, False)
-            if 2 <= n <= last:
+            if PACK + 2 <= n <= last:
                 stage_grad(*tiles[n - 2])
             if 1 <= n <= last:
                 stage_mean(*tiles[n - 1])
-            if n == PACK:
-                turn_queries(1)
+            if n in (PACK, PACK + 1):
+                stage_grad(0, 2 * (n - PACK))
+                stage_grad(0, 2 * (n - PACK) + 1)
+            if n == PACK + 3:
+                turn_queries(1, 0)
             if n == last:
-                quantise_queries_along_r(1)
-                finish_head(0)
+                quantise_queries_along_r(1, 0)
+            if n in (PACK + 2, PACK + 3):
+                a = n - PACK - 2
+                turn_gradient(0, 2 * a)
+                turn_gradient(0, 2 * a + 1)
+                return_gradient(0, a)
+            if n == last:
+                quantise_gradient(0)
                 for j in range(2):
                     sums[j] = psum.tile([P, SLOTS], F32, name="sums", tag="turned", bufs=2)
                     key_gradient_pass(j, 0)
+                for j in range(2, PACK):
+                    sums[j] = psum.tile([P, SLOTS], F32, name="late_sums", tag="scores", bufs=3)
+                    key_gradient_pass(j, 0)
+                turn_queries(1, 1, "rows")
             if n == last + 1:
                 stage_grad(*tiles[n - 2])
         finish_head(1)
+        windows.append(keep.tile([P, TOKENS], F32, name="window3", tag="grad1", align_bytes=64))
+        nc.vector.memset(windows[-1][:].bitcast(I32), 0)
+        quantise_queries_along_r(1, 1)
 
         out_planes = out.rearrange("(p j) c -> j p c", j=PACK)
         for j in range(PACK):
-            if j >= 2:
-                sums[j] = psum.tile([P, SLOTS], F32, name="late_sums", tag="scores", bufs=3)
-                key_gradient_pass(j, 0)
             key_gradient_pass(j, 1)
             dk = held([P, SLOTS], F32, f"dk{j}")
             nc.scalar.copy(dk[:], sums[j][:])

@@ -21,6 +21,7 @@ R = 512
 SLOTS = 512
 TOKENS = 2048
 HALF = SLOTS // 2
+DIRECT = 4
 RUN = TOKENS // P
 FLOPS = 4 * 2 * D * R * SLOTS
 
@@ -87,8 +88,10 @@ def tile_attend_ggqa_sm_k_kernel(tc, q1, q2, kT, dp1, dp2, us, ts, w1, w2, offs,
         qr_scales = [held([P, D], U8, f"qr_scales{h}") for h in range(2)]
 
         def weave_queries(h, copy):
-            copy(q_woven[h][:].rearrange("p (c i) j -> p c j i", i=4),
-                 q_raw[h][:].rearrange("p j (c i) -> p c j i", i=4))
+            if h == 0:
+                copy(q_woven[h][:].rearrange("p (t s) j -> p s j t", t=PACK), q_raw[h][:].rearrange("p j (s t) -> p s j t", t=PACK))
+            else:
+                copy(q_woven[h][:].rearrange("p (c i) j -> p c j i", i=4), q_raw[h][:].rearrange("p j (c i) -> p c j i", i=4))
 
         def quantise_queries_along_d(h):
             quantise(q_woven[h][:].rearrange("p r j -> p (r j)"), E4M3, qd_codes[h][:], qd_scales[h][:])
@@ -97,7 +100,7 @@ def tile_attend_ggqa_sm_k_kernel(tc, q1, q2, kT, dp1, dp2, us, ts, w1, w2, offs,
             words = q_woven[h][:].rearrange("p r j -> p (r j)").bitcast(F32)
             bank = psum.tile([P, PACK, P], F32, name="turned", tag=tag, bufs=2)
             for t in range(PACK):
-                nc.tensor.transpose(bank[:, t, :], words[:, 2 * t + u :: 2 * PACK], ident[:])
+                nc.tensor.transpose(bank[:, t, :], words[:, 2 * P * t + u : 2 * P * (t + 1) : 2] if h == 0 else words[:, 2 * t + u :: 2 * PACK], ident[:])
             halves = bank[:].rearrange("s t p -> s (t p)").bitcast(BF16)
             nc.scalar.copy(qr_woven[h][u][:], halves.rearrange("s (t p e) -> s e p t", t=PACK, e=2))
 
@@ -143,15 +146,17 @@ def tile_attend_ggqa_sm_k_kernel(tc, q1, q2, kT, dp1, dp2, us, ts, w1, w2, offs,
 
         def score_block(h, b, on_vector):
             a, c = divmod(b, 2)
-            bank = psum.tile([P, R], F32, name="scores", tag="scores", bufs=3)
+            first = DIRECT if h == 0 else 0
+            rows_used = slice(first * P, R)
+            bank = psum.tile([P, R - first * P], F32, name="scores", tag="scores", bufs=3)
             nc.tensor.matmul_mx(out=bank[:], lhsT=k_codes[a][:, c * P : (c + 1) * P].bitcast(E4M3),
                                 lhsT_scale=k_scales[a][:, c * P : (c + 1) * P],
-                                rhs=qd_codes[h][:].bitcast(E4M3), rhs_scale=qd_scales[h][:], start=True, stop=True)
-            dealt = bank[:].rearrange("i (s t) -> i t s", t=PACK)
+                                rhs=qd_codes[h][:, rows_used].bitcast(E4M3), rhs_scale=qd_scales[h][:, rows_used], start=True, stop=True)
+            dealt = bank[:].rearrange("i (t s) -> i t s", s=P) if h == 0 else bank[:].rearrange("i (s t) -> i t s", t=PACK)
             if on_vector:
                 nc.vector.tensor_scalar(scaled[h][b][:], dealt, ts_cols[:, b : b + 1], None, ALU.mult)
             else:
-                nc.scalar.activation(scaled[h][b][:], dealt, ACT.Copy, scale=ts_cols[:, b : b + 1])
+                nc.scalar.activation(scaled[h][b][:, first:, :], dealt, ACT.Copy, scale=ts_cols[:, b : b + 1])
 
         grad = [held([P, PACK, SLOTS], F32, f"grad{h}") for h in range(2)]
         g_woven = [[held([P, HALF, PACK], BF16, f"g_woven{h}_{a}") for a in range(2)] for h in range(2)]
@@ -165,11 +170,19 @@ def tile_attend_ggqa_sm_k_kernel(tc, q1, q2, kT, dp1, dp2, us, ts, w1, w2, offs,
 
         def stage_max(h, t):
             rows = psum.tile([P, SLOTS], F32, name="rows", tag="rows", bufs=2)
-            for b in range(PACK):
-                nc.tensor.transpose(rows[:, b * P : (b + 1) * P], scaled[h][b][:, t, :], ident[:])
             neg_z = ring.tile([P, SLOTS], F32, name="neg_z")
             neg_max = column("neg_max")
-            nc.vector.tensor_scalar(neg_z[:], rows[:], neg_us[:, t : t + 1], None, ALU.mult, ALU.min, accum_out=neg_max[:])
+            if h == 0 and t < DIRECT:
+                for a in range(2):
+                    nc.tensor.matmul_mx(out=rows[:, a * HALF : (a + 1) * HALF], lhsT=qd_codes[h][:, t * P : (t + 1) * P].bitcast(E4M3),
+                                        lhsT_scale=qd_scales[h][:, t * P : (t + 1) * P],
+                                        rhs=k_codes[a][:].bitcast(E4M3), rhs_scale=k_scales[a][:], start=True, stop=True)
+                nc.vector.scalar_tensor_tensor(neg_z[:], rows[:], neg_us[:, t : t + 1], ts_slots[:], ALU.mult, ALU.mult)
+                nc.vector.tensor_reduce(neg_max[:], neg_z[:], mybir.AxisListType.X, ALU.min)
+            else:
+                for b in range(PACK):
+                    nc.tensor.transpose(rows[:, b * P : (b + 1) * P], scaled[h][b][:, t, :], ident[:])
+                nc.vector.tensor_scalar(neg_z[:], rows[:], neg_us[:, t : t + 1], None, ALU.mult, ALU.min, accum_out=neg_max[:])
             e = ring.tile([P, SLOTS], F32, name="e", bufs=6)
             total = column("total")
             nc.scalar.activation(e[:], neg_z[:], ACT.Exp, bias=neg_max[:], scale=-1.0, accum_out=total[:])
@@ -249,23 +262,24 @@ def tile_attend_ggqa_sm_k_kernel(tc, q1, q2, kT, dp1, dp2, us, ts, w1, w2, offs,
             nc.tensor.matmul_mx(out=sums[j][:], lhsT=qr_codes[h][:, feats].bitcast(E4M3), lhsT_scale=qr_scales[h][:, feats],
                                 rhs=g_codes[h][:].bitcast(E5M2), rhs_scale=g_scales[h][:], start=(h == 0), stop=(h == 1))
 
-        for b in range(PACK):
-            score_block(0, b, False)
+        stage_max(0, 0)
         quantise_queries_along_r(0, 1)
-        weave_queries(1, nc.vector.tensor_copy)
-        quantise_queries_along_d(1)
 
         tiles = [(h, t) for h in range(2) for t in range(PACK)]
         last = len(tiles)
         for n in range(last + 2):
             if 1 <= n <= last:
                 stage_inverse(*tiles[n - 1])
-            if n < last:
+            if 1 <= n < last:
                 stage_max(*tiles[n])
             if 1 <= n <= last:
                 stage_factors(*tiles[n - 1])
-            if n < PACK:
-                score_block(1, n, False)
+            if n == 1:
+                weave_queries(1, nc.scalar.copy)
+                quantise_queries_along_d(1)
+            if 2 <= n <= 3:
+                score_block(1, 2 * n - 4, False)
+                score_block(1, 2 * n - 3, False)
             if PACK + 2 <= n <= last:
                 stage_grad(*tiles[n - 2])
             if 1 <= n <= last:

@@ -5,8 +5,8 @@ from concourse.masks import make_identity
 
 F32 = mybir.dt.float32
 BF16 = mybir.dt.bfloat16
-U32 = mybir.dt.uint32
 I32 = mybir.dt.int32
+U32 = mybir.dt.uint32
 U16 = mybir.dt.uint16
 U8 = mybir.dt.uint8
 E4M3 = mybir.dt.float8_e4m3fn_x4
@@ -20,9 +20,11 @@ D = 512
 R = 512
 SLOTS = 512
 TOKENS = 2048
+HEADS = 2
 HALF = SLOTS // 2
-DIRECT = 4
 RUN = TOKENS // P
+LINE = 4
+FIRST, SECOND = 0, 1
 FLOPS = 4 * 2 * D * R * SLOTS
 
 
@@ -36,86 +38,101 @@ def tile_attend_ggqa_sm_k_kernel(tc, q1, q2, kT, dp1, dp2, us, ts, w1, w2, offs,
         def held(shape, dtype, name):
             return keep.tile(shape, dtype, name=name, align_bytes=64)
 
+        def wide_bank(shape, name):
+            return psum.tile(shape, F32, name=name, tag="wide", bufs=3)
+
+        def turn_bank(shape, name):
+            return psum.tile(shape, F32, name=name, tag="turn", bufs=2)
+
+        def row_bank(shape, name):
+            return psum.tile(shape, F32, name=name, tag="row", bufs=2)
+
         offsets = keep.tile([P, SLOTS // 16], U16, name="offsets")
         nc.sync.dma_start(offsets[:], offs)
 
-        q_raw = [held([P, PACK, R], F32, f"q_raw{h}") for h in range(2)]
-        dp_sb = [held([P, PACK, SLOTS], F32, f"dp_sb{h}") for h in range(2)]
-        k_raw = [held([P, TOKENS], F32, f"k_raw{j}") for j in range(PACK)]
+        q_raw = [held([P, PACK, R], F32, f"q_raw{h}") for h in range(HEADS)]
+        dp_sb = [held([P, PACK, SLOTS], F32, f"dp_sb{h}") for h in range(HEADS)]
+        k_planes = [held([P, TOKENS], F32, f"k_plane{j}") for j in range(PACK)]
         us_sb = held([P, PACK], F32, "us_sb")
-        w_sb = [held([P, PACK], F32, f"w_sb{h}") for h in range(2)]
-        ts_win = held([P, TOKENS], F32, "ts_win")
+        w_sb = [held([P, PACK], F32, f"w_sb{h}") for h in range(HEADS)]
+        ts_window = held([P, TOKENS], F32, "ts_window")
         ident = held([P, P], F32, "ident")
 
         make_identity(nc, ident[:])
-        warm = held([P, 1], F32, "warm")
-        warm_out = held([P, 1], F32, "warm_out")
-        nc.vector.memset(warm[:], 0.0)
-        nc.scalar.activation(warm_out[:], warm[:], ACT.Exp)
 
         ts_runs = held([P, RUN], F32, "ts_runs")
         nc.sync.dma_start(ts_runs[:], ts[0:1, :].rearrange("o (p c) -> p (o c)", c=RUN))
-        nc.sync.dma_start(q_raw[0][:], q1.rearrange("(p j) r -> p j r", j=PACK))
-        k_planes = kT.rearrange("(p j) t -> j p t", j=PACK)
+        nc.sync.dma_start(q_raw[FIRST][:], q1.rearrange("(p j) r -> p j r", j=PACK))
+        k_hbm = kT.rearrange("(p j) t -> j p t", j=PACK)
         for j in range(PACK):
-            nc.sync.dma_start(k_raw[j][:], k_planes[j])
+            nc.sync.dma_start(k_planes[j][:], k_hbm[j])
         nc.scalar.dma_start(us_sb[:], us.rearrange("(s t) o -> s (t o)", t=PACK))
         for h, w in enumerate((w1, w2)):
             nc.scalar.dma_start(w_sb[h][:], w.rearrange("(s t) o -> s (t o)", t=PACK))
-        nc.sync.dma_start(q_raw[1][:], q2.rearrange("(p j) r -> p j r", j=PACK))
+        nc.sync.dma_start(q_raw[SECOND][:], q2.rearrange("(p j) r -> p j r", j=PACK))
         for h, dp in enumerate((dp1, dp2)):
             nc.sync.dma_start(dp_sb[h][:], dp.rearrange("(s t) i -> s t i", t=PACK))
 
-        windows = [held([P, TOKENS], F32, f"window{j}") for j in range(PACK - 1)]
-        for j in range(PACK - 1):
-            nc.vector.memset(windows[j][:].bitcast(I32), 0)
+        windows = [held([P, TOKENS], F32, f"window{j}") for j in range(PACK)]
+        for j in range(PACK):
+            for half in range(2):
+                columns = slice(half * TOKENS // 2, (half + 1) * TOKENS // 2)
+                (nc.vector if j == 0 else nc.gpsimd).memset(windows[j][:, columns].bitcast(I32), 0)
 
         for g in range(RUN // PACK):
-            bank = psum.tile([P, PACK, P], F32, name="spread", tag="scores", bufs=3)
+            bank = wide_bank([P, PACK, P], "spread")
             for c in range(PACK):
-                nc.tensor.transpose(bank[:, c, :], ts_runs[:, PACK * g + c : PACK * g + c + 1].to_broadcast([P, P]), ident[:])
+                column = ts_runs[:, PACK * g + c : PACK * g + c + 1]
+                nc.tensor.transpose(bank[:, c, :], column.to_broadcast([P, P]), ident[:])
             copy = nc.scalar.copy if g % 2 == 0 else nc.vector.tensor_copy
-            copy(ts_win[:].rearrange("m (p c) -> m p c", c=RUN)[:, :, PACK * g : PACK * (g + 1)], bank[:].rearrange("m c p -> m p c"))
+            copy(ts_window[:].rearrange("m (p c) -> m p c", c=RUN)[:, :, PACK * g : PACK * (g + 1)],
+                 bank[:].rearrange("m c p -> m p c"))
 
         def quantise(source, fmt, codes, scales):
             nc.vector.quantize_mx(out=codes.bitcast(fmt), scales=scales, in_=source)
 
-        q_woven = [held([P, R, PACK], BF16, f"q_woven{h}") for h in range(2)]
-        qd_codes = [held([P, R], U32, f"qd_codes{h}") for h in range(2)]
-        qd_scales = [held([P, R], U8, f"qd_scales{h}") for h in range(2)]
-        qr_woven = [[held([P, 2, P, PACK], BF16, f"qr_woven{h}_{u}") for u in range(2)] for h in range(2)]
-        qr_codes = [held([P, D], U32, f"qr_codes{h}") for h in range(2)]
-        qr_scales = [held([P, D], U8, f"qr_scales{h}") for h in range(2)]
+        q_woven = [held([P, R, PACK], BF16, f"q_woven{h}") for h in range(HEADS)]
+        qd_codes = [held([P, R], U32, f"qd_codes{h}") for h in range(HEADS)]
+        qd_scales = [held([P, R], U8, f"qd_scales{h}") for h in range(HEADS)]
+        qr_woven = [[held([P, 2, P, PACK], BF16, f"qr_woven{h}_{u}") for u in range(2)] for h in range(HEADS)]
+        qr_codes = {(h, 0): held([P, 2 * P], U32, f"qr_codes{h}")[:] for h in range(HEADS)}
+        qr_scales = [held([P, D], U8, f"qr_scales{h}") for h in range(HEADS)]
 
-        def weave_queries(h, copy):
-            if h == 0:
-                copy(q_woven[h][:].rearrange("p (t s) j -> p s j t", t=PACK), q_raw[h][:].rearrange("p j (s t) -> p s j t", t=PACK))
+        def weave_queries(h):
+            if h == FIRST:
+                nc.scalar.copy(q_woven[h][:].rearrange("p (t s) j -> p s j t", t=PACK),
+                               q_raw[h][:].rearrange("p j (s t) -> p s j t", t=PACK))
             else:
-                copy(q_woven[h][:].rearrange("p (c i) j -> p c j i", i=4), q_raw[h][:].rearrange("p j (c i) -> p c j i", i=4))
+                nc.scalar.copy(q_woven[h][:].rearrange("p (c i) j -> p c j i", i=LINE),
+                               q_raw[h][:].rearrange("p j (c i) -> p c j i", i=LINE))
 
         def quantise_queries_along_d(h):
             quantise(q_woven[h][:].rearrange("p r j -> p (r j)"), E4M3, qd_codes[h][:], qd_scales[h][:])
 
-        def turn_queries(h, u, tag="turned"):
+        def turn_queries(h, u, new_bank):
             words = q_woven[h][:].rearrange("p r j -> p (r j)").bitcast(F32)
-            bank = psum.tile([P, PACK, P], F32, name="turned", tag=tag, bufs=2)
+            bank = new_bank([P, PACK, P], "turned")
             for t in range(PACK):
-                nc.tensor.transpose(bank[:, t, :], words[:, 2 * P * t + u : 2 * P * (t + 1) : 2] if h == 0 else words[:, 2 * t + u :: 2 * PACK], ident[:])
-            halves = bank[:].rearrange("s t p -> s (t p)").bitcast(BF16)
-            nc.scalar.copy(qr_woven[h][u][:], halves.rearrange("s (t p e) -> s e p t", t=PACK, e=2))
+                if h == FIRST:
+                    tile_words = words[:, 2 * P * t + u : 2 * P * (t + 1) : 2]
+                else:
+                    tile_words = words[:, 2 * t + u :: 2 * PACK]
+                nc.tensor.transpose(bank[:, t, :], tile_words, ident[:])
+            values = bank[:].rearrange("s t p -> s (t p)").bitcast(BF16)
+            nc.scalar.copy(qr_woven[h][u][:], values.rearrange("s (t p e) -> s e p t", t=PACK, e=2))
 
         def quantise_queries_along_r(h, u):
-            feats = slice(2 * u * P, 2 * (u + 1) * P)
-            quantise(qr_woven[h][u][:].rearrange("s e p t -> s (e p t)"), E4M3, qr_codes[h][:, feats], qr_scales[h][:, feats])
+            quantise(qr_woven[h][u][:].rearrange("s e p t -> s (e p t)"), E4M3, qr_codes[h, u],
+                     qr_scales[h][:, 2 * u * P : 2 * (u + 1) * P])
 
-        weave_queries(0, nc.scalar.copy)
-        quantise_queries_along_d(0)
+        weave_queries(FIRST)
+        quantise_queries_along_d(FIRST)
         for u in range(2):
-            turn_queries(0, u)
+            turn_queries(FIRST, u, turn_bank)
 
         ts_slots = held([P, SLOTS], F32, "ts_slots")
-        nc.vector.tensor_copy(ts_slots[:], ts_win[:].indirect(offsets[:]))
-        ts_turned = psum.tile([P, PACK, P], F32, name="ts_turned", tag="scores", bufs=3)
+        nc.vector.tensor_copy(ts_slots[:], ts_window[:].indirect(offsets[:]))
+        ts_turned = wide_bank([P, PACK, P], "ts_turned")
         for b in range(PACK):
             nc.tensor.transpose(ts_turned[:, b, :], ts_slots[:, b * P : (b + 1) * P], ident[:])
         ts_cols = held([P, PACK], F32, "ts_cols")
@@ -127,194 +144,189 @@ def tile_attend_ggqa_sm_k_kernel(tc, q1, q2, kT, dp1, dp2, us, ts, w1, w2, offs,
         k_woven = [held([P, HALF, PACK], BF16, f"k_woven{a}") for a in range(2)]
         k_codes = [held([P, HALF], U32, f"k_codes{a}") for a in range(2)]
         k_scales = [held([P, HALF], U8, f"k_scales{a}") for a in range(2)]
-        cols = HALF // 16
+        list_columns = HALF // 16
         for j in range(PACK):
             for a in range(2):
-                nc.vector.tensor_copy(k_woven[a][:, :, j], k_raw[j][:].indirect(offsets[:, a * cols : (a + 1) * cols]))
-            if j == 1:
-                quantise_queries_along_r(0, 0)
+                half_list = offsets[:, a * list_columns : (a + 1) * list_columns]
+                nc.vector.tensor_copy(k_woven[a][:, :, j], k_planes[j][:].indirect(half_list))
+            if j == PACK // 2 - 1:
+                quantise_queries_along_r(FIRST, 0)
         for a in range(2):
             quantise(k_woven[a][:].rearrange("p i j -> p (i j)"), E4M3, k_codes[a][:], k_scales[a][:])
 
         neg_us = held([P, PACK], F32, "neg_us")
         nc.gpsimd.tensor_scalar(neg_us[:], us_sb[:], -1.0, 0.0, ALU.mult, ALU.add)
-        neg_gate = [held([P, PACK], F32, f"neg_gate{h}") for h in range(2)]
-        for h in range(2):
-            nc.gpsimd.tensor_tensor(neg_gate[h][:], w_sb[h][:], (us_sb, neg_us)[h][:], ALU.mult)
+        gates = [held([P, PACK], F32, f"gates{h}") for h in range(HEADS)]
+        for h in range(HEADS):
+            nc.gpsimd.tensor_tensor(gates[h][:], w_sb[h][:], (us_sb, neg_us)[h][:], ALU.mult)
 
-        scaled = [[held([P, PACK, P], F32, f"scaled{h}_{b}") for b in range(PACK)] for h in range(2)]
+        scaled = [held([P, PACK, P], F32, f"scaled{b}") for b in range(PACK)]
 
-        def score_block(h, b, on_vector):
+        def score_second_head(b):
             a, c = divmod(b, 2)
-            first = DIRECT if h == 0 else 0
-            rows_used = slice(first * P, R)
-            bank = psum.tile([P, R - first * P], F32, name="scores", tag="scores", bufs=3)
+            bank = wide_bank([P, R], "scores")
             nc.tensor.matmul_mx(out=bank[:], lhsT=k_codes[a][:, c * P : (c + 1) * P].bitcast(E4M3),
                                 lhsT_scale=k_scales[a][:, c * P : (c + 1) * P],
-                                rhs=qd_codes[h][:, rows_used].bitcast(E4M3), rhs_scale=qd_scales[h][:, rows_used], start=True, stop=True)
-            dealt = bank[:].rearrange("i (t s) -> i t s", s=P) if h == 0 else bank[:].rearrange("i (s t) -> i t s", t=PACK)
-            if on_vector:
-                nc.vector.tensor_scalar(scaled[h][b][:], dealt, ts_cols[:, b : b + 1], None, ALU.mult)
-            else:
-                nc.scalar.activation(scaled[h][b][:, first:, :], dealt, ACT.Copy, scale=ts_cols[:, b : b + 1])
+                                rhs=qd_codes[SECOND][:].bitcast(E4M3), rhs_scale=qd_scales[SECOND][:],
+                                start=True, stop=True)
+            nc.scalar.activation(scaled[b][:], bank[:].rearrange("i (s t) -> i t s", t=PACK), ACT.Copy,
+                                 scale=ts_cols[:, b : b + 1])
 
-        grad = [held([P, PACK, SLOTS], F32, f"grad{h}") for h in range(2)]
-        g_woven = [[held([P, HALF, PACK], BF16, f"g_woven{h}_{a}") for a in range(2)] for h in range(2)]
-        g_codes = [held([P, SLOTS], U32, f"g_codes{h}") for h in range(2)]
-        g_scales = [held([P, SLOTS], U8, f"g_scales{h}") for h in range(2)]
-        mean_part = held([P, PACK, SLOTS], F32, "mean_part")
-        state = {}
+        dp_term = held([P, PACK, SLOTS], F32, "dp_term")
+        grad_second = held([P, PACK, SLOTS], F32, "grad_second")
+        g_woven = [[held([P, HALF, PACK], BF16, f"g_woven{h}_{a}") for a in range(2)] for h in range(HEADS)]
+        g_codes = [held([P, SLOTS], U32, f"g_codes{h}") for h in range(HEADS)]
+        g_scales = [held([P, SLOTS], U8, f"g_scales{h}") for h in range(HEADS)]
+        mean_term = held([P, PACK, SLOTS], F32, "mean_term")
+        exps, totals, inverses, coefs, products, shifts = {}, {}, {}, {}, {}, {}
 
-        def column(name):
-            return ring.tile([P, 1], F32, name=name, tag=name, bufs=8)
+        def statistic(name):
+            return ring.tile([P, 1], F32, name=name, tag=name, bufs=HEADS * PACK)
 
-        def stage_max(h, t):
-            rows = psum.tile([P, SLOTS], F32, name="rows", tag="rows", bufs=2)
+        def stage_exp(h, t):
+            rows = row_bank([P, SLOTS], "rows")
             neg_z = ring.tile([P, SLOTS], F32, name="neg_z")
-            neg_max = column("neg_max")
-            if h == 0 and t < DIRECT:
+            neg_max = statistic("neg_max")
+            if h == FIRST:
                 for a in range(2):
-                    nc.tensor.matmul_mx(out=rows[:, a * HALF : (a + 1) * HALF], lhsT=qd_codes[h][:, t * P : (t + 1) * P].bitcast(E4M3),
+                    nc.tensor.matmul_mx(out=rows[:, a * HALF : (a + 1) * HALF],
+                                        lhsT=qd_codes[h][:, t * P : (t + 1) * P].bitcast(E4M3),
                                         lhsT_scale=qd_scales[h][:, t * P : (t + 1) * P],
-                                        rhs=k_codes[a][:].bitcast(E4M3), rhs_scale=k_scales[a][:], start=True, stop=True)
+                                        rhs=k_codes[a][:].bitcast(E4M3), rhs_scale=k_scales[a][:],
+                                        start=True, stop=True)
                 nc.vector.scalar_tensor_tensor(neg_z[:], rows[:], neg_us[:, t : t + 1], ts_slots[:], ALU.mult, ALU.mult)
                 nc.vector.tensor_reduce(neg_max[:], neg_z[:], mybir.AxisListType.X, ALU.min)
             else:
                 for b in range(PACK):
-                    nc.tensor.transpose(rows[:, b * P : (b + 1) * P], scaled[h][b][:, t, :], ident[:])
-                nc.vector.tensor_scalar(neg_z[:], rows[:], neg_us[:, t : t + 1], None, ALU.mult, ALU.min, accum_out=neg_max[:])
-            e = ring.tile([P, SLOTS], F32, name="e", bufs=6)
-            total = column("total")
-            nc.scalar.activation(e[:], neg_z[:], ACT.Exp, bias=neg_max[:], scale=-1.0, accum_out=total[:])
-            state[h, t] = (e, total)
+                    nc.tensor.transpose(rows[:, b * P : (b + 1) * P], scaled[b][:, t, :], ident[:])
+                nc.vector.tensor_scalar(neg_z[:], rows[:], neg_us[:, t : t + 1], None, ALU.mult, ALU.min,
+                                        accum_out=neg_max[:])
+            exps[h, t] = ring.tile([P, SLOTS], F32, name="e", bufs=PACK + 2)
+            totals[h, t] = statistic("total")
+            nc.scalar.activation(exps[h, t][:], neg_z[:], ACT.Exp, bias=neg_max[:], scale=-1.0, accum_out=totals[h, t][:])
 
         def stage_inverse(h, t):
-            e, total = state[h, t]
-            inv = column("inv")
-            nc.vector.reciprocal(inv[:], total[:])
-            state[h, t] = (e, inv)
+            inverses[h, t] = statistic("inverse")
+            nc.vector.reciprocal(inverses[h, t][:], totals[h, t][:])
 
-        def stage_factors(h, t):
-            e, inv = state[h, t]
-            neg_coef = column("neg_coef")
-            nc.vector.tensor_scalar(neg_coef[:], inv[:], neg_gate[h][:, t : t + 1], None, ALU.mult)
-            state[h, t] = (e, inv, neg_coef)
+        def stage_coef(h, t):
+            coefs[h, t] = statistic("coef")
+            nc.vector.tensor_scalar(coefs[h, t][:], inverses[h, t][:], gates[h][:, t : t + 1], None, ALU.mult)
 
-        def stage_mean(h, t):
-            e, inv, neg_coef = state[h, t]
-            products = ring.tile([P, SLOTS], F32, name="products") if h == 1 else grad[0][:, t, :]
-            row_sum = column("row_sum")
-            nc.vector.scalar_tensor_tensor(products[:], e[:], neg_coef[:], dp_sb[h][:, t, :], ALU.mult, ALU.mult,
-                                           accum_out=row_sum[:])
-            shift = column("shift")
-            if (h, t) == (1, PACK - 1):
-                nc.vector.tensor_scalar(shift[:], row_sum[:], inv[:], None, ALU.mult)
-            elif h == 1:
-                nc.scalar.activation(shift[:], row_sum[:], ACT.Copy, scale=inv[:])
+        def stage_shift(h, t):
+            products[h, t] = dp_term[:, t, :] if h == FIRST else ring.tile([P, SLOTS], F32, name="products")[:]
+            row_sum = statistic("row_sum")
+            nc.vector.scalar_tensor_tensor(products[h, t], exps[h, t][:], coefs[h, t][:], dp_sb[h][:, t, :],
+                                           ALU.mult, ALU.mult, accum_out=row_sum[:])
+            shifts[h, t] = statistic("shift")
+            if h == FIRST:
+                nc.vector.tensor_scalar(shifts[h, t][:], row_sum[:], inverses[h, t][:], -1.0, ALU.mult, ALU.mult)
+            elif t == PACK - 1:
+                nc.vector.tensor_scalar(shifts[h, t][:], row_sum[:], inverses[h, t][:], None, ALU.mult)
             else:
-                nc.vector.tensor_scalar(shift[:], row_sum[:], inv[:], -1.0, ALU.mult, ALU.mult)
-            state[h, t] = (e, products, shift)
+                nc.scalar.activation(shifts[h, t][:], row_sum[:], ACT.Copy, scale=inverses[h, t][:])
 
-        def stage_grad(h, t):
-            e, products, shift = state[h, t]
-            if h == 1:
-                nc.vector.scalar_tensor_tensor(grad[h][:, t, :], e[:], shift[:], products[:], ALU.mult, ALU.subtract)
-            else:
-                nc.scalar.activation(mean_part[:, t, :], e[:], ACT.Copy, scale=shift[:])
+        def mean_term_first_head(t):
+            nc.scalar.activation(mean_term[:, t, :], exps[FIRST, t][:], ACT.Copy, scale=shifts[FIRST, t][:])
+
+        def gradient_second_head(t):
+            nc.vector.scalar_tensor_tensor(grad_second[:, t, :], exps[SECOND, t][:], shifts[SECOND, t][:],
+                                           products[SECOND, t], ALU.mult, ALU.subtract)
 
         g_turned = [held([P, 2, P, 2], BF16, f"g_turned{b}") for b in range(PACK)]
 
-        def turn_gradient(h, b):
-            bank = psum.tile([P, PACK, P], F32, name="grad_turned", tag="scores", bufs=3)
+        def turn_first_gradient(b):
+            bank = wide_bank([P, PACK, P], "grad_turned")
             for t in range(PACK):
-                for first, part in ((True, grad[h]), (False, mean_part)):
-                    nc.tensor.matmul(bank[:, t, :], part[:, t, b * P : (b + 1) * P], ident[:], start=first, stop=not first,
-                                     is_transpose=True)
+                for opens, term in ((True, dp_term), (False, mean_term)):
+                    nc.tensor.matmul(bank[:, t, :], term[:, t, b * P : (b + 1) * P], ident[:], start=opens,
+                                     stop=not opens, is_transpose=True)
             nc.scalar.activation(g_turned[b][:], bank[:].rearrange("i (u e) s -> i u s e", e=2), ACT.Copy,
                                  scale=ts_cols[:, b : b + 1])
 
-        def return_gradient(h, a):
-            bank = psum.tile([P, 2, HALF], F32, name="grad_back", tag="turned", bufs=2)
+        def return_first_gradient(a):
+            bank = turn_bank([P, 2, HALF], "grad_back")
             for c in range(2):
                 words = g_turned[2 * a + c][:].rearrange("i u s e -> i (u s e)").bitcast(F32)
                 for u in range(2):
                     nc.tensor.transpose(bank[:, u, c * P : (c + 1) * P], words[:, u * P : (u + 1) * P], ident[:])
-            target = g_woven[h][a][:].rearrange("s i t -> s (i t)").bitcast(F32).rearrange("s (i u) -> s i u", u=2)
+            target = g_woven[FIRST][a][:].rearrange("s i t -> s (i t)").bitcast(F32).rearrange("s (i u) -> s i u", u=2)
             nc.scalar.copy(target, bank[:].rearrange("s u i -> s i u"))
+
+        def weave_second_gradient(a):
+            slots = slice(a * HALF, (a + 1) * HALF)
+            factors = ts_rows[:, slots].rearrange("p (c i) -> p c i", i=LINE).unsqueeze(2)
+            nc.vector.tensor_tensor(g_woven[SECOND][a][:].rearrange("p (c i) t -> p c t i", i=LINE),
+                                    grad_second[:, :, slots].rearrange("p t (c i) -> p c t i", i=LINE),
+                                    factors.to_broadcast([P, HALF // LINE, PACK, LINE]), ALU.mult)
 
         def quantise_gradient(h):
             for a in range(2):
                 slots = slice(a * HALF, (a + 1) * HALF)
                 quantise(g_woven[h][a][:].rearrange("p i t -> p (i t)"), E5M2, g_codes[h][:, slots], g_scales[h][:, slots])
 
-        def finish_head(h):
-            for a in range(2):
-                slots = slice(a * HALF, (a + 1) * HALF)
-                factors = ts_rows[:, slots].rearrange("p (c i) -> p c i", i=4).unsqueeze(2).to_broadcast([P, HALF // 4, PACK, 4])
-                nc.vector.tensor_tensor(g_woven[h][a][:].rearrange("p (c i) t -> p c t i", i=4),
-                                        grad[h][:, :, slots].rearrange("p t (c i) -> p c t i", i=4), factors, ALU.mult)
-            quantise_gradient(h)
-
         sums = {}
 
         def key_gradient_pass(j, h):
-            feats = slice(j * P, (j + 1) * P)
-            nc.tensor.matmul_mx(out=sums[j][:], lhsT=qr_codes[h][:, feats].bitcast(E4M3), lhsT_scale=qr_scales[h][:, feats],
-                                rhs=g_codes[h][:].bitcast(E5M2), rhs_scale=g_scales[h][:], start=(h == 0), stop=(h == 1))
+            nc.tensor.matmul_mx(out=sums[j][:], lhsT=qr_codes[h, j // 2][:, j % 2 * P : (j % 2 + 1) * P].bitcast(E4M3),
+                                lhsT_scale=qr_scales[h][:, j * P : (j + 1) * P],
+                                rhs=g_codes[h][:].bitcast(E5M2), rhs_scale=g_scales[h][:],
+                                start=(h == FIRST), stop=(h == SECOND))
 
-        stage_max(0, 0)
-        quantise_queries_along_r(0, 1)
-
-        tiles = [(h, t) for h in range(2) for t in range(PACK)]
+        tiles = [(h, t) for h in range(HEADS) for t in range(PACK)]
         last = len(tiles)
         for n in range(last + 2):
             if 1 <= n <= last:
                 stage_inverse(*tiles[n - 1])
-            if 1 <= n < last:
-                stage_max(*tiles[n])
+            if n < last:
+                stage_exp(*tiles[n])
             if 1 <= n <= last:
-                stage_factors(*tiles[n - 1])
+                stage_coef(*tiles[n - 1])
             if n == 1:
-                weave_queries(1, nc.scalar.copy)
-                quantise_queries_along_d(1)
-            if 2 <= n <= 3:
-                score_block(1, 2 * n - 4, False)
-                score_block(1, 2 * n - 3, False)
+                weave_queries(SECOND)
+                quantise_queries_along_d(SECOND)
+            if n in (PACK - 2, PACK - 1):
+                for b in range(2 * (n - PACK + 2), 2 * (n - PACK + 3)):
+                    score_second_head(b)
             if PACK + 2 <= n <= last:
-                stage_grad(*tiles[n - 2])
+                gradient_second_head(n - 2 - PACK)
             if 1 <= n <= last:
-                stage_mean(*tiles[n - 1])
+                stage_shift(*tiles[n - 1])
             if n in (PACK, PACK + 1):
-                stage_grad(0, 2 * (n - PACK))
-                stage_grad(0, 2 * (n - PACK) + 1)
+                for t in range(2 * (n - PACK), 2 * (n - PACK + 1)):
+                    mean_term_first_head(t)
             if n == PACK + 3:
-                turn_queries(1, 0)
+                turn_queries(SECOND, 0, turn_bank)
             if n == last:
-                quantise_queries_along_r(1, 0)
+                quantise_queries_along_r(SECOND, 0)
             if n in (PACK + 2, PACK + 3):
                 a = n - PACK - 2
-                turn_gradient(0, 2 * a)
-                turn_gradient(0, 2 * a + 1)
-                return_gradient(0, a)
+                turn_first_gradient(2 * a)
+                turn_first_gradient(2 * a + 1)
+                return_first_gradient(a)
             if n == last:
-                quantise_gradient(0)
+                quantise_gradient(FIRST)
                 for j in range(2):
-                    sums[j] = psum.tile([P, SLOTS], F32, name="sums", tag="turned", bufs=2)
-                    key_gradient_pass(j, 0)
-                for j in range(2, PACK):
-                    sums[j] = psum.tile([P, SLOTS], F32, name="late_sums", tag="scores", bufs=3)
-                    key_gradient_pass(j, 0)
-                turn_queries(1, 1, "rows")
+                    sums[j] = turn_bank([P, SLOTS], "sums")
+                    key_gradient_pass(j, FIRST)
+                turn_queries(SECOND, 1, row_bank)
             if n == last + 1:
-                stage_grad(*tiles[n - 2])
-        finish_head(1)
-        windows.append(keep.tile([P, TOKENS], F32, name="window3", tag="grad1", align_bytes=64))
-        nc.vector.memset(windows[-1][:].bitcast(I32), 0)
-        quantise_queries_along_r(1, 1)
+                gradient_second_head(PACK - 1)
+        for a in range(2):
+            weave_second_gradient(a)
+        quantise_gradient(SECOND)
+
+        late_codes = keep.tile([P, HEADS, 2 * P], U32, name="late_codes", tag="grad_second", align_bytes=64)
+        for h in range(HEADS):
+            qr_codes[h, 1] = late_codes[:, h, :]
+            quantise_queries_along_r(h, 1)
 
         out_planes = out.rearrange("(p j) c -> j p c", j=PACK)
         for j in range(PACK):
-            key_gradient_pass(j, 1)
+            if j not in sums:
+                sums[j] = wide_bank([P, SLOTS], "late_sums")
+                key_gradient_pass(j, FIRST)
+            key_gradient_pass(j, SECOND)
             dk = held([P, SLOTS], F32, f"dk{j}")
             nc.scalar.copy(dk[:], sums[j][:])
             nc.vector.tensor_copy(windows[j][:].indirect(offsets[:]), dk[:])

@@ -25,6 +25,8 @@ HALF = SLOTS // 2
 RUN = TOKENS // P
 LINE = 4
 FIRST, SECOND = 0, 1
+EARLY = 3
+TILES = HEADS * PACK
 FLOPS = 4 * 2 * D * R * SLOTS
 
 
@@ -35,17 +37,17 @@ def tile_attend_ggqa_sm_k_kernel(tc, q1, q2, kT, dp1, dp2, us, ts, w1, w2, offs,
         ring = ctx.enter_context(tc.tile_pool(name="ring", bufs=3))
         psum = ctx.enter_context(tc.psum_pool(name="psum", bufs=1))
 
-        def held(shape, dtype, name):
-            return keep.tile(shape, dtype, name=name, align_bytes=64)
+        def held(shape, dtype, name, tag=None):
+            return keep.tile(shape, dtype, name=name, tag=tag or name, align_bytes=64)
 
-        def wide_bank(shape, name):
-            return psum.tile(shape, F32, name=name, tag="wide", bufs=3)
+        spread_banks = [psum.tile([P, SLOTS], F32, name=f"spread{n}", tag=f"bank{n}") for n in range(RUN // PACK)]
+        banks = [psum.tile([P, SLOTS], F32, name=f"bank{n}", tag=f"bank{n}") for n in range(8)]
 
-        def turn_bank(shape, name):
-            return psum.tile(shape, F32, name=name, tag="turn", bufs=2)
+        def quarters(bank):
+            return bank[:].rearrange("p (c i) -> p c i", c=PACK)
 
-        def row_bank(shape, name):
-            return psum.tile(shape, F32, name=name, tag="row", bufs=2)
+        def halves(bank):
+            return bank[:].rearrange("p (c i) -> p c i", c=2)
 
         offsets = keep.tile([P, SLOTS // 16], U16, name="offsets")
         nc.sync.dma_start(offsets[:], offs)
@@ -73,6 +75,11 @@ def tile_attend_ggqa_sm_k_kernel(tc, q1, q2, kT, dp1, dp2, us, ts, w1, w2, offs,
         for h, dp in enumerate((dp1, dp2)):
             nc.sync.dma_start(dp_sb[h][:], dp.rearrange("(s t) i -> s t i", t=PACK))
 
+        g_codes = [held([P, (2 + h) * HALF], U32, f"g_codes{h}") for h in range(HEADS)]
+        g_scales = [held([P, (2 + h) * HALF], U8, f"g_scales{h}") for h in range(HEADS)]
+        nc.gpsimd.memset(g_codes[SECOND][:, HALF : 2 * HALF], 0)
+        nc.gpsimd.memset(g_scales[SECOND][:, HALF : 2 * HALF].bitcast(U32), 0)
+
         windows = [held([P, TOKENS], F32, f"window{j}") for j in range(PACK)]
         for j in range(PACK):
             for half in range(2):
@@ -80,254 +87,276 @@ def tile_attend_ggqa_sm_k_kernel(tc, q1, q2, kT, dp1, dp2, us, ts, w1, w2, offs,
                 (nc.vector if j == 0 else nc.gpsimd).memset(windows[j][:, columns].bitcast(I32), 0)
 
         for g in range(RUN // PACK):
-            bank = wide_bank([P, PACK, P], "spread")
+            bank = quarters(spread_banks[g])
             for c in range(PACK):
                 column = ts_runs[:, PACK * g + c : PACK * g + c + 1]
                 nc.tensor.transpose(bank[:, c, :], column.to_broadcast([P, P]), ident[:])
             copy = nc.scalar.copy if g % 2 == 0 else nc.vector.tensor_copy
             copy(ts_window[:].rearrange("m (p c) -> m p c", c=RUN)[:, :, PACK * g : PACK * (g + 1)],
-                 bank[:].rearrange("m c p -> m p c"))
+                 bank.rearrange("m c p -> m p c"))
+
+        ts_slots = held([P, SLOTS], F32, "ts_slots")
+        nc.vector.tensor_copy(ts_slots[:], ts_window[:].indirect(offsets[:]))
 
         def quantise(source, fmt, codes, scales):
             nc.vector.quantize_mx(out=codes.bitcast(fmt), scales=scales, in_=source)
 
-        q_woven = [held([P, R, PACK], BF16, f"q_woven{h}") for h in range(HEADS)]
-        qd_codes = [held([P, R], U32, f"qd_codes{h}") for h in range(HEADS)]
+        first_woven = held([P, 2, 2, P, PACK], BF16, "first_woven", "ts_runs")
+        q_woven = [[first_woven[:, u] for u in range(2)],
+                   [held([P, 2, P, PACK], BF16, f"second_woven{u}")[:] for u in range(2)]]
+        qd_codes = [held([P, R], U32, f"qd_codes{h}", "ts_window" if h == FIRST else None) for h in range(HEADS)]
         qd_scales = [held([P, R], U8, f"qd_scales{h}") for h in range(HEADS)]
-        qr_woven = [[held([P, 2, P, PACK], BF16, f"qr_woven{h}_{u}") for u in range(2)] for h in range(HEADS)]
-        qr_codes = {(h, 0): held([P, 2 * P], U32, f"qr_codes{h}")[:] for h in range(HEADS)}
-        qr_scales = [held([P, D], U8, f"qr_scales{h}") for h in range(HEADS)]
+        qr_woven = {(FIRST, v): held([P, 2 * P * PACK], BF16, f"qr_woven{v}")[:] for v in range(2)}
+        qr_codes = [[held([P, 2 * P], U32, f"qr_codes{h}_{v}", f"k_plane{v + 1}" if h == FIRST else None) for v in range(2)]
+                    for h in range(HEADS)]
+        qr_scales = [[held([P, 2 * P], U8, f"qr_scales{h}_{v}") for v in range(2)] for h in range(HEADS)]
 
-        def weave_queries(h):
-            if h == FIRST:
-                nc.scalar.copy(q_woven[h][:].rearrange("p (t s) j -> p s j t", t=PACK),
-                               q_raw[h][:].rearrange("p j (s t) -> p s j t", t=PACK))
-            else:
-                nc.scalar.copy(q_woven[h][:].rearrange("p (c i) j -> p c j i", i=LINE),
-                               q_raw[h][:].rearrange("p j (c i) -> p c j i", i=LINE))
+        def weave_queries(h, u):
+            nc.scalar.copy(q_woven[h][u].rearrange("p e s j -> p s j e"),
+                           q_raw[h][:].rearrange("p j (s t) -> p s j t", t=PACK)[:, :, :, 2 * u : 2 * u + 2])
 
-        def quantise_queries_along_d(h):
-            quantise(q_woven[h][:].rearrange("p r j -> p (r j)"), E4M3, qd_codes[h][:], qd_scales[h][:])
+        def quantise_queries_along_d(h, u):
+            quantise(q_woven[h][u].rearrange("p e s j -> p (e s j)"), E4M3,
+                     qd_codes[h][:, 2 * P * u : 2 * P * (u + 1)], qd_scales[h][:, 2 * P * u : 2 * P * (u + 1)])
 
-        def turn_queries(h, u, new_bank):
-            words = q_woven[h][:].rearrange("p r j -> p (r j)").bitcast(F32)
-            bank = new_bank([P, PACK, P], "turned")
+        def turn_queries(h, v, bank):
             for t in range(PACK):
-                if h == FIRST:
-                    tile_words = words[:, 2 * P * t + u : 2 * P * (t + 1) : 2]
-                else:
-                    tile_words = words[:, 2 * t + u :: 2 * PACK]
-                nc.tensor.transpose(bank[:, t, :], tile_words, ident[:])
-            values = bank[:].rearrange("s t p -> s (t p)").bitcast(BF16)
-            nc.scalar.copy(qr_woven[h][u][:], values.rearrange("s (t p e) -> s e p t", t=PACK, e=2))
+                words = q_woven[h][t // 2].rearrange("p e s j -> p (e s j)").bitcast(F32)
+                nc.tensor.transpose(quarters(bank)[:, t, :], words[:, 2 * P * (t % 2) + v : 2 * P * (t % 2 + 1) : 2], ident[:])
 
-        def quantise_queries_along_r(h, u):
-            quantise(qr_woven[h][u][:].rearrange("s e p t -> s (e p t)"), E4M3, qr_codes[h, u],
-                     qr_scales[h][:, 2 * u * P : 2 * (u + 1) * P])
+        def weave_turned_queries(h, v, bank):
+            nc.scalar.copy(qr_woven[h, v].rearrange("s (e p t) -> s e p t", e=2, t=PACK),
+                           bank[:].bitcast(BF16).rearrange("s (t p e) -> s e p t", t=PACK, e=2))
 
-        weave_queries(FIRST)
-        quantise_queries_along_d(FIRST)
+        def quantise_queries_along_r(h, v):
+            quantise(qr_woven[h, v], E4M3, qr_codes[h][v][:], qr_scales[h][v][:])
+
         for u in range(2):
-            turn_queries(FIRST, u, turn_bank)
+            weave_queries(FIRST, u)
+            quantise_queries_along_d(FIRST, u)
+        for v in range(2):
+            turn_queries(FIRST, v, banks[4 + v])
+            weave_turned_queries(FIRST, v, banks[4 + v])
 
-        ts_slots = held([P, SLOTS], F32, "ts_slots")
-        nc.vector.tensor_copy(ts_slots[:], ts_window[:].indirect(offsets[:]))
-        ts_turned = wide_bank([P, PACK, P], "ts_turned")
+        ts_turned = quarters(banks[4])
         for b in range(PACK):
             nc.tensor.transpose(ts_turned[:, b, :], ts_slots[:, b * P : (b + 1) * P], ident[:])
         ts_cols = held([P, PACK], F32, "ts_cols")
         nc.scalar.copy(ts_cols[:], ts_turned[:, :, 0])
-        ts_rows = psum.tile([P, SLOTS], F32, name="ts_rows")
-        for b in range(PACK):
-            nc.tensor.transpose(ts_rows[:, b * P : (b + 1) * P], ts_cols[:, b : b + 1].to_broadcast([P, P]), ident[:])
 
         k_woven = [held([P, HALF, PACK], BF16, f"k_woven{a}") for a in range(2)]
         k_codes = [held([P, HALF], U32, f"k_codes{a}") for a in range(2)]
         k_scales = [held([P, HALF], U8, f"k_scales{a}") for a in range(2)]
-        list_columns = HALF // 16
+        half_lists = [offsets[:, a * HALF // 16 : (a + 1) * HALF // 16] for a in range(2)]
         for j in range(PACK):
             for a in range(2):
-                half_list = offsets[:, a * list_columns : (a + 1) * list_columns]
-                nc.vector.tensor_copy(k_woven[a][:, :, j], k_planes[j][:].indirect(half_list))
-            if j == PACK // 2 - 1:
-                quantise_queries_along_r(FIRST, 0)
+                nc.vector.tensor_copy(k_woven[a][:, :, j], k_planes[j][:].indirect(half_lists[a]))
+            if j in (1, 2):
+                quantise_queries_along_r(FIRST, j - 1)
         for a in range(2):
             quantise(k_woven[a][:].rearrange("p i j -> p (i j)"), E4M3, k_codes[a][:], k_scales[a][:])
 
         neg_us = held([P, PACK], F32, "neg_us")
         nc.gpsimd.tensor_scalar(neg_us[:], us_sb[:], -1.0, 0.0, ALU.mult, ALU.add)
-        gates = [held([P, PACK], F32, f"gates{h}") for h in range(HEADS)]
+        numerators = held([P, 2, TILES], F32, "numerators")
         for h in range(HEADS):
-            nc.gpsimd.tensor_tensor(gates[h][:], w_sb[h][:], (us_sb, neg_us)[h][:], ALU.mult)
+            nc.gpsimd.tensor_tensor(numerators[:, 0, PACK * h : PACK * (h + 1)], w_sb[h][:], us_sb[:], ALU.mult)
+        nc.gpsimd.memset(numerators[:, 1, :], -1.0)
 
-        scaled = [held([P, PACK, P], F32, f"scaled{b}") for b in range(PACK)]
+        products = [held([P, PACK, SLOTS], F32, "products0"), held([P, PACK, SLOTS], F32, "products1", "q_raw0")]
+        first_gradient = held([P, 2, HALF, PACK], BF16, "first_gradient")
+        g_woven = [[first_gradient[:, a] for a in range(2)],
+                   [held([P, HALF, PACK], BF16, f"second_gradient{a}")[:] for a in range(2)]]
+        neg_z = [held([P, SLOTS], F32, f"neg_z{t}") for t in range(PACK)]
+        scaled = [held([P, R], F32, f"scaled{b}") for b in range(PACK)]
+        means = [held([P, SLOTS], F32, f"mean{t}", tag) for t, tag in enumerate(("qd_codes1", "k_codes1", None, None))]
+        neg_max = [held([P, 1], F32, f"neg_max{n}") for n in range(TILES)]
+        totals = held([P, TILES], F32, "totals")
+        factors = held([P, 2, TILES], F32, "factors")
+        row_sums = held([P, TILES], F32, "row_sums")
+        shifts = held([P, TILES], F32, "shifts")
+        exps, turned = {}, {}
 
-        def score_second_head(b):
+        def half(a):
+            return slice(a * HALF, (a + 1) * HALF)
+
+        def as_floats(view):
+            return view.rearrange("p a b c -> p (a b c)").bitcast(F32)
+
+        centred = [held([P, PACK, HALF], F32, "centred")[:],
+                   as_floats(first_gradient[:]).rearrange("p (t i) -> p t i", t=PACK)]
+
+        def first_head_scores(t, bank):
+            for a in range(2):
+                nc.tensor.matmul_mx(out=bank[:, half(a)], lhsT=qd_codes[FIRST][:, t * P : (t + 1) * P].bitcast(E4M3),
+                                    lhsT_scale=qd_scales[FIRST][:, t * P : (t + 1) * P],
+                                    rhs=k_codes[a][:].bitcast(E4M3), rhs_scale=k_scales[a][:], start=True, stop=True)
+            nc.vector.scalar_tensor_tensor(neg_z[t][:], bank[:], neg_us[:, t : t + 1], ts_slots[:], ALU.mult, ALU.mult)
+
+        def first_head_maximum(t):
+            nc.vector.tensor_reduce(neg_max[t][:], neg_z[t][:], mybir.AxisListType.X, ALU.min)
+
+        def second_head_scores(b, bank):
             a, c = divmod(b, 2)
-            bank = wide_bank([P, R], "scores")
             nc.tensor.matmul_mx(out=bank[:], lhsT=k_codes[a][:, c * P : (c + 1) * P].bitcast(E4M3),
                                 lhsT_scale=k_scales[a][:, c * P : (c + 1) * P],
                                 rhs=qd_codes[SECOND][:].bitcast(E4M3), rhs_scale=qd_scales[SECOND][:],
                                 start=True, stop=True)
-            nc.scalar.activation(scaled[b][:], bank[:].rearrange("i (s t) -> i t s", t=PACK), ACT.Copy,
-                                 scale=ts_cols[:, b : b + 1])
+            nc.scalar.activation(scaled[b][:], bank[:], ACT.Copy, scale=ts_cols[:, b : b + 1])
 
-        dp_term = held([P, PACK, SLOTS], F32, "dp_term")
-        grad_second = held([P, PACK, SLOTS], F32, "grad_second")
-        g_woven = [[held([P, HALF, PACK], BF16, f"g_woven{h}_{a}") for a in range(2)] for h in range(HEADS)]
-        g_codes = [held([P, SLOTS], U32, f"g_codes{h}") for h in range(HEADS)]
-        g_scales = [held([P, SLOTS], U8, f"g_scales{h}") for h in range(HEADS)]
-        mean_term = held([P, PACK, SLOTS], F32, "mean_term")
-        exps, totals, inverses, coefs, products, shifts = {}, {}, {}, {}, {}, {}
+        def second_head_rows(t, bank):
+            for b in range(PACK):
+                nc.tensor.transpose(bank[:, b * P : (b + 1) * P], scaled[b][:, t * P : (t + 1) * P], ident[:])
+            nc.vector.tensor_scalar(neg_z[t][:], bank[:], neg_us[:, t : t + 1], None, ALU.mult, ALU.min,
+                                    accum_out=neg_max[PACK + t][:])
 
-        def statistic(name):
-            return ring.tile([P, 1], F32, name=name, tag=name, bufs=HEADS * PACK)
+        def exponentials(n, target):
+            exps[n] = target
+            nc.scalar.activation(target, neg_z[n % PACK][:], ACT.Exp, bias=neg_max[n][:], scale=-1.0,
+                                 accum_out=totals[:, n : n + 1])
 
-        def stage_exp(h, t):
-            rows = row_bank([P, SLOTS], "rows")
-            neg_z = ring.tile([P, SLOTS], F32, name="neg_z")
-            neg_max = statistic("neg_max")
-            if h == FIRST:
-                for a in range(2):
-                    nc.tensor.matmul_mx(out=rows[:, a * HALF : (a + 1) * HALF],
-                                        lhsT=qd_codes[h][:, t * P : (t + 1) * P].bitcast(E4M3),
-                                        lhsT_scale=qd_scales[h][:, t * P : (t + 1) * P],
-                                        rhs=k_codes[a][:].bitcast(E4M3), rhs_scale=k_scales[a][:],
-                                        start=True, stop=True)
-                nc.vector.scalar_tensor_tensor(neg_z[:], rows[:], neg_us[:, t : t + 1], ts_slots[:], ALU.mult, ALU.mult)
-                nc.vector.tensor_reduce(neg_max[:], neg_z[:], mybir.AxisListType.X, ALU.min)
-            else:
-                for b in range(PACK):
-                    nc.tensor.transpose(rows[:, b * P : (b + 1) * P], scaled[b][:, t, :], ident[:])
-                nc.vector.tensor_scalar(neg_z[:], rows[:], neg_us[:, t : t + 1], None, ALU.mult, ALU.min,
-                                        accum_out=neg_max[:])
-            exps[h, t] = ring.tile([P, SLOTS], F32, name="e", bufs=PACK + 2)
-            totals[h, t] = statistic("total")
-            nc.scalar.activation(exps[h, t][:], neg_z[:], ACT.Exp, bias=neg_max[:], scale=-1.0, accum_out=totals[h, t][:])
+        def make_factors(first, last, inverses):
+            nc.vector.reciprocal(inverses, totals[:, first:last])
+            nc.vector.tensor_tensor(factors[:, :, first:last], numerators[:, :, first:last],
+                                    inverses.unsqueeze(1).to_broadcast([P, 2, last - first]), ALU.mult)
 
-        def stage_inverse(h, t):
-            inverses[h, t] = statistic("inverse")
-            nc.vector.reciprocal(inverses[h, t][:], totals[h, t][:])
+        def make_products(n):
+            h, t = divmod(n, PACK)
+            nc.vector.scalar_tensor_tensor(products[h][:, t, :], exps[n], factors[:, 0, n : n + 1], dp_sb[h][:, t, :],
+                                           ALU.mult, ALU.mult, accum_out=row_sums[:, n : n + 1])
 
-        def stage_coef(h, t):
-            coefs[h, t] = statistic("coef")
-            nc.vector.tensor_scalar(coefs[h, t][:], inverses[h, t][:], gates[h][:, t : t + 1], None, ALU.mult)
+        def make_shifts(first, last):
+            nc.vector.tensor_tensor(shifts[:, first:last], row_sums[:, first:last], factors[:, 1, first:last], ALU.mult)
 
-        def stage_shift(h, t):
-            products[h, t] = dp_term[:, t, :] if h == FIRST else ring.tile([P, SLOTS], F32, name="products")[:]
-            row_sum = statistic("row_sum")
-            nc.vector.scalar_tensor_tensor(products[h, t], exps[h, t][:], coefs[h, t][:], dp_sb[h][:, t, :],
-                                           ALU.mult, ALU.mult, accum_out=row_sum[:])
-            shifts[h, t] = statistic("shift")
-            if h == FIRST:
-                nc.vector.tensor_scalar(shifts[h, t][:], row_sum[:], inverses[h, t][:], -1.0, ALU.mult, ALU.mult)
-            elif t == PACK - 1:
-                nc.vector.tensor_scalar(shifts[h, t][:], row_sum[:], inverses[h, t][:], None, ALU.mult)
-            else:
-                nc.scalar.activation(shifts[h, t][:], row_sum[:], ACT.Copy, scale=inverses[h, t][:])
+        def mean_term(t):
+            nc.scalar.activation(means[t][:], exps[t], ACT.Copy, scale=shifts[:, t : t + 1])
 
-        def mean_term_first_head(t):
-            nc.scalar.activation(mean_term[:, t, :], exps[FIRST, t][:], ACT.Copy, scale=shifts[FIRST, t][:])
+        def centre(t, a):
+            n = PACK + t
+            nc.vector.scalar_tensor_tensor(centred[a][:, t, :], exps[n][:, half(a)], shifts[:, n : n + 1],
+                                           products[SECOND][:, t, half(a)], ALU.mult, ALU.add)
 
-        def gradient_second_head(t):
-            nc.vector.scalar_tensor_tensor(grad_second[:, t, :], exps[SECOND, t][:], shifts[SECOND, t][:],
-                                           products[SECOND, t], ALU.mult, ALU.subtract)
-
-        g_turned = [held([P, 2, P, 2], BF16, f"g_turned{b}") for b in range(PACK)]
-
-        def turn_first_gradient(b):
-            bank = wide_bank([P, PACK, P], "grad_turned")
+        def turn_gradient(h, b, bank):
+            block = slice(b * P, (b + 1) * P)
             for t in range(PACK):
-                for opens, term in ((True, dp_term), (False, mean_term)):
-                    nc.tensor.matmul(bank[:, t, :], term[:, t, b * P : (b + 1) * P], ident[:], start=opens,
-                                     stop=not opens, is_transpose=True)
-            nc.scalar.activation(g_turned[b][:], bank[:].rearrange("i (u e) s -> i u s e", e=2), ACT.Copy,
+                if h == FIRST:
+                    for opens, term in ((True, products[FIRST][:, t, block]), (False, means[t][:, block])):
+                        nc.tensor.matmul(quarters(bank)[:, t, :], term, ident[:], start=opens, stop=not opens,
+                                         is_transpose=True)
+                else:
+                    nc.tensor.transpose(quarters(bank)[:, t, :], centred[1][:, t, b % 2 * P : (b % 2 + 1) * P], ident[:])
+            turned[h, b] = held([P, 2, P, 2], BF16, f"g_turned{h}_{b}")
+            nc.scalar.activation(turned[h, b][:], quarters(bank).rearrange("i (u e) s -> i u s e", e=2), ACT.Copy,
                                  scale=ts_cols[:, b : b + 1])
 
-        def return_first_gradient(a):
-            bank = turn_bank([P, 2, HALF], "grad_back")
+        def return_gradient(h, a, bank):
             for c in range(2):
-                words = g_turned[2 * a + c][:].rearrange("i u s e -> i (u s e)").bitcast(F32)
+                words = as_floats(turned[h, 2 * a + c][:])
                 for u in range(2):
-                    nc.tensor.transpose(bank[:, u, c * P : (c + 1) * P], words[:, u * P : (u + 1) * P], ident[:])
-            target = g_woven[FIRST][a][:].rearrange("s i t -> s (i t)").bitcast(F32).rearrange("s (i u) -> s i u", u=2)
-            nc.scalar.copy(target, bank[:].rearrange("s u i -> s i u"))
+                    nc.tensor.transpose(halves(bank)[:, u, c * P : (c + 1) * P], words[:, u * P : (u + 1) * P], ident[:])
+            target = g_woven[h][a].rearrange("s i t -> s (i t)").bitcast(F32).rearrange("s (i u) -> s i u", u=2)
+            nc.scalar.copy(target, halves(bank).rearrange("s u i -> s i u"))
 
-        def weave_second_gradient(a):
-            slots = slice(a * HALF, (a + 1) * HALF)
-            factors = ts_rows[:, slots].rearrange("p (c i) -> p c i", i=LINE).unsqueeze(2)
-            nc.vector.tensor_tensor(g_woven[SECOND][a][:].rearrange("p (c i) t -> p c t i", i=LINE),
-                                    grad_second[:, :, slots].rearrange("p t (c i) -> p c t i", i=LINE),
-                                    factors.to_broadcast([P, HALF // LINE, PACK, LINE]), ALU.mult)
+        def weave_centred():
+            ts_lines = ts_slots[:, half(0)].rearrange("p (c i) -> p c i", i=LINE).unsqueeze(2)
+            nc.vector.tensor_tensor(g_woven[SECOND][0].rearrange("p (c i) t -> p c t i", i=LINE),
+                                    centred[0].rearrange("p t (c i) -> p c t i", i=LINE),
+                                    ts_lines.to_broadcast([P, HALF // LINE, PACK, LINE]), ALU.mult)
 
-        def quantise_gradient(h):
-            for a in range(2):
-                slots = slice(a * HALF, (a + 1) * HALF)
-                quantise(g_woven[h][a][:].rearrange("p i t -> p (i t)"), E5M2, g_codes[h][:, slots], g_scales[h][:, slots])
+        def quantise_gradient(h, a):
+            columns = half(a * (1 + h))
+            quantise(g_woven[h][a].rearrange("p i t -> p (i t)"), E5M2, g_codes[h][:, columns], g_scales[h][:, columns])
 
-        sums = {}
-
-        def key_gradient_pass(j, h):
-            nc.tensor.matmul_mx(out=sums[j][:], lhsT=qr_codes[h, j // 2][:, j % 2 * P : (j % 2 + 1) * P].bitcast(E4M3),
-                                lhsT_scale=qr_scales[h][:, j * P : (j + 1) * P],
-                                rhs=g_codes[h][:].bitcast(E5M2), rhs_scale=g_scales[h][:],
-                                start=(h == FIRST), stop=(h == SECOND))
-
-        tiles = [(h, t) for h in range(HEADS) for t in range(PACK)]
-        last = len(tiles)
-        for n in range(last + 2):
-            if 1 <= n <= last:
-                stage_inverse(*tiles[n - 1])
-            if n < last:
-                stage_exp(*tiles[n])
-            if 1 <= n <= last:
-                stage_coef(*tiles[n - 1])
-            if n == 1:
-                weave_queries(SECOND)
-                quantise_queries_along_d(SECOND)
-            if n in (PACK - 2, PACK - 1):
-                for b in range(2 * (n - PACK + 2), 2 * (n - PACK + 3)):
-                    score_second_head(b)
-            if PACK + 2 <= n <= last:
-                gradient_second_head(n - 2 - PACK)
-            if 1 <= n <= last:
-                stage_shift(*tiles[n - 1])
-            if n in (PACK, PACK + 1):
-                for t in range(2 * (n - PACK), 2 * (n - PACK + 1)):
-                    mean_term_first_head(t)
-            if n == PACK + 3:
-                turn_queries(SECOND, 0, turn_bank)
-            if n == last:
-                quantise_queries_along_r(SECOND, 0)
-            if n in (PACK + 2, PACK + 3):
-                a = n - PACK - 2
-                turn_first_gradient(2 * a)
-                turn_first_gradient(2 * a + 1)
-                return_first_gradient(a)
-            if n == last:
-                quantise_gradient(FIRST)
-                for j in range(2):
-                    sums[j] = turn_bank([P, SLOTS], "sums")
-                    key_gradient_pass(j, FIRST)
-                turn_queries(SECOND, 1, row_bank)
-            if n == last + 1:
-                gradient_second_head(PACK - 1)
-        for a in range(2):
-            weave_second_gradient(a)
-        quantise_gradient(SECOND)
-
-        late_codes = keep.tile([P, HEADS, 2 * P], U32, name="late_codes", tag="grad_second", align_bytes=64)
-        for h in range(HEADS):
-            qr_codes[h, 1] = late_codes[:, h, :]
-            quantise_queries_along_r(h, 1)
+        def key_gradient_pass(bank, j, h, first_column, start, stop):
+            columns = slice(first_column, first_column + SLOTS)
+            planes = slice(j % 2 * P, (j % 2 + 1) * P)
+            nc.tensor.matmul_mx(out=bank[:], lhsT=qr_codes[h][j // 2][:, planes].bitcast(E4M3),
+                                lhsT_scale=qr_scales[h][j // 2][:, planes],
+                                rhs=g_codes[h][:, columns].bitcast(E5M2), rhs_scale=g_scales[h][:, columns],
+                                start=start, stop=stop)
 
         out_planes = out.rearrange("(p j) c -> j p c", j=PACK)
-        for j in range(PACK):
-            if j not in sums:
-                sums[j] = wide_bank([P, SLOTS], "late_sums")
-                key_gradient_pass(j, FIRST)
-            key_gradient_pass(j, SECOND)
-            dk = held([P, SLOTS], F32, f"dk{j}")
-            nc.scalar.copy(dk[:], sums[j][:])
-            nc.vector.tensor_copy(windows[j][:].indirect(offsets[:]), dk[:])
+
+        for t in range(2):
+            first_head_scores(t, banks[t])
+        for t in range(2):
+            first_head_maximum(t)
+        for u in range(2):
+            weave_queries(SECOND, u)
+            quantise_queries_along_d(SECOND, u)
+        for t in range(2, PACK):
+            first_head_scores(t, banks[t])
+        for t in range(2, PACK):
+            first_head_maximum(t)
+        for t in range(PACK):
+            exponentials(t, q_raw[SECOND][:, t, :])
+        turn_queries(SECOND, 0, banks[7])
+        qr_woven[SECOND, 0] = held([P, 2 * P * PACK], BF16, "second_qr_woven")[:]
+        weave_turned_queries(SECOND, 0, banks[7])
+        for b, bank in enumerate((banks[4], banks[5], banks[0], banks[1])):
+            second_head_scores(b, bank)
+        for first in (0, 2):
+            make_factors(first, first + 2, held([P, 2], F32, f"inverses{first}")[:])
+            for n in range(first, first + 2):
+                make_products(n)
+        quantise_queries_along_r(SECOND, 0)
+        for first in (0, 2):
+            make_shifts(first, first + 2)
+        for t, bank in enumerate((banks[2], banks[3], banks[4], banks[5])):
+            second_head_rows(t, bank)
+            exponentials(PACK + t, held([P, SLOTS], F32, f"e{t}")[:])
+        for t in range(PACK):
+            mean_term(t)
+        make_factors(4, 6, neg_us[:, 2:4])
+        for n in range(4, 6):
+            make_products(n)
+        make_factors(6, TILES, held([P, 2], F32, "last_inverses")[:])
+        make_shifts(4, 6)
+        for n in range(6, TILES):
+            make_products(n)
+        for b, bank in enumerate((banks[0], banks[1], banks[6], banks[7])):
+            turn_gradient(FIRST, b, bank)
+        for a, bank in enumerate((banks[2], banks[3])):
+            return_gradient(FIRST, a, bank)
+        centre(0, 0)
+        make_shifts(6, TILES)
+        for t in range(1, PACK):
+            centre(t, 0)
+        weave_centred()
+        quantise(first_gradient[:].rearrange("p a i t -> p (a i t)"), E5M2, g_codes[FIRST][:], g_scales[FIRST][:])
+        quantise_gradient(SECOND, 0)
+        partial = [held([P, HALF], F32, f"partial{j}") for j in range(EARLY)]
+
+        def early_plane(j, dk):
+            key_gradient_pass(banks[j], j, FIRST, 0, True, False)
+            key_gradient_pass(banks[j], j, SECOND, 0, False, True)
+            nc.scalar.copy(dk, banks[j][:, half(0)])
+            nc.vector.tensor_copy(windows[j][:].indirect(half_lists[0]), dk)
+
+        early_plane(0, held([P, HALF], F32, "early0")[:])
+        qr_woven[SECOND, 1] = held([P, 2 * P * PACK], BF16, "late_qr_woven")[:]
+        turn_queries(SECOND, 1, banks[6])
+        weave_turned_queries(SECOND, 1, banks[6])
+        for t in range(PACK):
+            centre(t, 1)
+        early_plane(1, held([P, HALF], F32, "early1")[:])
+        for b, bank in ((2, banks[3]), (3, banks[4])):
+            turn_gradient(SECOND, b, bank)
+        return_gradient(SECOND, 1, banks[5])
+        quantise_queries_along_r(SECOND, 1)
+        quantise_gradient(SECOND, 1)
+        early_plane(2, as_floats(turned[SECOND, PACK - 1][:]))
+        for j, bank in enumerate((banks[3], banks[4], banks[6])):
+            key_gradient_pass(bank, j, SECOND, HALF, True, True)
+            nc.scalar.copy(partial[j][:], banks[j][:, half(1)])
+            late = held([P, HALF], F32, f"late{j}")
+            nc.scalar.copy(late[:], bank[:, half(1)])
+            nc.vector.tensor_tensor(windows[j][:].indirect(half_lists[1]), partial[j][:], late[:], ALU.add)
             nc.sync.dma_start(out_planes[j], windows[j][:])
+        key_gradient_pass(banks[7], EARLY, FIRST, 0, True, False)
+        key_gradient_pass(banks[7], EARLY, SECOND, 0, False, False)
+        key_gradient_pass(banks[7], EARLY, SECOND, HALF, False, True)
+        dk = held([P, SLOTS], F32, "dk")
+        nc.scalar.copy(dk[:], banks[7][:])
+        nc.vector.tensor_copy(windows[EARLY][:].indirect(offsets[:]), dk[:])
+        nc.sync.dma_start(out_planes[EARLY], windows[EARLY][:])

@@ -50,7 +50,6 @@ def tile_attend_ggqa_sm_k_kernel(tc, q1, q2, kT, dp1, dp2, us, ts, w1, w2, offs,
             return bank[:].rearrange("p (c i) -> p c i", c=2)
 
         offsets = keep.tile([P, SLOTS // 16], U16, name="offsets")
-        nc.sync.dma_start(offsets[:], offs)
 
         q_raw = [held([P, PACK, R], F32, f"q_raw{h}") for h in range(HEADS)]
         dp_sb = [held([P, PACK, SLOTS], F32, f"dp_sb{h}") for h in range(HEADS)]
@@ -65,6 +64,7 @@ def tile_attend_ggqa_sm_k_kernel(tc, q1, q2, kT, dp1, dp2, us, ts, w1, w2, offs,
         ts_runs = held([P, RUN], F32, "ts_runs")
         nc.sync.dma_start(ts_runs[:], ts[0:1, :].rearrange("o (p c) -> p (o c)", c=RUN))
         nc.sync.dma_start(q_raw[FIRST][:], q1.rearrange("(p j) r -> p j r", j=PACK))
+        nc.sync.dma_start(offsets[:], offs)
         k_hbm = kT.rearrange("(p j) t -> j p t", j=PACK)
         for j in range(PACK):
             nc.sync.dma_start(k_planes[j][:], k_hbm[j])
@@ -80,11 +80,14 @@ def tile_attend_ggqa_sm_k_kernel(tc, q1, q2, kT, dp1, dp2, us, ts, w1, w2, offs,
         nc.gpsimd.memset(g_codes[SECOND][:, HALF : 2 * HALF], 0)
         nc.gpsimd.memset(g_scales[SECOND][:, HALF : 2 * HALF].bitcast(U32), 0)
 
-        windows = [held([P, TOKENS], F32, f"window{j}") for j in range(PACK)]
-        for j in range(PACK):
-            for half in range(2):
-                columns = slice(half * TOKENS // 2, (half + 1) * TOKENS // 2)
-                (nc.vector if j == 0 else nc.gpsimd).memset(windows[j][:, columns].bitcast(I32), 0)
+        windows = {}
+
+        def zero_window(j, engine, tag=None):
+            windows[j] = held([P, TOKENS], F32, f"window{j}", tag)
+            for columns in (slice(0, TOKENS // 2), slice(TOKENS // 2, TOKENS)):
+                engine.memset(windows[j][:, columns].bitcast(I32), 0)
+
+        zero_window(PACK - 1, nc.vector)
 
         for g in range(RUN // PACK):
             bank = quarters(spread_banks[g])
@@ -107,7 +110,7 @@ def tile_attend_ggqa_sm_k_kernel(tc, q1, q2, kT, dp1, dp2, us, ts, w1, w2, offs,
         qd_codes = [held([P, R], U32, f"qd_codes{h}", "ts_window" if h == FIRST else None) for h in range(HEADS)]
         qd_scales = [held([P, R], U8, f"qd_scales{h}") for h in range(HEADS)]
         qr_woven = {(FIRST, v): held([P, 2 * P * PACK], BF16, f"qr_woven{v}")[:] for v in range(2)}
-        qr_codes = [[held([P, 2 * P], U32, f"qr_codes{h}_{v}", f"k_plane{v + 1}" if h == FIRST else None) for v in range(2)]
+        qr_codes = [[held([P, 2 * P], U32, f"qr_codes{h}_{v}", f"k_plane{2 * v + 1}" if h == FIRST else None) for v in range(2)]
                     for h in range(HEADS)]
         qr_scales = [[held([P, 2 * P], U8, f"qr_scales{h}_{v}") for v in range(2)] for h in range(HEADS)]
 
@@ -151,10 +154,11 @@ def tile_attend_ggqa_sm_k_kernel(tc, q1, q2, kT, dp1, dp2, us, ts, w1, w2, offs,
         for j in range(PACK):
             for a in range(2):
                 nc.vector.tensor_copy(k_woven[a][:, :, j], k_planes[j][:].indirect(half_lists[a]))
-            if j in (1, 2):
-                quantise_queries_along_r(FIRST, j - 1)
+            if j == 1:
+                quantise_queries_along_r(FIRST, 0)
         for a in range(2):
             quantise(k_woven[a][:].rearrange("p i j -> p (i j)"), E4M3, k_codes[a][:], k_scales[a][:])
+        quantise_queries_along_r(FIRST, 1)
 
         neg_us = held([P, PACK], F32, "neg_us")
         nc.gpsimd.tensor_scalar(neg_us[:], us_sb[:], -1.0, 0.0, ALU.mult, ALU.add)
@@ -168,7 +172,7 @@ def tile_attend_ggqa_sm_k_kernel(tc, q1, q2, kT, dp1, dp2, us, ts, w1, w2, offs,
         g_woven = [[first_gradient[:, a] for a in range(2)],
                    [held([P, HALF, PACK], BF16, f"second_gradient{a}")[:] for a in range(2)]]
         neg_z = [held([P, SLOTS], F32, f"neg_z{t}") for t in range(PACK)]
-        scaled = [held([P, R], F32, f"scaled{b}") for b in range(PACK)]
+        scaled = held([P, PACK, R], F32, "scaled")
         means = [held([P, SLOTS], F32, f"mean{t}", tag) for t, tag in enumerate(("qd_codes1", "k_codes1", None, None))]
         neg_max = [held([P, 1], F32, f"neg_max{n}") for n in range(TILES)]
         totals = held([P, TILES], F32, "totals")
@@ -202,11 +206,11 @@ def tile_attend_ggqa_sm_k_kernel(tc, q1, q2, kT, dp1, dp2, us, ts, w1, w2, offs,
                                 lhsT_scale=k_scales[a][:, c * P : (c + 1) * P],
                                 rhs=qd_codes[SECOND][:].bitcast(E4M3), rhs_scale=qd_scales[SECOND][:],
                                 start=True, stop=True)
-            nc.scalar.activation(scaled[b][:], bank[:], ACT.Copy, scale=ts_cols[:, b : b + 1])
+            nc.scalar.activation(scaled[:, b, :], bank[:], ACT.Copy, scale=ts_cols[:, b : b + 1])
 
         def second_head_rows(t, bank):
             for b in range(PACK):
-                nc.tensor.transpose(bank[:, b * P : (b + 1) * P], scaled[b][:, t * P : (t + 1) * P], ident[:])
+                nc.tensor.transpose(bank[:, b * P : (b + 1) * P], scaled[:, b, t * P : (t + 1) * P], ident[:])
             nc.vector.tensor_scalar(neg_z[t][:], bank[:], neg_us[:, t : t + 1], None, ALU.mult, ALU.min,
                                     accum_out=neg_max[PACK + t][:])
 
@@ -307,6 +311,8 @@ def tile_attend_ggqa_sm_k_kernel(tc, q1, q2, kT, dp1, dp2, us, ts, w1, w2, offs,
             exponentials(PACK + t, held([P, SLOTS], F32, f"e{t}")[:])
         for t in range(PACK):
             mean_term(t)
+        for j, tag in enumerate(("dp_sb0", "scaled", "q_raw1")):
+            zero_window(j, nc.gpsimd, tag)
         make_factors(4, 6, neg_us[:, 2:4])
         for n in range(4, 6):
             make_products(n)

@@ -75,10 +75,11 @@ def tile_attend_ggqa_sm_k_kernel(tc, q1, q2, kT, dp1, dp2, us, ts, w1, w2, offs,
         for h, dp in enumerate((dp1, dp2)):
             nc.sync.dma_start(dp_sb[h][:], dp.rearrange("(s t) i -> s t i", t=PACK))
 
-        g_codes = [held([P, (2 + h) * HALF], U32, f"g_codes{h}") for h in range(HEADS)]
-        g_scales = [held([P, (2 + h) * HALF], U8, f"g_scales{h}") for h in range(HEADS)]
-        nc.gpsimd.memset(g_codes[SECOND][:, HALF : 2 * HALF], 0)
-        nc.gpsimd.memset(g_scales[SECOND][:, HALF : 2 * HALF].bitcast(U32), 0)
+        g_codes = [held([P, SLOTS], U32, f"g_codes{h}") for h in range(HEADS)]
+        g_scales = [held([P, SLOTS], U8, f"g_scales{h}") for h in range(HEADS)]
+        for h in range(HEADS):
+            nc.gpsimd.memset(g_codes[h][:, HALF:], 0)
+            nc.gpsimd.memset(g_scales[h][:, HALF:].bitcast(U32), 0)
 
         windows = {}
 
@@ -88,6 +89,8 @@ def tile_attend_ggqa_sm_k_kernel(tc, q1, q2, kT, dp1, dp2, us, ts, w1, w2, offs,
                 engine.memset(windows[j][:, columns].bitcast(I32), 0)
 
         zero_window(PACK - 1, nc.vector)
+        for j in range(PACK - 1):
+            zero_window(j, nc.gpsimd)
 
         for g in range(RUN // PACK):
             bank = quarters(spread_banks[g])
@@ -168,10 +171,9 @@ def tile_attend_ggqa_sm_k_kernel(tc, q1, q2, kT, dp1, dp2, us, ts, w1, w2, offs,
         nc.gpsimd.memset(numerators[:, 1, :], -1.0)
 
         products = [held([P, PACK, SLOTS], F32, "products0"), held([P, PACK, SLOTS], F32, "products1", "q_raw0")]
-        first_gradient = held([P, 2, HALF, PACK], BF16, "first_gradient")
-        g_woven = [[first_gradient[:, a] for a in range(2)],
-                   [held([P, HALF, PACK], BF16, f"second_gradient{a}")[:] for a in range(2)]]
-        neg_z = [held([P, SLOTS], F32, f"neg_z{t}") for t in range(PACK)]
+        first_gradient = [held([P, HALF, PACK], BF16, f"first_gradient{a}")[:] for a in range(2)]
+        g_woven = [first_gradient, [first_gradient[0], held([P, HALF, PACK], BF16, "second_gradient")[:]]]
+        neg_z = [held([P, SLOTS], F32, f"neg_z{t}")[:] for t in range(2)] + [q_raw[SECOND][:, t, :] for t in range(2, PACK)]
         scaled = held([P, PACK, R], F32, "scaled")
         means = [held([P, SLOTS], F32, f"mean{t}", tag) for t, tag in enumerate(("qd_codes1", "k_codes1", None, None))]
         neg_max = [held([P, 1], F32, f"neg_max{n}") for n in range(TILES)]
@@ -187,18 +189,17 @@ def tile_attend_ggqa_sm_k_kernel(tc, q1, q2, kT, dp1, dp2, us, ts, w1, w2, offs,
         def as_floats(view):
             return view.rearrange("p a b c -> p (a b c)").bitcast(F32)
 
-        centred = [held([P, PACK, HALF], F32, "centred")[:],
-                   as_floats(first_gradient[:]).rearrange("p (t i) -> p t i", t=PACK)]
+        centred = held([P, PACK, HALF], F32, "centred")
 
         def first_head_scores(t, bank):
             for a in range(2):
                 nc.tensor.matmul_mx(out=bank[:, half(a)], lhsT=qd_codes[FIRST][:, t * P : (t + 1) * P].bitcast(E4M3),
                                     lhsT_scale=qd_scales[FIRST][:, t * P : (t + 1) * P],
                                     rhs=k_codes[a][:].bitcast(E4M3), rhs_scale=k_scales[a][:], start=True, stop=True)
-            nc.vector.scalar_tensor_tensor(neg_z[t][:], bank[:], neg_us[:, t : t + 1], ts_slots[:], ALU.mult, ALU.mult)
+            nc.vector.scalar_tensor_tensor(neg_z[t], bank[:], neg_us[:, t : t + 1], ts_slots[:], ALU.mult, ALU.mult)
 
         def first_head_maximum(t):
-            nc.vector.tensor_reduce(neg_max[t][:], neg_z[t][:], mybir.AxisListType.X, ALU.min)
+            nc.vector.tensor_reduce(neg_max[t][:], neg_z[t], mybir.AxisListType.X, ALU.min)
 
         def second_head_scores(b, bank):
             a, c = divmod(b, 2)
@@ -211,12 +212,12 @@ def tile_attend_ggqa_sm_k_kernel(tc, q1, q2, kT, dp1, dp2, us, ts, w1, w2, offs,
         def second_head_rows(t, bank):
             for b in range(PACK):
                 nc.tensor.transpose(bank[:, b * P : (b + 1) * P], scaled[:, b, t * P : (t + 1) * P], ident[:])
-            nc.vector.tensor_scalar(neg_z[t][:], bank[:], neg_us[:, t : t + 1], None, ALU.mult, ALU.min,
+            nc.vector.tensor_scalar(neg_z[t], bank[:], neg_us[:, t : t + 1], None, ALU.mult, ALU.min,
                                     accum_out=neg_max[PACK + t][:])
 
         def exponentials(n, target):
             exps[n] = target
-            nc.scalar.activation(target, neg_z[n % PACK][:], ACT.Exp, bias=neg_max[n][:], scale=-1.0,
+            nc.scalar.activation(target, neg_z[n % PACK], ACT.Exp, bias=neg_max[n][:], scale=-1.0,
                                  accum_out=totals[:, n : n + 1])
 
         def make_factors(first, last, inverses):
@@ -237,18 +238,19 @@ def tile_attend_ggqa_sm_k_kernel(tc, q1, q2, kT, dp1, dp2, us, ts, w1, w2, offs,
 
         def centre(t, a):
             n = PACK + t
-            nc.vector.scalar_tensor_tensor(centred[a][:, t, :], exps[n][:, half(a)], shifts[:, n : n + 1],
+            nc.vector.scalar_tensor_tensor(centred[:, t, :], exps[n][:, half(a)], shifts[:, n : n + 1],
                                            products[SECOND][:, t, half(a)], ALU.mult, ALU.add)
 
-        def turn_gradient(h, b, bank):
-            block = slice(b * P, (b + 1) * P)
+        def turn_term(term, t, blocks, opens):
+            for b in blocks:
+                nc.tensor.matmul(quarters(turn_banks[b])[:, t, :], term[:, b * P : (b + 1) * P], ident[:],
+                                 start=opens and t == 0, stop=not opens and t == PACK - 1, is_transpose=True)
+
+        def turn_centred(c, bank):
             for t in range(PACK):
-                if h == FIRST:
-                    for opens, term in ((True, products[FIRST][:, t, block]), (False, means[t][:, block])):
-                        nc.tensor.matmul(quarters(bank)[:, t, :], term, ident[:], start=opens, stop=not opens,
-                                         is_transpose=True)
-                else:
-                    nc.tensor.transpose(quarters(bank)[:, t, :], centred[1][:, t, b % 2 * P : (b % 2 + 1) * P], ident[:])
+                nc.tensor.transpose(quarters(bank)[:, t, :], centred[:, t, c * P : (c + 1) * P], ident[:])
+
+        def round_turned(h, b, bank):
             turned[h, b] = held([P, 2, P, 2], BF16, f"g_turned{h}_{b}")
             nc.scalar.activation(turned[h, b][:], quarters(bank).rearrange("i (u e) s -> i u s e", e=2), ACT.Copy,
                                  scale=ts_cols[:, b : b + 1])
@@ -264,19 +266,18 @@ def tile_attend_ggqa_sm_k_kernel(tc, q1, q2, kT, dp1, dp2, us, ts, w1, w2, offs,
         def weave_centred():
             ts_lines = ts_slots[:, half(0)].rearrange("p (c i) -> p c i", i=LINE).unsqueeze(2)
             nc.vector.tensor_tensor(g_woven[SECOND][0].rearrange("p (c i) t -> p c t i", i=LINE),
-                                    centred[0].rearrange("p t (c i) -> p c t i", i=LINE),
+                                    centred[:].rearrange("p t (c i) -> p c t i", i=LINE),
                                     ts_lines.to_broadcast([P, HALF // LINE, PACK, LINE]), ALU.mult)
 
         def quantise_gradient(h, a):
-            columns = half(a * (1 + h))
+            columns = half(a)
             quantise(g_woven[h][a].rearrange("p i t -> p (i t)"), E5M2, g_codes[h][:, columns], g_scales[h][:, columns])
 
-        def key_gradient_pass(bank, j, h, first_column, start, stop):
-            columns = slice(first_column, first_column + SLOTS)
+        def key_gradient_pass(bank, j, h, start, stop):
             planes = slice(j % 2 * P, (j % 2 + 1) * P)
             nc.tensor.matmul_mx(out=bank[:], lhsT=qr_codes[h][j // 2][:, planes].bitcast(E4M3),
                                 lhsT_scale=qr_scales[h][j // 2][:, planes],
-                                rhs=g_codes[h][:, columns].bitcast(E5M2), rhs_scale=g_scales[h][:, columns],
+                                rhs=g_codes[h][:].bitcast(E5M2), rhs_scale=g_scales[h][:],
                                 start=start, stop=stop)
 
         out_planes = out.rearrange("(p j) c -> j p c", j=PACK)
@@ -290,19 +291,22 @@ def tile_attend_ggqa_sm_k_kernel(tc, q1, q2, kT, dp1, dp2, us, ts, w1, w2, offs,
             quantise_queries_along_d(SECOND, u)
         for t in range(2, PACK):
             first_head_scores(t, banks[t])
+        for t in range(2):
+            exponentials(t, q_raw[SECOND][:, t, :])
+        make_factors(0, 2, held([P, 2], F32, "inverses0")[:])
         for t in range(2, PACK):
             first_head_maximum(t)
-        for t in range(PACK):
-            exponentials(t, q_raw[SECOND][:, t, :])
+            exponentials(t, held([P, SLOTS], F32, f"first_e{t}")[:])
         turn_queries(SECOND, 0, banks[7])
         qr_woven[SECOND, 0] = held([P, 2 * P * PACK], BF16, "second_qr_woven")[:]
         weave_turned_queries(SECOND, 0, banks[7])
         for b, bank in enumerate((banks[4], banks[5], banks[0], banks[1])):
             second_head_scores(b, bank)
-        for first in (0, 2):
-            make_factors(first, first + 2, held([P, 2], F32, f"inverses{first}")[:])
-            for n in range(first, first + 2):
-                make_products(n)
+        for n in range(2):
+            make_products(n)
+        make_factors(2, PACK, held([P, 2], F32, "inverses2")[:])
+        for n in range(2, PACK):
+            make_products(n)
         quantise_queries_along_r(SECOND, 0)
         for first in (0, 2):
             make_shifts(first, first + 2)
@@ -311,58 +315,76 @@ def tile_attend_ggqa_sm_k_kernel(tc, q1, q2, kT, dp1, dp2, us, ts, w1, w2, offs,
             exponentials(PACK + t, held([P, SLOTS], F32, f"e{t}")[:])
         for t in range(PACK):
             mean_term(t)
-        for j, tag in enumerate(("dp_sb0", "scaled", "q_raw1")):
-            zero_window(j, nc.gpsimd, tag)
         make_factors(4, 6, neg_us[:, 2:4])
-        for n in range(4, 6):
-            make_products(n)
+        make_products(4)
         make_factors(6, TILES, held([P, 2], F32, "last_inverses")[:])
+        make_products(5)
         make_shifts(4, 6)
         for n in range(6, TILES):
             make_products(n)
-        for b, bank in enumerate((banks[0], banks[1], banks[6], banks[7])):
-            turn_gradient(FIRST, b, bank)
-        for a, bank in enumerate((banks[2], banks[3])):
-            return_gradient(FIRST, a, bank)
+        turn_banks = (banks[6], banks[7], banks[0], banks[1])
+
+        def turn_first(blocks, opens):
+            for t in range(PACK):
+                turn_term(products[FIRST][:, t, :] if opens else means[t][:], t, blocks, opens)
+
+        turn_first(range(2), True)
+        turn_first(range(2), False)
+        for b in range(2):
+            round_turned(FIRST, b, turn_banks[b])
+        turn_first(range(2, PACK), True)
+        return_gradient(FIRST, 0, banks[2])
+        turn_first(range(2, PACK), False)
+        for b in range(2, PACK):
+            round_turned(FIRST, b, turn_banks[b])
         centre(0, 0)
         make_shifts(6, TILES)
         for t in range(1, PACK):
             centre(t, 0)
+        quantise_gradient(FIRST, 0)
+        early_banks = (banks[4], banks[5], banks[6])
+        key_gradient_pass(early_banks[0], 0, FIRST, True, False)
+        return_gradient(FIRST, 1, banks[3])
+        qr_woven[SECOND, 1] = held([P, 2 * P * PACK], BF16, "late_qr_woven")[:]
+        turn_queries(SECOND, 1, banks[7])
+        weave_turned_queries(SECOND, 1, banks[7])
         weave_centred()
-        quantise(first_gradient[:].rearrange("p a i t -> p (a i t)"), E5M2, g_codes[FIRST][:], g_scales[FIRST][:])
         quantise_gradient(SECOND, 0)
-        partial = [held([P, HALF], F32, f"partial{j}") for j in range(EARLY)]
+        key_gradient_pass(early_banks[0], 0, SECOND, False, True)
 
         def early_plane(j, dk):
-            key_gradient_pass(banks[j], j, FIRST, 0, True, False)
-            key_gradient_pass(banks[j], j, SECOND, 0, False, True)
-            nc.scalar.copy(dk, banks[j][:, half(0)])
+            nc.scalar.copy(dk, early_banks[j][:, half(0)])
             nc.vector.tensor_copy(windows[j][:].indirect(half_lists[0]), dk)
 
-        early_plane(0, held([P, HALF], F32, "early0")[:])
-        qr_woven[SECOND, 1] = held([P, 2 * P * PACK], BF16, "late_qr_woven")[:]
-        turn_queries(SECOND, 1, banks[6])
-        weave_turned_queries(SECOND, 1, banks[6])
+        quantise_gradient(FIRST, 1)
+        quantise_queries_along_r(SECOND, 1)
         for t in range(PACK):
             centre(t, 1)
+        early_plane(0, held([P, HALF], F32, "early0")[:])
+        for h in range(HEADS):
+            key_gradient_pass(early_banks[1], 1, h, h == FIRST, h == SECOND)
+        for c in range(2):
+            turn_centred(c, banks[c])
         early_plane(1, held([P, HALF], F32, "early1")[:])
-        for b, bank in ((2, banks[3]), (3, banks[4])):
-            turn_gradient(SECOND, b, bank)
-        return_gradient(SECOND, 1, banks[5])
-        quantise_queries_along_r(SECOND, 1)
+        for c in range(2):
+            round_turned(SECOND, 2 + c, banks[c])
+        for h in range(HEADS):
+            key_gradient_pass(early_banks[2], 2, h, h == FIRST, h == SECOND)
+        return_gradient(SECOND, 1, banks[2])
         quantise_gradient(SECOND, 1)
         early_plane(2, as_floats(turned[SECOND, PACK - 1][:]))
-        for j, bank in enumerate((banks[3], banks[4], banks[6])):
-            key_gradient_pass(bank, j, SECOND, HALF, True, True)
-            nc.scalar.copy(partial[j][:], banks[j][:, half(1)])
-            late = held([P, HALF], F32, f"late{j}")
-            nc.scalar.copy(late[:], bank[:, half(1)])
-            nc.vector.tensor_tensor(windows[j][:].indirect(half_lists[1]), partial[j][:], late[:], ALU.add)
+        for j, bank in enumerate((banks[3], banks[7], banks[0], banks[1])):
+            adds = 0 < j < EARLY
+            columns, entries = (half(1), half_lists[1]) if j < EARLY else (slice(0, SLOTS), offsets[:])
+            if not adds:
+                key_gradient_pass(bank, j, FIRST, True, False)
+            key_gradient_pass(bank, j, SECOND, adds, True)
+            late = held([P, columns.stop - columns.start], F32, f"late{j}")
+            nc.scalar.copy(late[:], bank[:, columns])
+            if adds:
+                partial = held([P, HALF], F32, f"partial{j}")
+                nc.scalar.copy(partial[:], early_banks[j][:, half(1)])
+                nc.vector.tensor_tensor(windows[j][:].indirect(entries), partial[:], late[:], ALU.add)
+            else:
+                nc.vector.tensor_copy(windows[j][:].indirect(entries), late[:])
             nc.sync.dma_start(out_planes[j], windows[j][:])
-        key_gradient_pass(banks[7], EARLY, FIRST, 0, True, False)
-        key_gradient_pass(banks[7], EARLY, SECOND, 0, False, False)
-        key_gradient_pass(banks[7], EARLY, SECOND, HALF, False, True)
-        dk = held([P, SLOTS], F32, "dk")
-        nc.scalar.copy(dk[:], banks[7][:])
-        nc.vector.tensor_copy(windows[EARLY][:].indirect(offsets[:]), dk[:])
-        nc.sync.dma_start(out_planes[EARLY], windows[EARLY][:])

@@ -191,6 +191,8 @@ def tile_attend_ggqa_sm_k_kernel(tc, q1, q2, kT, dp1, dp2, us, ts, w1, w2, offs,
 
         centred = held([P, PACK, HALF], F32, "centred")
 
+        second_means = held([P, PACK, HALF], F32, "second_means")
+
         def first_head_scores(t, bank):
             for a in range(2):
                 nc.tensor.matmul_mx(out=bank[:, half(a)], lhsT=qd_codes[FIRST][:, t * P : (t + 1) * P].bitcast(E4M3),
@@ -246,9 +248,16 @@ def tile_attend_ggqa_sm_k_kernel(tc, q1, q2, kT, dp1, dp2, us, ts, w1, w2, offs,
                 nc.tensor.matmul(quarters(turn_banks[b])[:, t, :], term[:, b * P : (b + 1) * P], ident[:],
                                  start=opens and t == 0, stop=not opens and t == PACK - 1, is_transpose=True)
 
+        def second_mean_term(t):
+            nc.scalar.activation(second_means[:, t, :], exps[PACK + t][:, half(1)], ACT.Copy,
+                                 scale=shifts[:, PACK + t : PACK + t + 1])
+
         def turn_centred(c, bank):
+            block = slice(c * P, (c + 1) * P)
             for t in range(PACK):
-                nc.tensor.transpose(quarters(bank)[:, t, :], centred[:, t, c * P : (c + 1) * P], ident[:])
+                for opens, term in ((True, products[SECOND][:, t, half(1)]), (False, second_means[:, t, :])):
+                    nc.tensor.matmul(quarters(bank)[:, t, :], term[:, block], ident[:], start=opens, stop=not opens,
+                                     is_transpose=True)
 
         def round_turned(h, b, bank):
             turned[h, b] = held([P, 2, P, 2], BF16, f"g_turned{h}_{b}")
@@ -359,7 +368,7 @@ def tile_attend_ggqa_sm_k_kernel(tc, q1, q2, kT, dp1, dp2, us, ts, w1, w2, offs,
         quantise_gradient(FIRST, 1)
         quantise_queries_along_r(SECOND, 1)
         for t in range(PACK):
-            centre(t, 1)
+            second_mean_term(t)
         early_plane(0, held([P, HALF], F32, "early0")[:])
         for h in range(HEADS):
             key_gradient_pass(early_banks[1], 1, h, h == FIRST, h == SECOND)

@@ -104,6 +104,7 @@ def tile_attend_ggqa_sm_k_kernel(tc, q1, q2, kT, dp1, dp2, us, ts, w1, w2, offs,
         ts_slots = held([P, SLOTS], F32, "ts_slots")
         nc.vector.tensor_copy(ts_slots[:], ts_window[:].indirect(offsets[:]))
 
+        centred = held([P, PACK, HALF], F32, "centred")
         def quantise(source, fmt, codes, scales):
             nc.vector.quantize_mx(out=codes.bitcast(fmt), scales=scales, in_=source)
 
@@ -113,8 +114,9 @@ def tile_attend_ggqa_sm_k_kernel(tc, q1, q2, kT, dp1, dp2, us, ts, w1, w2, offs,
         qd_codes = [held([P, R], U32, f"qd_codes{h}", "ts_window" if h == FIRST else None) for h in range(HEADS)]
         qd_scales = [held([P, R], U8, f"qd_scales{h}") for h in range(HEADS)]
         qr_woven = {(FIRST, v): held([P, 2 * P * PACK], BF16, f"qr_woven{v}")[:] for v in range(2)}
-        qr_codes = [[held([P, 2 * P], U32, f"qr_codes{h}_{v}", f"k_plane{2 * v + 1}" if h == FIRST else None) for v in range(2)]
-                    for h in range(HEADS)]
+        qr_first = held([P, 2, 2 * P], U32, "qr_codes0", "k_plane1")
+        qr_codes = [[qr_first[:, v, :] for v in range(2)],
+                    [held([P, 2 * P], U32, f"qr_codes1_{v}", "ts_slots" if v else None)[:] for v in range(2)]]
         qr_scales = [[held([P, 2 * P], U8, f"qr_scales{h}_{v}") for v in range(2)] for h in range(HEADS)]
 
         def weave_queries(h, u):
@@ -134,8 +136,17 @@ def tile_attend_ggqa_sm_k_kernel(tc, q1, q2, kT, dp1, dp2, us, ts, w1, w2, offs,
             nc.scalar.copy(qr_woven[h, v].rearrange("s (e p t) -> s e p t", e=2, t=PACK),
                            bank[:].bitcast(BF16).rearrange("s (t p e) -> s e p t", t=PACK, e=2))
 
+        def turn_rounded_queries(rounded, v, bank):
+            for e in range(2):
+                words = rounded[:, 2 * v + e, :].bitcast(F32)
+                for u in range(2):
+                    nc.tensor.transpose(quarters(bank)[:, 2 * e + u, :], words[:, u::2], ident[:])
+            qr_woven[SECOND, v] = held([P, 2 * P * PACK], BF16, f"second_qr_woven{v}")[:]
+            nc.scalar.copy(qr_woven[SECOND, v].bitcast(F32).rearrange("s (e p u) -> s e p u", e=2, u=2),
+                           bank[:].rearrange("s (e u p) -> s e p u", e=2, u=2))
+
         def quantise_queries_along_r(h, v):
-            quantise(qr_woven[h, v], E4M3, qr_codes[h][v][:], qr_scales[h][v][:])
+            quantise(qr_woven[h, v], E4M3, qr_codes[h][v], qr_scales[h][v][:])
 
         for u in range(2):
             weave_queries(FIRST, u)
@@ -158,10 +169,10 @@ def tile_attend_ggqa_sm_k_kernel(tc, q1, q2, kT, dp1, dp2, us, ts, w1, w2, offs,
             for a in range(2):
                 nc.vector.tensor_copy(k_woven[a][:, :, j], k_planes[j][:].indirect(half_lists[a]))
             if j == 1:
-                quantise_queries_along_r(FIRST, 0)
+                for v in range(2):
+                    quantise_queries_along_r(FIRST, v)
         for a in range(2):
             quantise(k_woven[a][:].rearrange("p i j -> p (i j)"), E4M3, k_codes[a][:], k_scales[a][:])
-        quantise_queries_along_r(FIRST, 1)
 
         neg_us = held([P, PACK], F32, "neg_us")
         nc.gpsimd.tensor_scalar(neg_us[:], us_sb[:], -1.0, 0.0, ALU.mult, ALU.add)
@@ -170,18 +181,21 @@ def tile_attend_ggqa_sm_k_kernel(tc, q1, q2, kT, dp1, dp2, us, ts, w1, w2, offs,
             nc.gpsimd.tensor_tensor(numerators[:, 0, PACK * h : PACK * (h + 1)], w_sb[h][:], us_sb[:], ALU.mult)
         nc.gpsimd.memset(numerators[:, 1, :], -1.0)
 
-        products = [held([P, PACK, SLOTS], F32, "products0"), held([P, PACK, SLOTS], F32, "products1", "q_raw0")]
         first_gradient = [held([P, HALF, PACK], BF16, f"first_gradient{a}")[:] for a in range(2)]
-        g_woven = [first_gradient, [first_gradient[0], held([P, HALF, PACK], BF16, "second_gradient")[:]]]
+        g_woven = [first_gradient, [held([P, HALF, PACK], BF16, f"second_gradient{a}")[:] for a in range(2)]]
         neg_z = [held([P, SLOTS], F32, f"neg_z{t}")[:] for t in range(2)] + [q_raw[SECOND][:, t, :] for t in range(2, PACK)]
         scaled = held([P, PACK, R], F32, "scaled")
-        means = [held([P, SLOTS], F32, f"mean{t}", tag) for t, tag in enumerate(("qd_codes1", "k_codes1", None, None))]
+        second_products = held([P, PACK, SLOTS], F32, "second_products", "q_raw0")
+        early_products = held([P, 2, SLOTS], F32, "early_products")
+        products = [early_products[:, 0, :], early_products[:, 1, :], scaled[:, 0, :], scaled[:, 1, :]]
+        products = products + [second_products[:, t, :] for t in range(PACK)]
+        means = held([P, 2, PACK, HALF], F32, "means")
         neg_max = [held([P, 1], F32, f"neg_max{n}") for n in range(TILES)]
         totals = held([P, TILES], F32, "totals")
-        factors = held([P, 2, TILES], F32, "factors")
+        factors = {}
         row_sums = held([P, TILES], F32, "row_sums")
         shifts = held([P, TILES], F32, "shifts")
-        exps, turned = {}, {}
+        exps, turned, inverses = {}, {}, {}
 
         def half(a):
             return slice(a * HALF, (a + 1) * HALF)
@@ -189,9 +203,8 @@ def tile_attend_ggqa_sm_k_kernel(tc, q1, q2, kT, dp1, dp2, us, ts, w1, w2, offs,
         def as_floats(view):
             return view.rearrange("p a b c -> p (a b c)").bitcast(F32)
 
-        centred = held([P, PACK, HALF], F32, "centred")
 
-        second_means = held([P, PACK, HALF], F32, "second_means")
+        second_means = {}
 
         def first_head_scores(t, bank):
             for a in range(2):
@@ -222,42 +235,53 @@ def tile_attend_ggqa_sm_k_kernel(tc, q1, q2, kT, dp1, dp2, us, ts, w1, w2, offs,
             nc.scalar.activation(target, neg_z[n % PACK], ACT.Exp, bias=neg_max[n][:], scale=-1.0,
                                  accum_out=totals[:, n : n + 1])
 
-        def make_factors(first, last, inverses):
-            nc.vector.reciprocal(inverses, totals[:, first:last])
-            nc.vector.tensor_tensor(factors[:, :, first:last], numerators[:, :, first:last],
-                                    inverses.unsqueeze(1).to_broadcast([P, 2, last - first]), ALU.mult)
+        def make_inverses(first, target):
+            inverses[first] = target
+            nc.vector.reciprocal(target, totals[:, first : first + 2])
+
+        def make_factors(first, target):
+            factors[first] = target.rearrange("p (k e) -> p k e", k=2)
+            nc.vector.tensor_tensor(factors[first], numerators[:, :, first : first + 2],
+                                    inverses[first].unsqueeze(1).to_broadcast([P, 2, 2]), ALU.mult)
 
         def make_products(n):
             h, t = divmod(n, PACK)
-            nc.vector.scalar_tensor_tensor(products[h][:, t, :], exps[n], factors[:, 0, n : n + 1], dp_sb[h][:, t, :],
-                                           ALU.mult, ALU.mult, accum_out=row_sums[:, n : n + 1])
+            nc.vector.scalar_tensor_tensor(products[n], exps[n], factors[n - n % 2][:, 0, n % 2 : n % 2 + 1],
+                                           dp_sb[h][:, t, :], ALU.mult, ALU.mult, accum_out=row_sums[:, n : n + 1])
 
-        def make_shifts(first, last):
-            nc.vector.tensor_tensor(shifts[:, first:last], row_sums[:, first:last], factors[:, 1, first:last], ALU.mult)
+        def make_shifts(first):
+            nc.vector.tensor_tensor(shifts[:, first : first + 2], row_sums[:, first : first + 2], factors[first][:, 1, :],
+                                    ALU.mult)
 
-        def mean_term(t):
-            nc.scalar.activation(means[t][:], exps[t], ACT.Copy, scale=shifts[:, t : t + 1])
+        def mean_term(t, a):
+            nc.scalar.activation(means[:, a, t, :], exps[t][:, half(a)], ACT.Copy, scale=shifts[:, t : t + 1])
 
         def centre(t, a):
             n = PACK + t
             nc.vector.scalar_tensor_tensor(centred[:, t, :], exps[n][:, half(a)], shifts[:, n : n + 1],
-                                           products[SECOND][:, t, half(a)], ALU.mult, ALU.add)
+                                           products[n][:, half(a)], ALU.mult, ALU.add)
 
-        def turn_term(term, t, blocks, opens):
-            for b in blocks:
-                nc.tensor.matmul(quarters(turn_banks[b])[:, t, :], term[:, b * P : (b + 1) * P], ident[:],
-                                 start=opens and t == 0, stop=not opens and t == PACK - 1, is_transpose=True)
+        def turn_first(a, opens):
+            for t in range(PACK):
+                term = products[t][:, half(a)] if opens else means[:, a, t, :]
+                for c in range(2):
+                    nc.tensor.matmul(quarters(turn_banks[2 * a + c])[:, t, :], term[:, c * P : (c + 1) * P], ident[:],
+                                     start=opens and t == 0, stop=not opens and t == PACK - 1, is_transpose=True)
 
         def second_mean_term(t):
-            nc.scalar.activation(second_means[:, t, :], exps[PACK + t][:, half(1)], ACT.Copy,
+            second_means[t] = as_floats(turned[FIRST, t][:])
+            nc.scalar.activation(second_means[t], exps[PACK + t][:, half(1)], ACT.Copy,
                                  scale=shifts[:, PACK + t : PACK + t + 1])
 
         def turn_centred(c, bank):
             block = slice(c * P, (c + 1) * P)
             for t in range(PACK):
-                for opens, term in ((True, products[SECOND][:, t, half(1)]), (False, second_means[:, t, :])):
-                    nc.tensor.matmul(quarters(bank)[:, t, :], term[:, block], ident[:], start=opens, stop=not opens,
-                                     is_transpose=True)
+                if t < 2:
+                    for opens, term in ((True, products[PACK + t][:, half(1)]), (False, second_means[t])):
+                        nc.tensor.matmul(quarters(bank)[:, t, :], term[:, block], ident[:], start=opens, stop=not opens,
+                                         is_transpose=True)
+                else:
+                    nc.tensor.transpose(quarters(bank)[:, t, :], centred[:, t, block], ident[:])
 
         def round_turned(h, b, bank):
             turned[h, b] = held([P, 2, P, 2], BF16, f"g_turned{h}_{b}")
@@ -295,69 +319,76 @@ def tile_attend_ggqa_sm_k_kernel(tc, q1, q2, kT, dp1, dp2, us, ts, w1, w2, offs,
             first_head_scores(t, banks[t])
         for t in range(2):
             first_head_maximum(t)
+        rounded = held([P, PACK, R], BF16, "rounded", "k_woven1")
+        for v in range(2):
+            nc.gpsimd.tensor_scalar(rounded[:, 2 * v : 2 * v + 2, :], q_raw[SECOND][:, 2 * v : 2 * v + 2, :], 1.0, 0.0,
+                                    ALU.mult, ALU.add)
         for u in range(2):
             weave_queries(SECOND, u)
             quantise_queries_along_d(SECOND, u)
         for t in range(2, PACK):
             first_head_scores(t, banks[t])
+
+        def small(columns, name):
+            return held([P, columns], F32, name)[:]
+
         for t in range(2):
             exponentials(t, q_raw[SECOND][:, t, :])
-        make_factors(0, 2, held([P, 2], F32, "inverses0")[:])
-        for t in range(2, PACK):
-            first_head_maximum(t)
-            exponentials(t, held([P, SLOTS], F32, f"first_e{t}")[:])
-        turn_queries(SECOND, 0, banks[7])
-        qr_woven[SECOND, 0] = held([P, 2 * P * PACK], BF16, "second_qr_woven")[:]
-        weave_turned_queries(SECOND, 0, banks[7])
+        make_inverses(0, small(2, "inverses0"))
+        first_head_maximum(2)
+        make_factors(0, small(4, "factors0"))
+        first_head_maximum(3)
         for b, bank in enumerate((banks[4], banks[5], banks[0], banks[1])):
             second_head_scores(b, bank)
+        for t, tag in ((2, "qd_codes1"), (3, "k_codes1")):
+            exponentials(t, held([P, SLOTS], F32, f"first_e{t}", tag)[:])
         for n in range(2):
             make_products(n)
-        make_factors(2, PACK, held([P, 2], F32, "inverses2")[:])
-        for n in range(2, PACK):
-            make_products(n)
-        quantise_queries_along_r(SECOND, 0)
-        for first in (0, 2):
-            make_shifts(first, first + 2)
+        make_shifts(0)
         for t, bank in enumerate((banks[2], banks[3], banks[4], banks[5])):
             second_head_rows(t, bank)
             exponentials(PACK + t, held([P, SLOTS], F32, f"e{t}")[:])
-        for t in range(PACK):
-            mean_term(t)
-        make_factors(4, 6, neg_us[:, 2:4])
+            if t == 1:
+                make_inverses(2, scaled[:, 3, P : P + 2])
+            if t == 2:
+                make_factors(2, scaled[:, 3, 2 * P : 2 * P + 4])
+        for v in range(2):
+            turn_rounded_queries(rounded, v, banks[6 + v])
+        make_products(2)
+        make_inverses(4, scaled[:, 3, 3 * P : 3 * P + 2])
+        make_products(3)
+        make_factors(4, small(4, "factors4"))
+        make_inverses(6, small(2, "inverses6"))
         make_products(4)
-        make_factors(6, TILES, held([P, 2], F32, "last_inverses")[:])
+        make_shifts(2)
+        make_factors(6, small(4, "factors6"))
         make_products(5)
-        make_shifts(4, 6)
-        for n in range(6, TILES):
-            make_products(n)
-        turn_banks = (banks[6], banks[7], banks[0], banks[1])
-
-        def turn_first(blocks, opens):
+        quantise_queries_along_r(SECOND, 0)
+        make_products(6)
+        make_shifts(4)
+        make_products(7)
+        turn_banks = (banks[2], banks[3], banks[6], banks[7])
+        for a in range(2):
             for t in range(PACK):
-                turn_term(products[FIRST][:, t, :] if opens else means[t][:], t, blocks, opens)
-
-        turn_first(range(2), True)
-        turn_first(range(2), False)
+                mean_term(t, a)
+        turn_first(0, True)
+        turn_first(0, False)
         for b in range(2):
             round_turned(FIRST, b, turn_banks[b])
-        turn_first(range(2, PACK), True)
-        return_gradient(FIRST, 0, banks[2])
-        turn_first(range(2, PACK), False)
+        turn_first(1, True)
+        return_gradient(FIRST, 0, banks[4])
+        turn_first(1, False)
         for b in range(2, PACK):
             round_turned(FIRST, b, turn_banks[b])
         centre(0, 0)
-        make_shifts(6, TILES)
+        make_shifts(6)
         for t in range(1, PACK):
             centre(t, 0)
-        quantise_gradient(FIRST, 0)
-        early_banks = (banks[4], banks[5], banks[6])
-        key_gradient_pass(early_banks[0], 0, FIRST, True, False)
-        return_gradient(FIRST, 1, banks[3])
-        qr_woven[SECOND, 1] = held([P, 2 * P * PACK], BF16, "late_qr_woven")[:]
-        turn_queries(SECOND, 1, banks[7])
-        weave_turned_queries(SECOND, 1, banks[7])
         weave_centred()
+        quantise_gradient(FIRST, 0)
+        early_banks = (banks[7], banks[1], banks[2])
+        return_gradient(FIRST, 1, banks[5])
+        key_gradient_pass(early_banks[0], 0, FIRST, True, False)
         quantise_gradient(SECOND, 0)
         key_gradient_pass(early_banks[0], 0, SECOND, False, True)
 
@@ -367,22 +398,23 @@ def tile_attend_ggqa_sm_k_kernel(tc, q1, q2, kT, dp1, dp2, us, ts, w1, w2, offs,
 
         quantise_gradient(FIRST, 1)
         quantise_queries_along_r(SECOND, 1)
-        for t in range(PACK):
+        for t in range(2):
             second_mean_term(t)
+            centre(2 + t, 1)
         early_plane(0, held([P, HALF], F32, "early0")[:])
+        turn_centred(0, banks[3])
+        round_turned(SECOND, 2, banks[3])
         for h in range(HEADS):
             key_gradient_pass(early_banks[1], 1, h, h == FIRST, h == SECOND)
-        for c in range(2):
-            turn_centred(c, banks[c])
+        turn_centred(1, banks[4])
         early_plane(1, held([P, HALF], F32, "early1")[:])
-        for c in range(2):
-            round_turned(SECOND, 2 + c, banks[c])
+        round_turned(SECOND, 3, banks[4])
         for h in range(HEADS):
             key_gradient_pass(early_banks[2], 2, h, h == FIRST, h == SECOND)
-        return_gradient(SECOND, 1, banks[2])
+        return_gradient(SECOND, 1, banks[6])
         quantise_gradient(SECOND, 1)
         early_plane(2, as_floats(turned[SECOND, PACK - 1][:]))
-        for j, bank in enumerate((banks[3], banks[7], banks[0], banks[1])):
+        for j, bank in enumerate((banks[0], banks[5], banks[3], banks[4])):
             adds = 0 < j < EARLY
             columns, entries = (half(1), half_lists[1]) if j < EARLY else (slice(0, SLOTS), offsets[:])
             if not adds:

@@ -51,9 +51,9 @@ def tile_attend_ggqa_sm_k_kernel(tc, q1, q2, kT, dp1, dp2, us, ts, w1, w2, offs,
 
         offsets = keep.tile([P, SLOTS // 16], U16, name="offsets")
 
-        q_raw = [held([P, PACK, R], F32, f"q_raw{h}") for h in range(HEADS)]
-        dp_sb = [held([P, PACK, SLOTS], F32, f"dp_sb{h}") for h in range(HEADS)]
-        k_planes = [held([P, TOKENS], F32, f"k_plane{j}") for j in range(PACK)]
+        q_raw = [held([P, PACK, R], F32, "q_raw0")]
+        dp_sb = []
+        k_planes = [held([P, TOKENS], F32, f"k_plane{j}") for j in range(PACK - 1)]
         us_sb = held([P, PACK], F32, "us_sb")
         w_sb = [held([P, PACK], F32, f"w_sb{h}") for h in range(HEADS)]
         ts_window = held([P, TOKENS], F32, "ts_window")
@@ -66,14 +66,11 @@ def tile_attend_ggqa_sm_k_kernel(tc, q1, q2, kT, dp1, dp2, us, ts, w1, w2, offs,
         nc.sync.dma_start(q_raw[FIRST][:], q1.rearrange("(p j) r -> p j r", j=PACK))
         nc.sync.dma_start(offsets[:], offs)
         k_hbm = kT.rearrange("(p j) t -> j p t", j=PACK)
-        for j in range(PACK):
+        for j in range(PACK - 1):
             nc.sync.dma_start(k_planes[j][:], k_hbm[j])
         nc.scalar.dma_start(us_sb[:], us.rearrange("(s t) o -> s (t o)", t=PACK))
         for h, w in enumerate((w1, w2)):
             nc.scalar.dma_start(w_sb[h][:], w.rearrange("(s t) o -> s (t o)", t=PACK))
-        nc.sync.dma_start(q_raw[SECOND][:], q2.rearrange("(p j) r -> p j r", j=PACK))
-        for h, dp in enumerate((dp1, dp2)):
-            nc.sync.dma_start(dp_sb[h][:], dp.rearrange("(s t) i -> s t i", t=PACK))
 
         g_codes = [held([P, SLOTS], U32, f"g_codes{h}") for h in range(HEADS)]
         g_scales = [held([P, SLOTS], U8, f"g_scales{h}") for h in range(HEADS)]
@@ -111,10 +108,10 @@ def tile_attend_ggqa_sm_k_kernel(tc, q1, q2, kT, dp1, dp2, us, ts, w1, w2, offs,
         first_woven = held([P, 2, 2, P, PACK], BF16, "first_woven", "ts_runs")
         q_woven = [[first_woven[:, u] for u in range(2)],
                    [held([P, 2, P, PACK], BF16, f"second_woven{u}")[:] for u in range(2)]]
-        qd_codes = [held([P, R], U32, f"qd_codes{h}", "ts_window" if h == FIRST else None) for h in range(HEADS)]
+        qd_codes = [held([P, R], U32, f"qd_codes{h}") for h in range(HEADS)]
         qd_scales = [held([P, R], U8, f"qd_scales{h}") for h in range(HEADS)]
         qr_woven = {(FIRST, v): held([P, 2 * P * PACK], BF16, f"qr_woven{v}")[:] for v in range(2)}
-        qr_first = held([P, 2, 2 * P], U32, "qr_codes0", "k_plane1")
+        qr_first = held([P, 2, 2 * P], U32, "qr_codes0")
         qr_codes = [[qr_first[:, v, :] for v in range(2)],
                     [held([P, 2 * P], U32, f"qr_codes1_{v}", "ts_slots" if v else None)[:] for v in range(2)]]
         qr_scales = [[held([P, 2 * P], U8, f"qr_scales{h}_{v}") for v in range(2)] for h in range(HEADS)]
@@ -161,18 +158,27 @@ def tile_attend_ggqa_sm_k_kernel(tc, q1, q2, kT, dp1, dp2, us, ts, w1, w2, offs,
         ts_cols = held([P, PACK], F32, "ts_cols")
         nc.scalar.copy(ts_cols[:], ts_turned[:, :, 0])
 
-        k_woven = [held([P, HALF, PACK], BF16, f"k_woven{a}") for a in range(2)]
+        both_woven = held([P, 2, HALF, PACK], BF16, "k_woven", "ts_window")
+        k_woven = [both_woven[:, a] for a in range(2)]
         k_codes = [held([P, HALF], U32, f"k_codes{a}") for a in range(2)]
         k_scales = [held([P, HALF], U8, f"k_scales{a}") for a in range(2)]
         half_lists = [offsets[:, a * HALF // 16 : (a + 1) * HALF // 16] for a in range(2)]
         for j in range(PACK):
             for a in range(2):
                 nc.vector.tensor_copy(k_woven[a][:, :, j], k_planes[j][:].indirect(half_lists[a]))
+            if j == 0:
+                k_planes.append(held([P, TOKENS], F32, "k_plane3", "k_plane0"))
+                nc.sync.dma_start(k_planes[-1][:], k_hbm[PACK - 1])
             if j == 1:
+                q_raw.append(held([P, PACK, R], F32, "q_raw1", "k_plane1"))
+                nc.sync.dma_start(q_raw[SECOND][:], q2.rearrange("(p j) r -> p j r", j=PACK))
                 for v in range(2):
                     quantise_queries_along_r(FIRST, v)
+            if j >= 2:
+                dp_sb.append(held([P, PACK, SLOTS], F32, f"dp_sb{j - 2}", f"k_plane{j % 3}"))
+                nc.sync.dma_start(dp_sb[-1][:], (dp1, dp2)[j - 2].rearrange("(s t) i -> s t i", t=PACK))
         for a in range(2):
-            quantise(k_woven[a][:].rearrange("p i j -> p (i j)"), E4M3, k_codes[a][:], k_scales[a][:])
+            quantise(k_woven[a].rearrange("p i j -> p (i j)"), E4M3, k_codes[a][:], k_scales[a][:])
 
         neg_us = held([P, PACK], F32, "neg_us")
         nc.gpsimd.tensor_scalar(neg_us[:], us_sb[:], -1.0, 0.0, ALU.mult, ALU.add)
@@ -319,7 +325,7 @@ def tile_attend_ggqa_sm_k_kernel(tc, q1, q2, kT, dp1, dp2, us, ts, w1, w2, offs,
             first_head_scores(t, banks[t])
         for t in range(2):
             first_head_maximum(t)
-        rounded = held([P, PACK, R], BF16, "rounded", "k_woven1")
+        rounded = held([P, PACK, R], BF16, "rounded", "ts_window")
         for v in range(2):
             nc.gpsimd.tensor_scalar(rounded[:, 2 * v : 2 * v + 2, :], q_raw[SECOND][:, 2 * v : 2 * v + 2, :], 1.0, 0.0,
                                     ALU.mult, ALU.add)

@@ -85,9 +85,8 @@ def tile_attend_ggqa_sm_k_kernel(tc, q1, q2, kT, dp1, dp2, us, ts, w1, w2, offs,
             for columns in (slice(0, TOKENS // 2), slice(TOKENS // 2, TOKENS)):
                 engine.memset(windows[j][:, columns].bitcast(I32), 0)
 
-        zero_window(PACK - 1, nc.vector)
-        for j in range(PACK - 1):
-            zero_window(j, nc.gpsimd)
+        for j in range(PACK):
+            zero_window(j, nc.gpsimd if j < 2 else nc.vector)
 
         for g in range(RUN // PACK):
             bank = quarters(spread_banks[g])
@@ -158,14 +157,20 @@ def tile_attend_ggqa_sm_k_kernel(tc, q1, q2, kT, dp1, dp2, us, ts, w1, w2, offs,
         ts_cols = held([P, PACK], F32, "ts_cols")
         nc.scalar.copy(ts_cols[:], ts_turned[:, :, 0])
 
-        both_woven = held([P, 2, HALF, PACK], BF16, "k_woven", "ts_window")
+        k_pair = held([P, 2, SLOTS], BF16, "k_pair", "ts_window")
+        both_woven = held([P, 2, HALF, PACK], BF16, "k_woven", "ts_runs")
         k_woven = [both_woven[:, a] for a in range(2)]
-        k_codes = [held([P, HALF], U32, f"k_codes{a}") for a in range(2)]
-        k_scales = [held([P, HALF], U8, f"k_scales{a}") for a in range(2)]
+        all_k_codes = held([P, SLOTS], U32, "k_codes")
+        all_k_scales = held([P, SLOTS], U8, "k_scales")
+        k_codes = [all_k_codes[:, a * HALF : (a + 1) * HALF] for a in range(2)]
+        k_scales = [all_k_scales[:, a * HALF : (a + 1) * HALF] for a in range(2)]
         half_lists = [offsets[:, a * HALF // 16 : (a + 1) * HALF // 16] for a in range(2)]
         for j in range(PACK):
-            for a in range(2):
-                nc.vector.tensor_copy(k_woven[a][:, :, j], k_planes[j][:].indirect(half_lists[a]))
+            if j < 2:
+                nc.vector.tensor_copy(k_pair[:, j, :], k_planes[j][:].indirect(offsets[:]))
+            else:
+                for a in range(2):
+                    nc.vector.tensor_copy(k_woven[a][:, :, j], k_planes[j][:].indirect(half_lists[a]))
             if j == 0:
                 k_planes.append(held([P, TOKENS], F32, "k_plane3", "k_plane0"))
                 nc.sync.dma_start(k_planes[-1][:], k_hbm[PACK - 1])
@@ -174,11 +179,13 @@ def tile_attend_ggqa_sm_k_kernel(tc, q1, q2, kT, dp1, dp2, us, ts, w1, w2, offs,
                 nc.sync.dma_start(q_raw[SECOND][:], q2.rearrange("(p j) r -> p j r", j=PACK))
                 for v in range(2):
                     quantise_queries_along_r(FIRST, v)
+                for a in range(2):
+                    nc.scalar.copy(k_woven[a][:, :, 0:2], k_pair[:, :, a * HALF : (a + 1) * HALF].rearrange("p j i -> p i j"))
             if j >= 2:
                 dp_sb.append(held([P, PACK, SLOTS], F32, f"dp_sb{j - 2}", f"k_plane{j % 3}"))
                 nc.sync.dma_start(dp_sb[-1][:], (dp1, dp2)[j - 2].rearrange("(s t) i -> s t i", t=PACK))
         for a in range(2):
-            quantise(k_woven[a].rearrange("p i j -> p (i j)"), E4M3, k_codes[a][:], k_scales[a][:])
+            quantise(k_woven[a].rearrange("p i j -> p (i j)"), E4M3, k_codes[a], k_scales[a])
 
         neg_us = held([P, PACK], F32, "neg_us")
         nc.gpsimd.tensor_scalar(neg_us[:], us_sb[:], -1.0, 0.0, ALU.mult, ALU.add)
@@ -213,10 +220,11 @@ def tile_attend_ggqa_sm_k_kernel(tc, q1, q2, kT, dp1, dp2, us, ts, w1, w2, offs,
         second_means = {}
 
         def first_head_scores(t, bank):
-            for a in range(2):
-                nc.tensor.matmul_mx(out=bank[:, half(a)], lhsT=qd_codes[FIRST][:, t * P : (t + 1) * P].bitcast(E4M3),
+            for columns in (half(0), half(1)) if t == 0 else (slice(0, SLOTS),):
+                nc.tensor.matmul_mx(out=bank[:, columns], lhsT=qd_codes[FIRST][:, t * P : (t + 1) * P].bitcast(E4M3),
                                     lhsT_scale=qd_scales[FIRST][:, t * P : (t + 1) * P],
-                                    rhs=k_codes[a][:].bitcast(E4M3), rhs_scale=k_scales[a][:], start=True, stop=True)
+                                    rhs=all_k_codes[:, columns].bitcast(E4M3), rhs_scale=all_k_scales[:, columns],
+                                    start=True, stop=True)
             nc.vector.scalar_tensor_tensor(neg_z[t], bank[:], neg_us[:, t : t + 1], ts_slots[:], ALU.mult, ALU.mult)
 
         def first_head_maximum(t):
@@ -325,7 +333,7 @@ def tile_attend_ggqa_sm_k_kernel(tc, q1, q2, kT, dp1, dp2, us, ts, w1, w2, offs,
             first_head_scores(t, banks[t])
         for t in range(2):
             first_head_maximum(t)
-        rounded = held([P, PACK, R], BF16, "rounded", "ts_window")
+        rounded = held([P, PACK, R], BF16, "rounded", "ts_runs")
         for v in range(2):
             nc.gpsimd.tensor_scalar(rounded[:, 2 * v : 2 * v + 2, :], q_raw[SECOND][:, 2 * v : 2 * v + 2, :], 1.0, 0.0,
                                     ALU.mult, ALU.add)
@@ -346,7 +354,7 @@ def tile_attend_ggqa_sm_k_kernel(tc, q1, q2, kT, dp1, dp2, us, ts, w1, w2, offs,
         first_head_maximum(3)
         for b, bank in enumerate((banks[4], banks[5], banks[0], banks[1])):
             second_head_scores(b, bank)
-        for t, tag in ((2, "qd_codes1"), (3, "k_codes1")):
+        for t, tag in ((2, "qd_codes1"), (3, "k_codes")):
             exponentials(t, held([P, SLOTS], F32, f"first_e{t}", tag)[:])
         for n in range(2):
             make_products(n)

@@ -34,7 +34,6 @@ def tile_attend_ggqa_sm_k_kernel(tc, q1, q2, kT, dp1, dp2, us, ts, w1, w2, offs,
     nc = tc.nc
     with ExitStack() as ctx:
         keep = ctx.enter_context(tc.tile_pool(name="keep", bufs=1))
-        ring = ctx.enter_context(tc.tile_pool(name="ring", bufs=3))
         psum = ctx.enter_context(tc.psum_pool(name="psum", bufs=1))
 
         def held(shape, dtype, name, tag=None):
@@ -134,7 +133,7 @@ def tile_attend_ggqa_sm_k_kernel(tc, q1, q2, kT, dp1, dp2, us, ts, w1, w2, offs,
 
         def turn_rounded_queries(rounded, v, bank):
             for e in range(2):
-                words = rounded[:, 2 * v + e, :].bitcast(F32)
+                words = rounded[2 * v + e].bitcast(F32)
                 for u in range(2):
                     nc.tensor.transpose(quarters(bank)[:, 2 * e + u, :], words[:, u::2], ident[:])
             qr_woven[SECOND, v] = held([P, 2 * P * PACK], BF16, f"second_qr_woven{v}")[:]
@@ -196,7 +195,7 @@ def tile_attend_ggqa_sm_k_kernel(tc, q1, q2, kT, dp1, dp2, us, ts, w1, w2, offs,
 
         first_gradient = [held([P, HALF, PACK], BF16, f"first_gradient{a}")[:] for a in range(2)]
         g_woven = [first_gradient, [held([P, HALF, PACK], BF16, f"second_gradient{a}")[:] for a in range(2)]]
-        neg_z = [held([P, SLOTS], F32, f"neg_z{t}")[:] for t in range(2)] + [q_raw[SECOND][:, t, :] for t in range(2, PACK)]
+        neg_z = [held([P, SLOTS], F32, f"neg_z{t}")[:] for t in range(2)] + [q_raw[SECOND][:, t, :] for t in range(2)]
         scaled = held([P, PACK, R], F32, "scaled")
         second_products = held([P, PACK, SLOTS], F32, "second_products", "q_raw0")
         early_products = held([P, 2, SLOTS], F32, "early_products")
@@ -204,7 +203,7 @@ def tile_attend_ggqa_sm_k_kernel(tc, q1, q2, kT, dp1, dp2, us, ts, w1, w2, offs,
         products = products + [second_products[:, t, :] for t in range(PACK)]
         means = held([P, 2, PACK, HALF], F32, "means")
         neg_max = [held([P, 1], F32, f"neg_max{n}") for n in range(TILES)]
-        totals = held([P, TILES], F32, "totals")
+        totals = q_raw[SECOND][:, 2, :TILES]
         factors = {}
         row_sums = held([P, TILES], F32, "row_sums")
         shifts = held([P, TILES], F32, "shifts")
@@ -333,13 +332,18 @@ def tile_attend_ggqa_sm_k_kernel(tc, q1, q2, kT, dp1, dp2, us, ts, w1, w2, offs,
             first_head_scores(t, banks[t])
         for t in range(2):
             first_head_maximum(t)
-        rounded = held([P, PACK, R], BF16, "rounded", "ts_runs")
-        for v in range(2):
-            nc.gpsimd.tensor_scalar(rounded[:, 2 * v : 2 * v + 2, :], q_raw[SECOND][:, 2 * v : 2 * v + 2, :], 1.0, 0.0,
-                                    ALU.mult, ALU.add)
+        rounded = []
+
+        def round_second_queries(start, stop, tag):
+            target = held([P, stop - start, R], BF16, f"rounded{start}", tag)
+            rounded.extend(target[:, j, :] for j in range(stop - start))
+            nc.gpsimd.tensor_scalar(target[:], q_raw[SECOND][:, start:stop, :], 1.0, 0.0, ALU.mult, ALU.add)
+
+        round_second_queries(0, PACK - 1, "ts_runs")
         for u in range(2):
             weave_queries(SECOND, u)
             quantise_queries_along_d(SECOND, u)
+        round_second_queries(PACK - 1, PACK, "second_woven1")
         for t in range(2, PACK):
             first_head_scores(t, banks[t])
 
@@ -347,7 +351,7 @@ def tile_attend_ggqa_sm_k_kernel(tc, q1, q2, kT, dp1, dp2, us, ts, w1, w2, offs,
             return held([P, columns], F32, name)[:]
 
         for t in range(2):
-            exponentials(t, q_raw[SECOND][:, t, :])
+            exponentials(t, held([P, SLOTS], F32, f"first_e{t}")[:])
         make_inverses(0, small(2, "inverses0"))
         first_head_maximum(2)
         make_factors(0, small(4, "factors0"))

@@ -99,7 +99,8 @@ def tile_attend_ggqa_sm_k_kernel(tc, q1, q2, kT, dp1, dp2, us, ts, w1, w2, offs,
         ts_slots = held([P, SLOTS], F32, "ts_slots")
         nc.vector.tensor_copy(ts_slots[:], ts_window[:].indirect(offsets[:]))
 
-        centred = held([P, PACK, HALF], F32, "centred")
+        first_centred = held([P, PACK, HALF], F32, "centred")
+        centred = [[first_centred[:, t, :] for t in range(PACK)]]
         def quantise(source, fmt, codes, scales):
             nc.vector.quantize_mx(out=codes.bitcast(fmt), scales=scales, in_=source)
 
@@ -111,7 +112,7 @@ def tile_attend_ggqa_sm_k_kernel(tc, q1, q2, kT, dp1, dp2, us, ts, w1, w2, offs,
         qr_woven = {(FIRST, v): held([P, 2 * P * PACK], BF16, f"qr_woven{v}")[:] for v in range(2)}
         qr_first = held([P, 2, 2 * P], U32, "qr_codes0")
         qr_codes = [[qr_first[:, v, :] for v in range(2)],
-                    [held([P, 2 * P], U32, f"qr_codes1_{v}", "ts_slots" if v else None)[:] for v in range(2)]]
+                    [held([P, 2 * P], U32, f"qr_codes1_{v}")[:] for v in range(2)]]
         qr_scales = [[held([P, 2 * P], U8, f"qr_scales{h}_{v}") for v in range(2)] for h in range(HEADS)]
 
         def weave_queries(h, u):
@@ -178,8 +179,8 @@ def tile_attend_ggqa_sm_k_kernel(tc, q1, q2, kT, dp1, dp2, us, ts, w1, w2, offs,
                 nc.sync.dma_start(q_raw[SECOND][:], q2.rearrange("(p j) r -> p j r", j=PACK))
                 for v in range(2):
                     quantise_queries_along_r(FIRST, v)
-                for a in range(2):
-                    nc.scalar.copy(k_woven[a][:, :, 0:2], k_pair[:, :, a * HALF : (a + 1) * HALF].rearrange("p j i -> p i j"))
+                for place in range(2):
+                    nc.scalar.copy(both_woven[:, :, :, place].rearrange("p a i -> p (a i)"), k_pair[:, place, :])
             if j >= 2:
                 dp_sb.append(held([P, PACK, SLOTS], F32, f"dp_sb{j - 2}", f"k_plane{j % 3}"))
                 nc.sync.dma_start(dp_sb[-1][:], (dp1, dp2)[j - 2].rearrange("(s t) i -> s t i", t=PACK))
@@ -271,7 +272,7 @@ def tile_attend_ggqa_sm_k_kernel(tc, q1, q2, kT, dp1, dp2, us, ts, w1, w2, offs,
 
         def centre(t, a):
             n = PACK + t
-            nc.vector.scalar_tensor_tensor(centred[:, t, :], exps[n][:, half(a)], shifts[:, n : n + 1],
+            nc.vector.scalar_tensor_tensor(centred[a][t], exps[n][:, half(a)], shifts[:, n : n + 1],
                                            products[n][:, half(a)], ALU.mult, ALU.add)
 
         def turn_first(a, opens):
@@ -282,19 +283,19 @@ def tile_attend_ggqa_sm_k_kernel(tc, q1, q2, kT, dp1, dp2, us, ts, w1, w2, offs,
                                      start=opens and t == 0, stop=not opens and t == PACK - 1, is_transpose=True)
 
         def second_mean_term(t):
-            second_means[t] = as_floats(turned[FIRST, t][:])
+            second_means[t] = means[:, 0, PACK - 1 - t, :]
             nc.scalar.activation(second_means[t], exps[PACK + t][:, half(1)], ACT.Copy,
                                  scale=shifts[:, PACK + t : PACK + t + 1])
 
-        def turn_centred(c, bank):
+        def turn_centred(c, bank, tiles):
             block = slice(c * P, (c + 1) * P)
-            for t in range(PACK):
+            for t in tiles:
                 if t < 2:
                     for opens, term in ((True, products[PACK + t][:, half(1)]), (False, second_means[t])):
                         nc.tensor.matmul(quarters(bank)[:, t, :], term[:, block], ident[:], start=opens, stop=not opens,
                                          is_transpose=True)
                 else:
-                    nc.tensor.transpose(quarters(bank)[:, t, :], centred[:, t, block], ident[:])
+                    nc.tensor.transpose(quarters(bank)[:, t, :], centred[1][t][:, block], ident[:])
 
         def round_turned(h, b, bank):
             turned[h, b] = held([P, 2, P, 2], BF16, f"g_turned{h}_{b}")
@@ -312,7 +313,7 @@ def tile_attend_ggqa_sm_k_kernel(tc, q1, q2, kT, dp1, dp2, us, ts, w1, w2, offs,
         def weave_centred():
             ts_lines = ts_slots[:, half(0)].rearrange("p (c i) -> p c i", i=LINE).unsqueeze(2)
             nc.vector.tensor_tensor(g_woven[SECOND][0].rearrange("p (c i) t -> p c t i", i=LINE),
-                                    centred[:].rearrange("p t (c i) -> p c t i", i=LINE),
+                                    first_centred[:].rearrange("p t (c i) -> p c t i", i=LINE),
                                     ts_lines.to_broadcast([P, HALF // LINE, PACK, LINE]), ALU.mult)
 
         def quantise_gradient(h, a):
@@ -394,45 +395,50 @@ def tile_attend_ggqa_sm_k_kernel(tc, q1, q2, kT, dp1, dp2, us, ts, w1, w2, offs,
         for b in range(2):
             round_turned(FIRST, b, turn_banks[b])
         turn_first(1, True)
-        return_gradient(FIRST, 0, banks[4])
         turn_first(1, False)
+        for t in range(2):
+            second_mean_term(t)
         for b in range(2, PACK):
             round_turned(FIRST, b, turn_banks[b])
+        return_gradient(FIRST, 0, banks[4])
+        for c in range(2):
+            turn_centred(c, banks[2 + c], range(2))
+        return_gradient(FIRST, 1, banks[5])
         centre(0, 0)
         make_shifts(6)
         for t in range(1, PACK):
             centre(t, 0)
+        quantise_queries_along_r(SECOND, 1)
         weave_centred()
+        early_banks = (banks[7], banks[1], banks[4])
         quantise_gradient(FIRST, 0)
-        early_banks = (banks[7], banks[1], banks[2])
-        return_gradient(FIRST, 1, banks[5])
-        key_gradient_pass(early_banks[0], 0, FIRST, True, False)
         quantise_gradient(SECOND, 0)
-        key_gradient_pass(early_banks[0], 0, SECOND, False, True)
+        key_gradient_pass(early_banks[0], 0, SECOND, True, False)
+        key_gradient_pass(early_banks[0], 0, FIRST, False, True)
 
         def early_plane(j, dk):
             nc.scalar.copy(dk, early_banks[j][:, half(0)])
             nc.vector.tensor_copy(windows[j][:].indirect(half_lists[0]), dk)
 
-        quantise_gradient(FIRST, 1)
-        quantise_queries_along_r(SECOND, 1)
+        behind_gradient = held([P, 2 * HALF], F32, "behind_gradient", "first_gradient0")
+        centred.append({2 + t: behind_gradient[:, t * HALF : (t + 1) * HALF] for t in range(2)})
         for t in range(2):
-            second_mean_term(t)
             centre(2 + t, 1)
+        quantise_gradient(FIRST, 1)
         early_plane(0, held([P, HALF], F32, "early0")[:])
-        turn_centred(0, banks[3])
-        round_turned(SECOND, 2, banks[3])
+        for c in range(2):
+            turn_centred(c, banks[2 + c], range(2, PACK))
+        round_turned(SECOND, 2, banks[2])
         for h in range(HEADS):
             key_gradient_pass(early_banks[1], 1, h, h == FIRST, h == SECOND)
-        turn_centred(1, banks[4])
         early_plane(1, held([P, HALF], F32, "early1")[:])
-        round_turned(SECOND, 3, banks[4])
+        round_turned(SECOND, 3, banks[3])
         for h in range(HEADS):
             key_gradient_pass(early_banks[2], 2, h, h == FIRST, h == SECOND)
         return_gradient(SECOND, 1, banks[6])
         quantise_gradient(SECOND, 1)
         early_plane(2, as_floats(turned[SECOND, PACK - 1][:]))
-        for j, bank in enumerate((banks[0], banks[5], banks[3], banks[4])):
+        for j, bank in enumerate((banks[0], banks[5], banks[3], banks[2])):
             adds = 0 < j < EARLY
             columns, entries = (half(1), half_lists[1]) if j < EARLY else (slice(0, SLOTS), offsets[:])
             if not adds:

@@ -203,8 +203,9 @@ def tile_attend_ggqa_sm_k_kernel(tc, q1, q2, kT, dp1, dp2, us, ts, w1, w2, offs,
         products = [early_products[:, 0, :], early_products[:, 1, :], scaled[:, 0, :], scaled[:, 1, :]]
         products = products + [second_products[:, t, :] for t in range(PACK)]
         means = held([P, 2, PACK, HALF], F32, "means")
-        neg_max = [held([P, 1], F32, f"neg_max{n}") for n in range(TILES)]
-        totals = q_raw[SECOND][:, 2, :TILES]
+        spare = q_raw[SECOND][:, 2, :]
+        neg_max = [spare[:, 2 * n : 2 * n + 1] if n == 1 else held([P, 1], F32, f"neg_max{n}")[:] for n in range(TILES)]
+        totals = spare[:, TILES : 2 * TILES]
         factors = {}
         row_sums = held([P, TILES], F32, "row_sums")
         shifts = held([P, TILES], F32, "shifts")
@@ -220,15 +221,18 @@ def tile_attend_ggqa_sm_k_kernel(tc, q1, q2, kT, dp1, dp2, us, ts, w1, w2, offs,
         second_means = {}
 
         def first_head_scores(t, bank):
-            for columns in (half(0), half(1)) if t == 0 else (slice(0, SLOTS),):
-                nc.tensor.matmul_mx(out=bank[:, columns], lhsT=qd_codes[FIRST][:, t * P : (t + 1) * P].bitcast(E4M3),
+            parts = ((half(0), banks[7]), (half(1), bank)) if t == 0 else ((slice(0, SLOTS), bank),)
+            for columns, target in parts:
+                nc.tensor.matmul_mx(out=target[:, columns], lhsT=qd_codes[FIRST][:, t * P : (t + 1) * P].bitcast(E4M3),
                                     lhsT_scale=qd_scales[FIRST][:, t * P : (t + 1) * P],
                                     rhs=all_k_codes[:, columns].bitcast(E4M3), rhs_scale=all_k_scales[:, columns],
                                     start=True, stop=True)
-            nc.vector.scalar_tensor_tensor(neg_z[t], bank[:], neg_us[:, t : t + 1], ts_slots[:], ALU.mult, ALU.mult)
+            for columns, target in parts:
+                nc.vector.scalar_tensor_tensor(neg_z[t][:, columns], target[:, columns], neg_us[:, t : t + 1],
+                                               ts_slots[:, columns], ALU.mult, ALU.mult)
 
         def first_head_maximum(t):
-            nc.vector.tensor_reduce(neg_max[t][:], neg_z[t], mybir.AxisListType.X, ALU.min)
+            nc.vector.tensor_reduce(neg_max[t], neg_z[t], mybir.AxisListType.X, ALU.min)
 
         def second_head_scores(b, bank):
             a, c = divmod(b, 2)
@@ -242,11 +246,11 @@ def tile_attend_ggqa_sm_k_kernel(tc, q1, q2, kT, dp1, dp2, us, ts, w1, w2, offs,
             for b in range(PACK):
                 nc.tensor.transpose(bank[:, b * P : (b + 1) * P], scaled[:, b, t * P : (t + 1) * P], ident[:])
             nc.vector.tensor_scalar(neg_z[t], bank[:], neg_us[:, t : t + 1], None, ALU.mult, ALU.min,
-                                    accum_out=neg_max[PACK + t][:])
+                                    accum_out=neg_max[PACK + t])
 
         def exponentials(n, target):
             exps[n] = target
-            nc.scalar.activation(target, neg_z[n % PACK], ACT.Exp, bias=neg_max[n][:], scale=-1.0,
+            nc.scalar.activation(target, neg_z[n % PACK], ACT.Exp, bias=neg_max[n], scale=-1.0,
                                  accum_out=totals[:, n : n + 1])
 
         def make_inverses(first, target):
@@ -275,15 +279,15 @@ def tile_attend_ggqa_sm_k_kernel(tc, q1, q2, kT, dp1, dp2, us, ts, w1, w2, offs,
             nc.vector.scalar_tensor_tensor(centred[a][t], exps[n][:, half(a)], shifts[:, n : n + 1],
                                            products[n][:, half(a)], ALU.mult, ALU.add)
 
-        def turn_first(a, opens):
-            for t in range(PACK):
+        def turn_first(a, opens, tiles):
+            for t in tiles:
                 term = products[t][:, half(a)] if opens else means[:, a, t, :]
                 for c in range(2):
                     nc.tensor.matmul(quarters(turn_banks[2 * a + c])[:, t, :], term[:, c * P : (c + 1) * P], ident[:],
                                      start=opens and t == 0, stop=not opens and t == PACK - 1, is_transpose=True)
 
         def second_mean_term(t):
-            second_means[t] = means[:, 0, PACK - 1 - t, :]
+            second_means[t] = means[:, 1, t, :]
             nc.scalar.activation(second_means[t], exps[PACK + t][:, half(1)], ACT.Copy,
                                  scale=shifts[:, PACK + t : PACK + t + 1])
 
@@ -331,8 +335,6 @@ def tile_attend_ggqa_sm_k_kernel(tc, q1, q2, kT, dp1, dp2, us, ts, w1, w2, offs,
 
         for t in range(2):
             first_head_scores(t, banks[t])
-        for t in range(2):
-            first_head_maximum(t)
         rounded = []
 
         def round_second_queries(start, stop, tag):
@@ -343,7 +345,10 @@ def tile_attend_ggqa_sm_k_kernel(tc, q1, q2, kT, dp1, dp2, us, ts, w1, w2, offs,
         round_second_queries(0, PACK - 1, "ts_runs")
         for u in range(2):
             weave_queries(SECOND, u)
+        first_head_maximum(0)
+        for u in range(2):
             quantise_queries_along_d(SECOND, u)
+        first_head_maximum(1)
         round_second_queries(PACK - 1, PACK, "second_woven1")
         for t in range(2, PACK):
             first_head_scores(t, banks[t])
@@ -371,8 +376,8 @@ def tile_attend_ggqa_sm_k_kernel(tc, q1, q2, kT, dp1, dp2, us, ts, w1, w2, offs,
                 make_inverses(2, scaled[:, 3, P : P + 2])
             if t == 2:
                 make_factors(2, scaled[:, 3, 2 * P : 2 * P + 4])
-        for v in range(2):
-            turn_rounded_queries(rounded, v, banks[6 + v])
+        for v, bank in enumerate((banks[6], banks[1])):
+            turn_rounded_queries(rounded, v, bank)
         make_products(2)
         make_inverses(4, scaled[:, 3, 3 * P : 3 * P + 2])
         make_products(3)
@@ -390,12 +395,14 @@ def tile_attend_ggqa_sm_k_kernel(tc, q1, q2, kT, dp1, dp2, us, ts, w1, w2, offs,
         for a in range(2):
             for t in range(PACK):
                 mean_term(t, a)
-        turn_first(0, True)
-        turn_first(0, False)
+        for a in range(2):
+            turn_first(a, True, range(2))
+        turn_first(0, True, range(2, PACK))
+        turn_first(0, False, range(PACK))
         for b in range(2):
             round_turned(FIRST, b, turn_banks[b])
-        turn_first(1, True)
-        turn_first(1, False)
+        turn_first(1, True, range(2, PACK))
+        turn_first(1, False, range(PACK))
         for t in range(2):
             second_mean_term(t)
         for b in range(2, PACK):
@@ -429,8 +436,8 @@ def tile_attend_ggqa_sm_k_kernel(tc, q1, q2, kT, dp1, dp2, us, ts, w1, w2, offs,
         for c in range(2):
             turn_centred(c, banks[2 + c], range(2, PACK))
         round_turned(SECOND, 2, banks[2])
-        for h in range(HEADS):
-            key_gradient_pass(early_banks[1], 1, h, h == FIRST, h == SECOND)
+        for h in (SECOND, FIRST):
+            key_gradient_pass(early_banks[1], 1, h, h == SECOND, h == FIRST)
         early_plane(1, held([P, HALF], F32, "early1")[:])
         round_turned(SECOND, 3, banks[3])
         for h in range(HEADS):

@@ -110,8 +110,7 @@ def tile_attend_ggqa_sm_k_kernel(tc, q1, q2, kT, dp1, dp2, us, ts, w1, w2, offs,
         qd_codes = [held([P, R], U32, f"qd_codes{h}") for h in range(HEADS)]
         qd_scales = [held([P, R], U8, f"qd_scales{h}") for h in range(HEADS)]
         qr_woven = {(FIRST, v): held([P, 2 * P * PACK], BF16, f"qr_woven{v}")[:] for v in range(2)}
-        qr_first = held([P, 2, 2 * P], U32, "qr_codes0")
-        qr_codes = [[qr_first[:, v, :] for v in range(2)],
+        qr_codes = [[held([P, 2 * P], U32, "qr_codes0_0")[:]],
                     [held([P, 2 * P], U32, f"qr_codes1_{v}")[:] for v in range(2)]]
         qr_scales = [[held([P, 2 * P], U8, f"qr_scales{h}_{v}") for v in range(2)] for h in range(HEADS)]
 
@@ -177,12 +176,14 @@ def tile_attend_ggqa_sm_k_kernel(tc, q1, q2, kT, dp1, dp2, us, ts, w1, w2, offs,
             if j == 1:
                 q_raw.append(held([P, PACK, R], F32, "q_raw1", "k_plane1"))
                 nc.sync.dma_start(q_raw[SECOND][:], q2.rearrange("(p j) r -> p j r", j=PACK))
-                for v in range(2):
-                    quantise_queries_along_r(FIRST, v)
+                quantise_queries_along_r(FIRST, 0)
                 for place in range(2):
                     nc.scalar.copy(both_woven[:, :, :, place].rearrange("p a i -> p (a i)"), k_pair[:, place, :])
+            if j == 2:
+                qr_codes[FIRST].append(held([P, 2 * P], U32, "qr_codes0_1", "k_plane2")[:])
+                quantise_queries_along_r(FIRST, 1)
             if j >= 2:
-                dp_sb.append(held([P, PACK, SLOTS], F32, f"dp_sb{j - 2}", f"k_plane{j % 3}"))
+                dp_sb.append(held([P, PACK, SLOTS], F32, f"dp_sb{j - 2}", "qr_woven1" if j == 2 else "k_plane0"))
                 nc.sync.dma_start(dp_sb[-1][:], (dp1, dp2)[j - 2].rearrange("(s t) i -> s t i", t=PACK))
         for a in range(2):
             quantise(k_woven[a].rearrange("p i j -> p (i j)"), E4M3, k_codes[a], k_scales[a])
@@ -203,9 +204,8 @@ def tile_attend_ggqa_sm_k_kernel(tc, q1, q2, kT, dp1, dp2, us, ts, w1, w2, offs,
         products = [early_products[:, 0, :], early_products[:, 1, :], scaled[:, 0, :], scaled[:, 1, :]]
         products = products + [second_products[:, t, :] for t in range(PACK)]
         means = held([P, 2, PACK, HALF], F32, "means")
-        spare = q_raw[SECOND][:, 2, :]
-        neg_max = [spare[:, 2 * n : 2 * n + 1] if n == 1 else held([P, 1], F32, f"neg_max{n}")[:] for n in range(TILES)]
-        totals = spare[:, TILES : 2 * TILES]
+        neg_max = [held([P, 1], F32, f"neg_max{n}")[:] for n in range(TILES)]
+        totals = q_raw[SECOND][:, 2, :TILES]
         factors = {}
         row_sums = held([P, TILES], F32, "row_sums")
         shifts = held([P, TILES], F32, "shifts")
@@ -335,6 +335,8 @@ def tile_attend_ggqa_sm_k_kernel(tc, q1, q2, kT, dp1, dp2, us, ts, w1, w2, offs,
 
         for t in range(2):
             first_head_scores(t, banks[t])
+        for t in range(2):
+            first_head_maximum(t)
         rounded = []
 
         def round_second_queries(start, stop, tag):
@@ -345,10 +347,8 @@ def tile_attend_ggqa_sm_k_kernel(tc, q1, q2, kT, dp1, dp2, us, ts, w1, w2, offs,
         round_second_queries(0, PACK - 1, "ts_runs")
         for u in range(2):
             weave_queries(SECOND, u)
-        first_head_maximum(0)
         for u in range(2):
             quantise_queries_along_d(SECOND, u)
-        first_head_maximum(1)
         round_second_queries(PACK - 1, PACK, "second_woven1")
         for t in range(2, PACK):
             first_head_scores(t, banks[t])
@@ -436,8 +436,8 @@ def tile_attend_ggqa_sm_k_kernel(tc, q1, q2, kT, dp1, dp2, us, ts, w1, w2, offs,
         for c in range(2):
             turn_centred(c, banks[2 + c], range(2, PACK))
         round_turned(SECOND, 2, banks[2])
-        for h in (SECOND, FIRST):
-            key_gradient_pass(early_banks[1], 1, h, h == SECOND, h == FIRST)
+        for h in range(HEADS):
+            key_gradient_pass(early_banks[1], 1, h, h == FIRST, h == SECOND)
         early_plane(1, held([P, HALF], F32, "early1")[:])
         round_turned(SECOND, 3, banks[3])
         for h in range(HEADS):

@@ -114,9 +114,9 @@ def tile_attend_ggqa_sm_k_kernel(tc, q1, q2, kT, dp1, dp2, us, ts, w1, w2, offs,
                     [held([P, 2 * P], U32, f"qr_codes1_{v}")[:] for v in range(2)]]
         qr_scales = [[held([P, 2 * P], U8, f"qr_scales{h}_{v}") for v in range(2)] for h in range(HEADS)]
 
-        def weave_queries(h, u):
-            nc.scalar.copy(q_woven[h][u].rearrange("p e s j -> p s j e"),
-                           q_raw[h][:].rearrange("p j (s t) -> p s j t", t=PACK)[:, :, :, 2 * u : 2 * u + 2])
+        def weave_queries(h, u, copy, rows=slice(0, P)):
+            copy(q_woven[h][u].rearrange("p e s j -> p s j e")[:, rows],
+                 q_raw[h][:].rearrange("p j (s t) -> p s j t", t=PACK)[:, rows, :, 2 * u : 2 * u + 2])
 
         def quantise_queries_along_d(h, u):
             quantise(q_woven[h][u].rearrange("p e s j -> p (e s j)"), E4M3,
@@ -144,7 +144,7 @@ def tile_attend_ggqa_sm_k_kernel(tc, q1, q2, kT, dp1, dp2, us, ts, w1, w2, offs,
             quantise(qr_woven[h, v], E4M3, qr_codes[h][v], qr_scales[h][v][:])
 
         for u in range(2):
-            weave_queries(FIRST, u)
+            weave_queries(FIRST, u, nc.scalar.copy)
             quantise_queries_along_d(FIRST, u)
         for v in range(2):
             turn_queries(FIRST, v, banks[4 + v])
@@ -197,15 +197,17 @@ def tile_attend_ggqa_sm_k_kernel(tc, q1, q2, kT, dp1, dp2, us, ts, w1, w2, offs,
 
         first_gradient = [held([P, HALF, PACK], BF16, f"first_gradient{a}")[:] for a in range(2)]
         g_woven = [first_gradient, [held([P, HALF, PACK], BF16, f"second_gradient{a}")[:] for a in range(2)]]
-        neg_z = [held([P, SLOTS], F32, f"neg_z{t}")[:] for t in range(2)] + [q_raw[SECOND][:, t, :] for t in range(2)]
-        scaled = held([P, PACK, R], F32, "scaled")
+        behind_weave = held([P, 2 * PACK, SLOTS], F32, "behind_weave", "second_woven0")
+        neg_z = [behind_weave[:, t, :] for t in range(PACK)]
+        scaled = behind_weave[:, PACK:, :]
+        first_scaled = scaled[:, 2:, :].rearrange("p a (c r) -> p (a c) r", c=2)
         second_products = held([P, PACK, SLOTS], F32, "second_products", "q_raw0")
         early_products = held([P, 2, SLOTS], F32, "early_products")
         products = [early_products[:, 0, :], early_products[:, 1, :], scaled[:, 0, :], scaled[:, 1, :]]
         products = products + [second_products[:, t, :] for t in range(PACK)]
         means = held([P, 2, PACK, HALF], F32, "means")
         neg_max = [held([P, 1], F32, f"neg_max{n}")[:] for n in range(TILES)]
-        totals = q_raw[SECOND][:, 2, :TILES]
+        totals = held([P, TILES], F32, "totals")[:]
         factors = {}
         row_sums = held([P, TILES], F32, "row_sums")
         shifts = held([P, TILES], F32, "shifts")
@@ -221,15 +223,25 @@ def tile_attend_ggqa_sm_k_kernel(tc, q1, q2, kT, dp1, dp2, us, ts, w1, w2, offs,
         second_means = {}
 
         def first_head_scores(t, bank):
-            parts = ((half(0), banks[7]), (half(1), bank)) if t == 0 else ((slice(0, SLOTS), bank),)
-            for columns, target in parts:
-                nc.tensor.matmul_mx(out=target[:, columns], lhsT=qd_codes[FIRST][:, t * P : (t + 1) * P].bitcast(E4M3),
-                                    lhsT_scale=qd_scales[FIRST][:, t * P : (t + 1) * P],
-                                    rhs=all_k_codes[:, columns].bitcast(E4M3), rhs_scale=all_k_scales[:, columns],
+            nc.tensor.matmul_mx(out=bank[:], lhsT=qd_codes[FIRST][:, t * P : (t + 1) * P].bitcast(E4M3),
+                                lhsT_scale=qd_scales[FIRST][:, t * P : (t + 1) * P],
+                                rhs=all_k_codes[:].bitcast(E4M3), rhs_scale=all_k_scales[:], start=True, stop=True)
+            nc.vector.scalar_tensor_tensor(neg_z[t], bank[:], neg_us[:, t : t + 1], ts_slots[:], ALU.mult, ALU.mult)
+
+        def late_first_scores(pair):
+            for b in range(PACK):
+                nc.tensor.matmul_mx(out=pair[b // 2][:, half(b % 2)], lhsT=all_k_codes[:, b * P : (b + 1) * P].bitcast(E4M3),
+                                    lhsT_scale=all_k_scales[:, b * P : (b + 1) * P],
+                                    rhs=qd_codes[FIRST][:, 2 * P :].bitcast(E4M3), rhs_scale=qd_scales[FIRST][:, 2 * P :],
                                     start=True, stop=True)
-            for columns, target in parts:
-                nc.vector.scalar_tensor_tensor(neg_z[t][:, columns], target[:, columns], neg_us[:, t : t + 1],
-                                               ts_slots[:, columns], ALU.mult, ALU.mult)
+            for b in range(PACK):
+                nc.scalar.activation(first_scaled[:, b, :], pair[b // 2][:, half(b % 2)], ACT.Copy,
+                                     scale=ts_cols[:, b : b + 1])
+
+        def late_first_rows(t, bank):
+            for b in range(PACK):
+                nc.tensor.transpose(bank[:, b * P : (b + 1) * P], first_scaled[:, b, (t - 2) * P : (t - 1) * P], ident[:])
+            nc.vector.tensor_scalar(neg_z[t], bank[:], neg_us[:, t : t + 1], None, ALU.mult, ALU.min, accum_out=neg_max[t])
 
         def first_head_maximum(t):
             nc.vector.tensor_reduce(neg_max[t], neg_z[t], mybir.AxisListType.X, ALU.min)
@@ -333,37 +345,33 @@ def tile_attend_ggqa_sm_k_kernel(tc, q1, q2, kT, dp1, dp2, us, ts, w1, w2, offs,
 
         out_planes = out.rearrange("(p j) c -> j p c", j=PACK)
 
-        for t in range(2):
-            first_head_scores(t, banks[t])
-        for t in range(2):
-            first_head_maximum(t)
-        rounded = []
-
-        def round_second_queries(start, stop, tag):
-            target = held([P, stop - start, R], BF16, f"rounded{start}", tag)
-            rounded.extend(target[:, j, :] for j in range(stop - start))
-            nc.gpsimd.tensor_scalar(target[:], q_raw[SECOND][:, start:stop, :], 1.0, 0.0, ALU.mult, ALU.add)
-
-        round_second_queries(0, PACK - 1, "ts_runs")
-        for u in range(2):
-            weave_queries(SECOND, u)
-        for u in range(2):
-            quantise_queries_along_d(SECOND, u)
-        round_second_queries(PACK - 1, PACK, "second_woven1")
-        for t in range(2, PACK):
-            first_head_scores(t, banks[t])
-
         def small(columns, name):
             return held([P, columns], F32, name)[:]
 
+        weave_queries(SECOND, 0, nc.vector.tensor_copy)
+        weave_queries(SECOND, 1, nc.vector.tensor_copy, slice(0, P // 2))
+        weave_queries(SECOND, 1, nc.scalar.copy, slice(P // 2, P))
+        for u in range(2):
+            quantise_queries_along_d(SECOND, u)
+        late_first_scores(banks[6:8])
         for t in range(2):
+            first_head_scores(t, banks[t])
+        all_rounded = held([P, PACK, R], BF16, "rounded", "second_woven1")
+        rounded = [all_rounded[:, j, :] for j in range(PACK)]
+        for v in range(2):
+            nc.gpsimd.tensor_scalar(all_rounded[:, 2 * v : 2 * v + 2, :], q_raw[SECOND][:, 2 * v : 2 * v + 2, :], 1.0, 0.0,
+                                    ALU.mult, ALU.add)
+        for b in range(2):
+            second_head_scores(b, banks[4 + b])
+        for t in range(2):
+            first_head_maximum(t)
             exponentials(t, held([P, SLOTS], F32, f"first_e{t}")[:])
+        late_first_rows(2, banks[0])
         make_inverses(0, small(2, "inverses0"))
-        first_head_maximum(2)
+        late_first_rows(3, banks[1])
         make_factors(0, small(4, "factors0"))
-        first_head_maximum(3)
-        for b, bank in enumerate((banks[4], banks[5], banks[0], banks[1])):
-            second_head_scores(b, bank)
+        for b in range(2, PACK):
+            second_head_scores(b, banks[b])
         for t, tag in ((2, "qd_codes1"), (3, "k_codes")):
             exponentials(t, held([P, SLOTS], F32, f"first_e{t}", tag)[:])
         for n in range(2):

@@ -353,9 +353,9 @@ def tile_attend_ggqa_sm_k_kernel(tc, q1, q2, kT, dp1, dp2, us, ts, w1, w2, offs,
         weave_queries(SECOND, 1, nc.scalar.copy, slice(P // 2, P))
         for u in range(2):
             quantise_queries_along_d(SECOND, u)
+        first_head_scores(0, banks[0])
         late_first_scores(banks[6:8])
-        for t in range(2):
-            first_head_scores(t, banks[t])
+        first_head_scores(1, banks[1])
         all_rounded = held([P, PACK, R], BF16, "rounded", "second_woven1")
         rounded = [all_rounded[:, j, :] for j in range(PACK)]
         for v in range(2):
@@ -371,7 +371,7 @@ def tile_attend_ggqa_sm_k_kernel(tc, q1, q2, kT, dp1, dp2, us, ts, w1, w2, offs,
         late_first_rows(3, banks[1])
         make_factors(0, small(4, "factors0"))
         for b in range(2, PACK):
-            second_head_scores(b, banks[b])
+            second_head_scores(b, banks[2 + b])
         for t, tag in ((2, "qd_codes1"), (3, "k_codes")):
             exponentials(t, held([P, SLOTS], F32, f"first_e{t}", tag)[:])
         for n in range(2):
@@ -384,7 +384,7 @@ def tile_attend_ggqa_sm_k_kernel(tc, q1, q2, kT, dp1, dp2, us, ts, w1, w2, offs,
                 make_inverses(2, scaled[:, 3, P : P + 2])
             if t == 2:
                 make_factors(2, scaled[:, 3, 2 * P : 2 * P + 4])
-        for v, bank in enumerate((banks[6], banks[1])):
+        for v, bank in enumerate((banks[0], banks[1])):
             turn_rounded_queries(rounded, v, bank)
         make_products(2)
         make_inverses(4, scaled[:, 3, 3 * P : 3 * P + 2])
@@ -425,7 +425,7 @@ def tile_attend_ggqa_sm_k_kernel(tc, q1, q2, kT, dp1, dp2, us, ts, w1, w2, offs,
             centre(t, 0)
         quantise_queries_along_r(SECOND, 1)
         weave_centred()
-        early_banks = (banks[7], banks[1], banks[4])
+        early_banks = (banks[7], banks[1], banks[3])
         quantise_gradient(FIRST, 0)
         quantise_gradient(SECOND, 0)
         key_gradient_pass(early_banks[0], 0, SECOND, True, False)
@@ -448,12 +448,12 @@ def tile_attend_ggqa_sm_k_kernel(tc, q1, q2, kT, dp1, dp2, us, ts, w1, w2, offs,
             key_gradient_pass(early_banks[1], 1, h, h == FIRST, h == SECOND)
         early_plane(1, held([P, HALF], F32, "early1")[:])
         round_turned(SECOND, 3, banks[3])
+        return_gradient(SECOND, 1, banks[6])
         for h in range(HEADS):
             key_gradient_pass(early_banks[2], 2, h, h == FIRST, h == SECOND)
-        return_gradient(SECOND, 1, banks[6])
         quantise_gradient(SECOND, 1)
         early_plane(2, as_floats(turned[SECOND, PACK - 1][:]))
-        for j, bank in enumerate((banks[0], banks[5], banks[3], banks[2])):
+        for j, bank in enumerate((banks[0], banks[5], banks[4], banks[2])):
             adds = 0 < j < EARLY
             columns, entries = (half(1), half_lists[1]) if j < EARLY else (slice(0, SLOTS), offsets[:])
             if not adds:

@@ -25,7 +25,6 @@ HALF = SLOTS // 2
 RUN = TOKENS // P
 LINE = 4
 FIRST, SECOND = 0, 1
-EARLY = 3
 TILES = HEADS * PACK
 FLOPS = 4 * 2 * D * R * SLOTS
 
@@ -73,9 +72,6 @@ def tile_attend_ggqa_sm_k_kernel(tc, q1, q2, kT, dp1, dp2, us, ts, w1, w2, offs,
 
         g_codes = [held([P, SLOTS], U32, f"g_codes{h}") for h in range(HEADS)]
         g_scales = [held([P, SLOTS], U8, f"g_scales{h}") for h in range(HEADS)]
-        for h in range(HEADS):
-            nc.gpsimd.memset(g_codes[h][:, HALF:], 0)
-            nc.gpsimd.memset(g_scales[h][:, HALF:].bitcast(U32), 0)
 
         windows = {}
 
@@ -220,8 +216,6 @@ def tile_attend_ggqa_sm_k_kernel(tc, q1, q2, kT, dp1, dp2, us, ts, w1, w2, offs,
             return view.rearrange("p a b c -> p (a b c)").bitcast(F32)
 
 
-        second_means = {}
-
         def first_head_scores(t, bank):
             nc.tensor.matmul_mx(out=bank[:], lhsT=qd_codes[FIRST][:, t * P : (t + 1) * P].bitcast(E4M3),
                                 lhsT_scale=qd_scales[FIRST][:, t * P : (t + 1) * P],
@@ -298,21 +292,6 @@ def tile_attend_ggqa_sm_k_kernel(tc, q1, q2, kT, dp1, dp2, us, ts, w1, w2, offs,
                     nc.tensor.matmul(quarters(turn_banks[2 * a + c])[:, t, :], term[:, c * P : (c + 1) * P], ident[:],
                                      start=opens and t == 0, stop=not opens and t == PACK - 1, is_transpose=True)
 
-        def second_mean_term(t):
-            second_means[t] = means[:, 1, t, :]
-            nc.scalar.activation(second_means[t], exps[PACK + t][:, half(1)], ACT.Copy,
-                                 scale=shifts[:, PACK + t : PACK + t + 1])
-
-        def turn_centred(c, bank, tiles):
-            block = slice(c * P, (c + 1) * P)
-            for t in tiles:
-                if t < 2:
-                    for opens, term in ((True, products[PACK + t][:, half(1)]), (False, second_means[t])):
-                        nc.tensor.matmul(quarters(bank)[:, t, :], term[:, block], ident[:], start=opens, stop=not opens,
-                                         is_transpose=True)
-                else:
-                    nc.tensor.transpose(quarters(bank)[:, t, :], centred[1][t][:, block], ident[:])
-
         def round_turned(h, b, bank):
             turned[h, b] = held([P, 2, P, 2], BF16, f"g_turned{h}_{b}")
             nc.scalar.activation(turned[h, b][:], quarters(bank).rearrange("i (u e) s -> i u s e", e=2), ACT.Copy,
@@ -326,22 +305,22 @@ def tile_attend_ggqa_sm_k_kernel(tc, q1, q2, kT, dp1, dp2, us, ts, w1, w2, offs,
             target = g_woven[h][a].rearrange("s i t -> s (i t)").bitcast(F32).rearrange("s (i u) -> s i u", u=2)
             nc.scalar.copy(target, halves(bank).rearrange("s u i -> s i u"))
 
-        def weave_centred():
-            ts_lines = ts_slots[:, half(0)].rearrange("p (c i) -> p c i", i=LINE).unsqueeze(2)
-            nc.vector.tensor_tensor(g_woven[SECOND][0].rearrange("p (c i) t -> p c t i", i=LINE),
-                                    first_centred[:].rearrange("p t (c i) -> p c t i", i=LINE),
+        def weave_centred(a, source):
+            ts_lines = ts_slots[:, half(a)].rearrange("p (c i) -> p c i", i=LINE).unsqueeze(2)
+            nc.vector.tensor_tensor(g_woven[SECOND][a].rearrange("p (c i) t -> p c t i", i=LINE),
+                                    source.rearrange("p t (c i) -> p c t i", i=LINE),
                                     ts_lines.to_broadcast([P, HALF // LINE, PACK, LINE]), ALU.mult)
 
         def quantise_gradient(h, a):
             columns = half(a)
             quantise(g_woven[h][a].rearrange("p i t -> p (i t)"), E5M2, g_codes[h][:, columns], g_scales[h][:, columns])
 
-        def key_gradient_pass(bank, j, h, start, stop):
+        def key_gradient_pass(target, j, h, columns):
             planes = slice(j % 2 * P, (j % 2 + 1) * P)
-            nc.tensor.matmul_mx(out=bank[:], lhsT=qr_codes[h][j // 2][:, planes].bitcast(E4M3),
+            nc.tensor.matmul_mx(out=target, lhsT=qr_codes[h][j // 2][:, planes].bitcast(E4M3),
                                 lhsT_scale=qr_scales[h][j // 2][:, planes],
-                                rhs=g_codes[h][:].bitcast(E5M2), rhs_scale=g_scales[h][:],
-                                start=start, stop=stop)
+                                rhs=g_codes[h][:, columns].bitcast(E5M2), rhs_scale=g_scales[h][:, columns],
+                                start=h == FIRST, stop=h == SECOND)
 
         out_planes = out.rearrange("(p j) c -> j p c", j=PACK)
 
@@ -411,60 +390,51 @@ def tile_attend_ggqa_sm_k_kernel(tc, q1, q2, kT, dp1, dp2, us, ts, w1, w2, offs,
             round_turned(FIRST, b, turn_banks[b])
         turn_first(1, True, range(2, PACK))
         turn_first(1, False, range(PACK))
-        for t in range(2):
-            second_mean_term(t)
         for b in range(2, PACK):
             round_turned(FIRST, b, turn_banks[b])
         return_gradient(FIRST, 0, banks[4])
-        for c in range(2):
-            turn_centred(c, banks[2 + c], range(2))
         return_gradient(FIRST, 1, banks[5])
         centre(0, 0)
         make_shifts(6)
         for t in range(1, PACK):
             centre(t, 0)
         quantise_queries_along_r(SECOND, 1)
-        weave_centred()
-        early_banks = (banks[7], banks[1], banks[3])
+        weave_centred(0, first_centred[:])
         quantise_gradient(FIRST, 0)
         quantise_gradient(SECOND, 0)
-        key_gradient_pass(early_banks[0], 0, SECOND, True, False)
-        key_gradient_pass(early_banks[0], 0, FIRST, False, True)
 
-        def early_plane(j, dk):
-            nc.scalar.copy(dk, early_banks[j][:, half(0)])
-            nc.vector.tensor_copy(windows[j][:].indirect(half_lists[0]), dk)
+        def sums(j, columns, bank, first=0):
+            target = bank[:, first : first + columns.stop - columns.start]
+            for h in range(HEADS):
+                key_gradient_pass(target, j, h, columns)
+            return target
 
-        behind_gradient = held([P, 2 * HALF], F32, "behind_gradient", "first_gradient0")
-        centred.append({2 + t: behind_gradient[:, t * HALF : (t + 1) * HALF] for t in range(2)})
-        for t in range(2):
-            centre(2 + t, 1)
+        def vector_scatter(j, name, source, entries):
+            dk = held(list(source.shape), F32, name)
+            nc.vector.tensor_copy(dk[:], source)
+            nc.vector.tensor_copy(windows[j][:].indirect(entries), dk[:])
+
+        def scalar_scatter(j, a, source):
+            dk = held([P, HALF], F32, f"dk{j}_{a}")
+            nc.scalar.copy(dk[:], source)
+            nc.scalar.activation(windows[j][:].indirect(half_lists[a]), dk[:], ACT.Copy)
+
+        scalar_scatter(0, 0, sums(0, half(0), banks[0]))
+        behind_gradient = held([P, PACK, HALF], F32, "behind_gradient", "first_gradient0")
+        centred.append([behind_gradient[:, t, :] for t in range(PACK)])
+        for t in range(PACK):
+            centre(t, 1)
+        scalar_scatter(1, 0, sums(1, half(0), banks[1]))
+        weave_centred(1, behind_gradient[:])
         quantise_gradient(FIRST, 1)
-        early_plane(0, held([P, HALF], F32, "early0")[:])
-        for c in range(2):
-            turn_centred(c, banks[2 + c], range(2, PACK))
-        round_turned(SECOND, 2, banks[2])
-        for h in range(HEADS):
-            key_gradient_pass(early_banks[1], 1, h, h == FIRST, h == SECOND)
-        early_plane(1, held([P, HALF], F32, "early1")[:])
-        round_turned(SECOND, 3, banks[3])
-        return_gradient(SECOND, 1, banks[6])
-        for h in range(HEADS):
-            key_gradient_pass(early_banks[2], 2, h, h == FIRST, h == SECOND)
         quantise_gradient(SECOND, 1)
-        early_plane(2, as_floats(turned[SECOND, PACK - 1][:]))
-        for j, bank in enumerate((banks[0], banks[5], banks[4], banks[2])):
-            adds = 0 < j < EARLY
-            columns, entries = (half(1), half_lists[1]) if j < EARLY else (slice(0, SLOTS), offsets[:])
-            if not adds:
-                key_gradient_pass(bank, j, FIRST, True, False)
-            key_gradient_pass(bank, j, SECOND, adds, True)
-            late = held([P, columns.stop - columns.start], F32, f"late{j}")
-            nc.scalar.copy(late[:], bank[:, columns])
-            if adds:
-                partial = held([P, HALF], F32, f"partial{j}")
-                nc.scalar.copy(partial[:], early_banks[j][:, half(1)])
-                nc.vector.tensor_tensor(windows[j][:].indirect(entries), partial[:], late[:], ALU.add)
-            else:
-                nc.vector.tensor_copy(windows[j][:].indirect(entries), late[:])
-            nc.sync.dma_start(out_planes[j], windows[j][:])
+        vector_scatter(0, "dk0_1", sums(0, half(1), banks[2]), half_lists[1])
+        nc.sync.dma_start(out_planes[0], windows[0][:])
+        scalar_scatter(1, 1, sums(1, half(1), banks[2], HALF))
+        nc.sync.dma_start(out_planes[1], windows[1][:])
+        vector_scatter(2, "dk2", sums(2, slice(0, SLOTS), banks[6]), offsets[:])
+        nc.sync.dma_start(out_planes[2], windows[2][:])
+        last = sums(3, slice(0, SLOTS), banks[7])
+        for a in range(2):
+            scalar_scatter(3, a, last[:, half(a)])
+        nc.sync.dma_start(out_planes[3], windows[3][:])

@@ -41,6 +41,12 @@ def tile_attend_ggqa_sm_k_kernel(tc, q1, q2, kT, dp1, dp2, us, ts, w1, w2, offs,
         spread_banks = [psum.tile([P, SLOTS], F32, name=f"spread{n}", tag=f"bank{n}") for n in range(RUN // PACK)]
         banks = [psum.tile([P, SLOTS], F32, name=f"bank{n}", tag=f"bank{n}") for n in range(8)]
 
+        def half(a):
+            return slice(a * HALF, (a + 1) * HALF)
+
+        def block(b):
+            return slice(b * P, (b + 1) * P)
+
         def quarters(bank):
             return bank[:].rearrange("p (c i) -> p c i", c=PACK)
 
@@ -95,8 +101,6 @@ def tile_attend_ggqa_sm_k_kernel(tc, q1, q2, kT, dp1, dp2, us, ts, w1, w2, offs,
         ts_slots = held([P, SLOTS], F32, "ts_slots")
         nc.vector.tensor_copy(ts_slots[:], ts_window[:].indirect(offsets[:]))
 
-        first_centred = held([P, PACK, HALF], F32, "centred")
-        centred = [[first_centred[:, t, :] for t in range(PACK)]]
         def quantise(source, fmt, codes, scales):
             nc.vector.quantize_mx(out=codes.bitcast(fmt), scales=scales, in_=source)
 
@@ -132,8 +136,10 @@ def tile_attend_ggqa_sm_k_kernel(tc, q1, q2, kT, dp1, dp2, us, ts, w1, w2, offs,
                 words = rounded[2 * v + e].bitcast(F32)
                 for u in range(2):
                     nc.tensor.transpose(quarters(bank)[:, 2 * e + u, :], words[:, u::2], ident[:])
-            qr_woven[SECOND, v] = held([P, 2 * P * PACK], BF16, f"second_qr_woven{v}")[:]
-            nc.scalar.copy(qr_woven[SECOND, v].bitcast(F32).rearrange("s (e p u) -> s e p u", e=2, u=2),
+
+        def weave_turned_words(v, bank, copy, tag):
+            qr_woven[SECOND, v] = held([P, 2 * P * PACK], BF16, f"second_qr_woven{v}", tag)[:]
+            copy(qr_woven[SECOND, v].bitcast(F32).rearrange("s (e p u) -> s e p u", e=2, u=2),
                            bank[:].rearrange("s (e u p) -> s e p u", e=2, u=2))
 
         def quantise_queries_along_r(h, v):
@@ -191,250 +197,275 @@ def tile_attend_ggqa_sm_k_kernel(tc, q1, q2, kT, dp1, dp2, us, ts, w1, w2, offs,
             nc.gpsimd.tensor_tensor(numerators[:, 0, PACK * h : PACK * (h + 1)], w_sb[h][:], us_sb[:], ALU.mult)
         nc.gpsimd.memset(numerators[:, 1, :], -1.0)
 
-        first_gradient = [held([P, HALF, PACK], BF16, f"first_gradient{a}")[:] for a in range(2)]
-        g_woven = [first_gradient, [held([P, HALF, PACK], BF16, f"second_gradient{a}")[:] for a in range(2)]]
-        behind_weave = held([P, 2 * PACK, SLOTS], F32, "behind_weave", "second_woven0")
-        neg_z = [behind_weave[:, t, :] for t in range(PACK)]
-        scaled = behind_weave[:, PACK:, :]
-        first_scaled = scaled[:, 2:, :].rearrange("p a (c r) -> p (a c) r", c=2)
-        second_products = held([P, PACK, SLOTS], F32, "second_products", "q_raw0")
-        early_products = held([P, 2, SLOTS], F32, "early_products")
-        products = [early_products[:, 0, :], early_products[:, 1, :], scaled[:, 0, :], scaled[:, 1, :]]
-        products = products + [second_products[:, t, :] for t in range(PACK)]
-        means = held([P, 2, PACK, HALF], F32, "means")
-        neg_max = [held([P, 1], F32, f"neg_max{n}")[:] for n in range(TILES)]
-        totals = held([P, TILES], F32, "totals")[:]
-        factors = {}
-        row_sums = held([P, TILES], F32, "row_sums")
-        shifts = held([P, TILES], F32, "shifts")
-        exps, turned, inverses = {}, {}, {}
-
-        def half(a):
-            return slice(a * HALF, (a + 1) * HALF)
-
-        def as_floats(view):
-            return view.rearrange("p a b c -> p (a b c)").bitcast(F32)
-
-
-        def first_head_scores(t, bank):
-            nc.tensor.matmul_mx(out=bank[:], lhsT=qd_codes[FIRST][:, t * P : (t + 1) * P].bitcast(E4M3),
-                                lhsT_scale=qd_scales[FIRST][:, t * P : (t + 1) * P],
-                                rhs=all_k_codes[:].bitcast(E4M3), rhs_scale=all_k_scales[:], start=True, stop=True)
-            nc.vector.scalar_tensor_tensor(neg_z[t], bank[:], neg_us[:, t : t + 1], ts_slots[:], ALU.mult, ALU.mult)
-
-        def late_first_scores(pair):
-            for b in range(PACK):
-                nc.tensor.matmul_mx(out=pair[b // 2][:, half(b % 2)], lhsT=all_k_codes[:, b * P : (b + 1) * P].bitcast(E4M3),
-                                    lhsT_scale=all_k_scales[:, b * P : (b + 1) * P],
-                                    rhs=qd_codes[FIRST][:, 2 * P :].bitcast(E4M3), rhs_scale=qd_scales[FIRST][:, 2 * P :],
-                                    start=True, stop=True)
-            for b in range(PACK):
-                nc.scalar.activation(first_scaled[:, b, :], pair[b // 2][:, half(b % 2)], ACT.Copy,
-                                     scale=ts_cols[:, b : b + 1])
-
-        def late_first_rows(t, bank):
-            for b in range(PACK):
-                nc.tensor.transpose(bank[:, b * P : (b + 1) * P], first_scaled[:, b, (t - 2) * P : (t - 1) * P], ident[:])
-            nc.vector.tensor_scalar(neg_z[t], bank[:], neg_us[:, t : t + 1], None, ALU.mult, ALU.min, accum_out=neg_max[t])
-
-        def first_head_maximum(t):
-            nc.vector.tensor_reduce(neg_max[t], neg_z[t], mybir.AxisListType.X, ALU.min)
-
-        def second_head_scores(b, bank):
-            a, c = divmod(b, 2)
-            nc.tensor.matmul_mx(out=bank[:], lhsT=k_codes[a][:, c * P : (c + 1) * P].bitcast(E4M3),
-                                lhsT_scale=k_scales[a][:, c * P : (c + 1) * P],
-                                rhs=qd_codes[SECOND][:].bitcast(E4M3), rhs_scale=qd_scales[SECOND][:],
-                                start=True, stop=True)
-            nc.scalar.activation(scaled[:, b, :], bank[:], ACT.Copy, scale=ts_cols[:, b : b + 1])
-
-        def second_head_rows(t, bank):
-            for b in range(PACK):
-                nc.tensor.transpose(bank[:, b * P : (b + 1) * P], scaled[:, b, t * P : (t + 1) * P], ident[:])
-            nc.vector.tensor_scalar(neg_z[t], bank[:], neg_us[:, t : t + 1], None, ALU.mult, ALU.min,
-                                    accum_out=neg_max[PACK + t])
-
-        def exponentials(n, target):
-            exps[n] = target
-            nc.scalar.activation(target, neg_z[n % PACK], ACT.Exp, bias=neg_max[n], scale=-1.0,
-                                 accum_out=totals[:, n : n + 1])
-
-        def make_inverses(first, target):
-            inverses[first] = target
-            nc.vector.reciprocal(target, totals[:, first : first + 2])
-
-        def make_factors(first, target):
-            factors[first] = target.rearrange("p (k e) -> p k e", k=2)
-            nc.vector.tensor_tensor(factors[first], numerators[:, :, first : first + 2],
-                                    inverses[first].unsqueeze(1).to_broadcast([P, 2, 2]), ALU.mult)
-
-        def make_products(n):
-            h, t = divmod(n, PACK)
-            nc.vector.scalar_tensor_tensor(products[n], exps[n], factors[n - n % 2][:, 0, n % 2 : n % 2 + 1],
-                                           dp_sb[h][:, t, :], ALU.mult, ALU.mult, accum_out=row_sums[:, n : n + 1])
-
-        def make_shifts(first):
-            nc.vector.tensor_tensor(shifts[:, first : first + 2], row_sums[:, first : first + 2], factors[first][:, 1, :],
-                                    ALU.mult)
-
-        def mean_term(t, a):
-            nc.scalar.activation(means[:, a, t, :], exps[t][:, half(a)], ACT.Copy, scale=shifts[:, t : t + 1])
-
-        def centre(t, a):
-            n = PACK + t
-            nc.vector.scalar_tensor_tensor(centred[a][t], exps[n][:, half(a)], shifts[:, n : n + 1],
-                                           products[n][:, half(a)], ALU.mult, ALU.add)
-
-        def turn_first(a, opens, tiles):
-            for t in tiles:
-                term = products[t][:, half(a)] if opens else means[:, a, t, :]
-                for c in range(2):
-                    nc.tensor.matmul(quarters(turn_banks[2 * a + c])[:, t, :], term[:, c * P : (c + 1) * P], ident[:],
-                                     start=opens and t == 0, stop=not opens and t == PACK - 1, is_transpose=True)
-
-        def round_turned(h, b, bank):
-            turned[h, b] = held([P, 2, P, 2], BF16, f"g_turned{h}_{b}")
-            nc.scalar.activation(turned[h, b][:], quarters(bank).rearrange("i (u e) s -> i u s e", e=2), ACT.Copy,
-                                 scale=ts_cols[:, b : b + 1])
-
-        def return_gradient(h, a, bank):
-            for c in range(2):
-                words = as_floats(turned[h, 2 * a + c][:])
-                for u in range(2):
-                    nc.tensor.transpose(halves(bank)[:, u, c * P : (c + 1) * P], words[:, u * P : (u + 1) * P], ident[:])
-            target = g_woven[h][a].rearrange("s i t -> s (i t)").bitcast(F32).rearrange("s (i u) -> s i u", u=2)
-            nc.scalar.copy(target, halves(bank).rearrange("s u i -> s i u"))
-
-        def weave_centred(a, source):
-            ts_lines = ts_slots[:, half(a)].rearrange("p (c i) -> p c i", i=LINE).unsqueeze(2)
-            nc.vector.tensor_tensor(g_woven[SECOND][a].rearrange("p (c i) t -> p c t i", i=LINE),
-                                    source.rearrange("p t (c i) -> p c t i", i=LINE),
-                                    ts_lines.to_broadcast([P, HALF // LINE, PACK, LINE]), ALU.mult)
-
-        def quantise_gradient(h, a):
-            columns = half(a)
-            quantise(g_woven[h][a].rearrange("p i t -> p (i t)"), E5M2, g_codes[h][:, columns], g_scales[h][:, columns])
-
-        def key_gradient_pass(target, j, h, columns):
-            planes = slice(j % 2 * P, (j % 2 + 1) * P)
-            nc.tensor.matmul_mx(out=target, lhsT=qr_codes[h][j // 2][:, planes].bitcast(E4M3),
-                                lhsT_scale=qr_scales[h][j // 2][:, planes],
-                                rhs=g_codes[h][:, columns].bitcast(E5M2), rhs_scale=g_scales[h][:, columns],
-                                start=h == FIRST, stop=h == SECOND)
-
-        out_planes = out.rearrange("(p j) c -> j p c", j=PACK)
-
-        def small(columns, name):
-            return held([P, columns], F32, name)[:]
 
         weave_queries(SECOND, 0, nc.vector.tensor_copy)
         weave_queries(SECOND, 1, nc.vector.tensor_copy, slice(0, P // 2))
         weave_queries(SECOND, 1, nc.scalar.copy, slice(P // 2, P))
         for u in range(2):
             quantise_queries_along_d(SECOND, u)
-        first_head_scores(0, banks[0])
-        late_first_scores(banks[6:8])
-        first_head_scores(1, banks[1])
-        all_rounded = held([P, PACK, R], BF16, "rounded", "second_woven1")
-        rounded = [all_rounded[:, j, :] for j in range(PACK)]
-        for v in range(2):
-            nc.gpsimd.tensor_scalar(all_rounded[:, 2 * v : 2 * v + 2, :], q_raw[SECOND][:, 2 * v : 2 * v + 2, :], 1.0, 0.0,
-                                    ALU.mult, ALU.add)
-        for b in range(2):
-            second_head_scores(b, banks[4 + b])
-        for t in range(2):
-            first_head_maximum(t)
-            exponentials(t, held([P, SLOTS], F32, f"first_e{t}")[:])
-        late_first_rows(2, banks[0])
-        make_inverses(0, small(2, "inverses0"))
-        late_first_rows(3, banks[1])
-        make_factors(0, small(4, "factors0"))
-        for b in range(2, PACK):
-            second_head_scores(b, banks[2 + b])
-        for t, tag in ((2, "qd_codes1"), (3, "k_codes")):
-            exponentials(t, held([P, SLOTS], F32, f"first_e{t}", tag)[:])
-        for n in range(2):
-            make_products(n)
-        make_shifts(0)
-        for t, bank in enumerate((banks[2], banks[3], banks[4], banks[5])):
-            second_head_rows(t, bank)
-            exponentials(PACK + t, held([P, SLOTS], F32, f"e{t}")[:])
-            if t == 1:
-                make_inverses(2, scaled[:, 3, P : P + 2])
-            if t == 2:
-                make_factors(2, scaled[:, 3, 2 * P : 2 * P + 4])
-        for v, bank in enumerate((banks[0], banks[1])):
-            turn_rounded_queries(rounded, v, bank)
-        make_products(2)
-        make_inverses(4, scaled[:, 3, 3 * P : 3 * P + 2])
-        make_products(3)
-        make_factors(4, small(4, "factors4"))
-        make_inverses(6, small(2, "inverses6"))
-        make_products(4)
-        make_shifts(2)
-        make_factors(6, small(4, "factors6"))
-        make_products(5)
-        quantise_queries_along_r(SECOND, 0)
-        make_products(6)
-        make_shifts(4)
-        make_products(7)
-        turn_banks = (banks[2], banks[3], banks[6], banks[7])
-        for a in range(2):
-            for t in range(PACK):
-                mean_term(t, a)
-        for a in range(2):
-            turn_first(a, True, range(2))
-        turn_first(0, True, range(2, PACK))
-        turn_first(0, False, range(PACK))
-        for b in range(2):
-            round_turned(FIRST, b, turn_banks[b])
-        turn_first(1, True, range(2, PACK))
-        turn_first(1, False, range(PACK))
-        for b in range(2, PACK):
-            round_turned(FIRST, b, turn_banks[b])
-        return_gradient(FIRST, 0, banks[4])
-        return_gradient(FIRST, 1, banks[5])
-        centre(0, 0)
-        make_shifts(6)
-        for t in range(1, PACK):
-            centre(t, 0)
-        quantise_queries_along_r(SECOND, 1)
-        weave_centred(0, first_centred[:])
-        quantise_gradient(FIRST, 0)
-        quantise_gradient(SECOND, 0)
 
-        def sums(j, columns, bank, first=0):
-            target = bank[:, first : first + columns.stop - columns.start]
-            for h in range(HEADS):
-                key_gradient_pass(target, j, h, columns)
+        behind_weave = held([P, 4 * SLOTS], F32, "behind_weave", "second_woven0")
+        neg_z = [behind_weave[:, t * SLOTS : (t + 1) * SLOTS] for t in range(2)]
+        neg_z = neg_z + [held([P, SLOTS], F32, f"neg_z{n}")[:] for n in range(2, TILES)]
+        exps = [held([P, SLOTS], F32, f"e{n}")[:] for n in range(TILES)]
+        neg_max = [held([P, 1], F32, f"neg_max{n}")[:] for n in range(TILES)]
+        second_scaled = held([P, PACK * R], F32, "second_scaled")
+        scaled = [[behind_weave[:, 2 * SLOTS + b * HALF : 2 * SLOTS + (b + 1) * HALF] for b in range(PACK)],
+                  [second_scaled[:, b * R : (b + 1) * R] for b in range(PACK)]]
+        products = [held([P, SLOTS], F32, f"products{n}")[:] for n in range(TILES)]
+        totals = held([P, TILES], F32, "totals")
+        row_sums = held([P, TILES], F32, "row_sums")
+        last_scaled = scaled[SECOND][PACK - 1]
+        inverses = [last_scaled[:, 2 * P : 2 * P + 2], last_scaled[:, 3 * P : 3 * P + 2], dp_sb[FIRST][:, 0, 0:2], dp_sb[FIRST][:, 2, 0:2]]
+        factors = [last_scaled[:, 3 * P + 4 : 3 * P + 8].rearrange("p (k e) -> p k e", k=2)]
+        factors = factors + [held([P, 2, 2], F32, f"factors{m}")[:] for m in range(1, PACK)]
+        shifts = {n: held([P, 2], F32, f"shifts{n}")[:] for n in (0, 1, 2, 3, 4, 6)}
+
+        def scores(target, stationary, stationary_scales, moving, moving_scales):
+            nc.tensor.matmul_mx(out=target, lhsT=stationary.bitcast(E4M3), lhsT_scale=stationary_scales,
+                                rhs=moving.bitcast(E4M3), rhs_scale=moving_scales, start=True, stop=True)
+
+        def direct_rows(t, bank):
+            scores(bank[:], qd_codes[FIRST][:, block(t)], qd_scales[FIRST][:, block(t)], all_k_codes[:], all_k_scales[:])
+            nc.vector.scalar_tensor_tensor(neg_z[t], bank[:], neg_us[:, t : t + 1], ts_slots[:], ALU.mult, ALU.mult)
+
+        def direct_maximum(t):
+            nc.vector.tensor_reduce(neg_max[t], neg_z[t], mybir.AxisListType.X, ALU.min)
+
+        def turned_scores(h, b, target):
+            rows = half(1) if h == FIRST else slice(0, R)
+            scores(target, all_k_codes[:, block(b)], all_k_scales[:, block(b)], qd_codes[h][:, rows], qd_scales[h][:, rows])
+
+        def scale_turned(h, b, target):
+            nc.scalar.activation(scaled[h][b], target, ACT.Copy, scale=ts_cols[:, b : b + 1])
+
+        def turned_rows(n, bank):
+            h, t = divmod(n, PACK)
+            for b in range(PACK):
+                nc.tensor.transpose(bank[:, block(b)], scaled[h][b][:, block(t - 2 * (1 - h))], ident[:])
+            nc.vector.tensor_scalar(neg_z[n], bank[:], neg_us[:, t : t + 1], None, ALU.mult, ALU.min, accum_out=neg_max[n])
+
+        def exponentials(n):
+            nc.scalar.activation(exps[n], neg_z[n], ACT.Exp, bias=neg_max[n], scale=-1.0, accum_out=totals[:, n : n + 1])
+
+        def make_inverses(m):
+            nc.vector.reciprocal(inverses[m], totals[:, 2 * m : 2 * m + 2])
+
+        def make_factors(m):
+            nc.vector.tensor_tensor(factors[m], numerators[:, :, 2 * m : 2 * m + 2],
+                                    inverses[m].unsqueeze(1).to_broadcast([P, 2, 2]), ALU.mult)
+
+        def make_products(n):
+            h, t = divmod(n, PACK)
+            nc.vector.scalar_tensor_tensor(products[n], exps[n], factors[n // 2][:, 0, n % 2 : n % 2 + 1],
+                                           dp_sb[h][:, t, :], ALU.mult, ALU.mult, accum_out=row_sums[:, n : n + 1])
+
+        def make_shifts(first, count):
+            nc.vector.tensor_tensor(shifts[first][:, :count], row_sums[:, first : first + count],
+                                    factors[first // 2][:, 1, first % 2 : first % 2 + count], ALU.mult)
+
+        def shift(n):
+            return shifts[n][:, 0:1] if n in shifts else shifts[n - 1][:, 1:2]
+
+        g_woven = {(FIRST, 0): held([P, HALF, PACK], BF16, "g_woven0_0")[:]}
+        means = [held([P, SLOTS], F32, f"means{t}")[:] for t in range(PACK - 1)]
+        final_means = [held([P, HALF], F32, f"final_means{a}")[:] for a in range(2)]
+        first_turned = held([P, 2 * R], BF16, "first_turned")
+        turned = [first_turned[:, b * R : (b + 1) * R].rearrange("i (u s e) -> i u s e", u=2, e=2) for b in range(2)]
+        turn_banks = (banks[2], banks[3], banks[4], banks[5])
+
+        def mean_term(t, columns, target):
+            nc.scalar.activation(target, exps[t][:, columns], ACT.Copy, scale=shift(t))
+
+        def turn_term(t, opens, blocks):
+            for b in blocks:
+                mean = means[t][:, block(b)] if t < PACK - 1 else final_means[b // 2][:, block(b % 2)]
+                term = products[t][:, block(b)] if opens else mean
+                nc.tensor.matmul(quarters(turn_banks[b])[:, t, :], term, ident[:],
+                                 start=opens and t == 0, stop=not opens and t == PACK - 1, is_transpose=True)
+
+        def round_turned(b):
+            nc.scalar.activation(turned[b], quarters(turn_banks[b]).rearrange("i (u e) s -> i u s e", e=2), ACT.Copy,
+                                 scale=ts_cols[:, b : b + 1])
+
+        def turn_back(a, bank):
+            for c in range(2):
+                words = turned[2 * a + c].rearrange("p a b c -> p (a b c)").bitcast(F32)
+                for u in range(2):
+                    nc.tensor.transpose(halves(bank)[:, u, block(c)], words[:, block(u)], ident[:])
+
+        def return_gradient(a, bank, copy):
+            target = g_woven[FIRST, a].rearrange("s i t -> s (i t)").bitcast(F32).rearrange("s (i u) -> s i u", u=2)
+            copy(target, halves(bank).rearrange("s u i -> s i u"))
+
+        def centre(t, columns, target):
+            n = PACK + t
+            nc.vector.scalar_tensor_tensor(target, exps[n][:, columns], shift(n), products[n][:, columns], ALU.mult, ALU.add)
+
+        def last_block_term(t, opens, bank, last_means):
+            n = PACK + t
+            term = products[n][:, block(PACK - 1)]
+            if not opens:
+                term = last_means[:, t, :]
+                nc.scalar.activation(term, exps[n][:, block(PACK - 1)], ACT.Copy, scale=shift(n))
+            nc.tensor.matmul(quarters(bank)[:, t, :], term, ident[:], start=opens and t == 0,
+                             stop=not opens and t == PACK - 1, is_transpose=True)
+
+        def last_block_round(bank, words):
+            nc.scalar.activation(words[:], quarters(bank).rearrange("i (u e) s -> i u s e", e=2), ACT.Copy,
+                                 scale=ts_cols[:, PACK - 1 : PACK])
+
+        def last_block_return(words, back):
+            for u in range(2):
+                nc.tensor.transpose(back[:, block(u)], words[:].rearrange("p a b c -> p (a b c)").bitcast(F32)[:, block(u)], ident[:])
+            target = g_woven[SECOND, 1][:, P:, :].rearrange("s i t -> s (i t)").bitcast(F32).rearrange("s (i u) -> s i u", u=2)
+            nc.scalar.copy(target, back.rearrange("s (u i) -> s i u", u=2))
+
+        def weave_centred(columns, source, target):
+            ts_lines = ts_slots[:, columns].rearrange("p (c i) -> p c i", i=LINE).unsqueeze(2)
+            nc.vector.tensor_tensor(target.rearrange("p (c i) t -> p c t i", i=LINE),
+                                    source.rearrange("p t (c i) -> p c t i", i=LINE),
+                                    ts_lines.to_broadcast([P, (columns.stop - columns.start) // LINE, PACK, LINE]), ALU.mult)
+
+        def quantise_gradient(h, a):
+            quantise(g_woven[h, a].rearrange("p i t -> p (i t)"), E5M2, g_codes[h][:, half(a)], g_scales[h][:, half(a)])
+
+        def key_gradient_pass(target, j, h, columns, opens):
+            nc.tensor.matmul_mx(out=target, lhsT=qr_codes[h][j // 2][:, block(j % 2)].bitcast(E4M3),
+                                lhsT_scale=qr_scales[h][j // 2][:, block(j % 2)],
+                                rhs=g_codes[h][:, columns].bitcast(E5M2), rhs_scale=g_scales[h][:, columns],
+                                start=opens, stop=not opens)
+
+        def sums(j, columns, target):
+            opener = FIRST if j == 0 else SECOND
+            for h in (opener, 1 - opener):
+                key_gradient_pass(target, j, h, columns, h == opener)
             return target
 
-        def vector_scatter(j, name, source, entries):
-            dk = held(list(source.shape), F32, name)
+        def vector_scatter(j, a, source):
+            dk = held([P, HALF], F32, f"dk{j}_{a}")
             nc.vector.tensor_copy(dk[:], source)
-            nc.vector.tensor_copy(windows[j][:].indirect(entries), dk[:])
+            nc.vector.tensor_copy(windows[j][:].indirect(half_lists[a]), dk[:])
 
         def scalar_scatter(j, a, source):
             dk = held([P, HALF], F32, f"dk{j}_{a}")
             nc.scalar.copy(dk[:], source)
             nc.scalar.activation(windows[j][:].indirect(half_lists[a]), dk[:], ACT.Copy)
 
-        scalar_scatter(0, 0, sums(0, half(0), banks[0]))
-        behind_gradient = held([P, PACK, HALF], F32, "behind_gradient", "first_gradient0")
-        centred.append([behind_gradient[:, t, :] for t in range(PACK)])
+        out_planes = out.rearrange("(p j) c -> j p c", j=PACK)
+        direct_rows(0, banks[0])
+        for b in range(PACK):
+            turned_scores(FIRST, b, banks[6 + b // 2][:, half(b % 2)])
+        for b in range(PACK):
+            scale_turned(FIRST, b, banks[6 + b // 2][:, half(b % 2)])
+        direct_rows(1, banks[1])
+        all_rounded = held([P, PACK, R], BF16, "rounded", "second_woven1")
+        rounded = [all_rounded[:, j, :] for j in range(PACK)]
+        for v in range(2):
+            nc.gpsimd.tensor_scalar(all_rounded[:, 2 * v : 2 * v + 2, :], q_raw[SECOND][:, 2 * v : 2 * v + 2, :], 1.0, 0.0,
+                                    ALU.mult, ALU.add)
+        for b in range(PACK):
+            turned_scores(SECOND, b, banks[2 + b][:])
+            scale_turned(SECOND, b, banks[2 + b][:])
+        for t in range(2):
+            direct_maximum(t)
+        for n, bank in zip(range(2, TILES), (banks[0], banks[1], banks[6], banks[7], banks[0], banks[1])):
+            turned_rows(n, bank)
+        for n in range(TILES):
+            exponentials(n)
+        turn_rounded_queries(rounded, 0, banks[6])
+        weave_turned_words(0, banks[6], nc.scalar.copy, None)
+        make_inverses(0)
+        make_factors(0)
+        make_inverses(1)
+        make_products(0)
+        make_factors(1)
+        make_products(1)
+        make_inverses(2)
+        make_shifts(0, 1)
+        make_products(2)
+        make_factors(2)
+        make_shifts(1, 1)
+        make_products(3)
+        make_inverses(3)
+        make_shifts(2, 1)
+        make_products(4)
+        make_shifts(3, 1)
+        make_factors(3)
+        turn_rounded_queries(rounded, 1, banks[0])
+        for t in range(PACK - 1):
+            mean_term(t, slice(0, SLOTS), means[t])
+        for a in range(2):
+            mean_term(PACK - 1, half(a), final_means[a])
+        early, late = range(2), range(2, PACK)
+        for t in range(2):
+            turn_term(t, True, range(PACK))
+        turn_term(2, True, early)
+        turn_term(0, False, early)
+        turn_term(2, True, late)
+        turn_term(3, True, early)
+        turn_term(1, False, early)
+        turn_term(0, False, late)
+        for t in range(2, PACK):
+            turn_term(t, False, early)
+        turn_term(3, True, late)
+        for t in range(1, PACK):
+            turn_term(t, False, late)
+        make_products(5)
+        make_products(6)
+        make_shifts(4, 2)
+        make_products(7)
+        for b in range(2):
+            round_turned(b)
+        centred = held([P, PACK, HALF], F32, "centred0")
+        centre(0, half(0), centred[:, 0, :])
+        make_shifts(6, 2)
+        turn_back(0, banks[7])
+        return_gradient(0, banks[7], nc.scalar.copy)
+        last_means = held([P, PACK, P], F32, "last_means", "final_means0")
+        for opens in (True, False):
+            for t in range(PACK):
+                last_block_term(t, opens, banks[6], last_means)
+        behind_return = held([P, 4 * R], BF16, "behind_return", "first_turned")
+        for b in range(2, PACK):
+            turned.append(behind_return[:, (b - 2) * R : (b - 1) * R].rearrange("i (u s e) -> i u s e", u=2, e=2))
+            round_turned(b)
+        g_woven[SECOND, 1] = held([P, HALF, PACK], BF16, "g_woven1_1")[:]
+        g_woven[FIRST, 1] = held([P, HALF, PACK], BF16, "g_woven0_1")[:]
+        turn_back(1, banks[2])
+        last_turned = held([P, 2, P, 2], BF16, "last_turned")
+        last_block_round(banks[6], last_turned)
+        return_gradient(1, banks[2], nc.scalar.copy)
+        last_block_return(last_turned, banks[4][:, half(0)])
+        for t in range(1, PACK):
+            centre(t, half(0), centred[:, t, :])
+        g_woven[SECOND, 0] = behind_return[:, 2 * R :].rearrange("s (i t) -> s i t", t=PACK)
+        weave_centred(half(0), centred[:], g_woven[SECOND, 0])
+        quantise_queries_along_r(SECOND, 0)
+        quantise_gradient(FIRST, 0)
+        quantise_gradient(SECOND, 0)
+        scalar_scatter(0, 0, sums(0, half(0), banks[1][:, half(0)]))
+        centred = held([P, PACK, P], F32, "centred1", "g_woven0_0")
         for t in range(PACK):
-            centre(t, 1)
-        scalar_scatter(1, 0, sums(1, half(0), banks[1]))
-        weave_centred(1, behind_gradient[:])
+            centre(t, block(2), centred[:, t, :])
+        scalar_scatter(1, 0, sums(1, half(0), banks[1][:, half(1)]))
         quantise_gradient(FIRST, 1)
+        key_gradient_pass(banks[3][:, half(0)], 0, FIRST, half(1), True)
+        weave_centred(block(2), centred[:], g_woven[SECOND, 1][:, :P, :])
         quantise_gradient(SECOND, 1)
-        vector_scatter(0, "dk0_1", sums(0, half(1), banks[2]), half_lists[1])
+        key_gradient_pass(banks[3][:, half(0)], 0, SECOND, half(1), False)
+        weave_turned_words(1, banks[0], nc.vector.tensor_copy, "g_woven0_1")
+        last_sums = held([P, HALF], F32, "dk0_1")
+        nc.vector.tensor_copy(last_sums[:], banks[3][:, half(0)])
+        quantise_queries_along_r(SECOND, 1)
+        nc.vector.tensor_copy(windows[0][:].indirect(half_lists[1]), last_sums[:])
         nc.sync.dma_start(out_planes[0], windows[0][:])
-        scalar_scatter(1, 1, sums(1, half(1), banks[2], HALF))
+        scalar_scatter(1, 1, sums(1, half(1), banks[4][:, half(0)]))
         nc.sync.dma_start(out_planes[1], windows[1][:])
-        vector_scatter(2, "dk2", sums(2, slice(0, SLOTS), banks[6]), offsets[:])
+        vector_scatter(2, 1, sums(2, half(1), banks[5][:, half(0)]))
+        vector_scatter(2, 0, sums(2, half(0), banks[3][:, half(1)]))
         nc.sync.dma_start(out_planes[2], windows[2][:])
-        last = sums(3, slice(0, SLOTS), banks[7])
+        last = sums(3, slice(0, SLOTS), banks[4][:])
         for a in range(2):
             scalar_scatter(3, a, last[:, half(a)])
         nc.sync.dma_start(out_planes[3], windows[3][:])

@@ -76,8 +76,6 @@ def tile_attend_ggqa_sm_k_kernel(tc, q1, q2, kT, dp1, dp2, us, ts, w1, w2, offs,
         for h, w in enumerate((w1, w2)):
             nc.scalar.dma_start(w_sb[h][:], w.rearrange("(s t) o -> s (t o)", t=PACK))
 
-        g_codes = [held([P, SLOTS], U32, f"g_codes{h}") for h in range(HEADS)]
-        g_scales = [held([P, SLOTS], U8, f"g_scales{h}") for h in range(HEADS)]
 
         windows = {}
 
@@ -214,10 +212,10 @@ def tile_attend_ggqa_sm_k_kernel(tc, q1, q2, kT, dp1, dp2, us, ts, w1, w2, offs,
                   [second_scaled[:, b * R : (b + 1) * R] for b in range(PACK)]]
         products = [held([P, SLOTS], F32, f"products{n}")[:] for n in range(TILES)]
         totals = held([P, TILES], F32, "totals")
-        row_sums = held([P, TILES], F32, "row_sums")
         last_scaled = scaled[SECOND][PACK - 1]
-        inverses = [last_scaled[:, 2 * P : 2 * P + 2], last_scaled[:, 3 * P : 3 * P + 2], dp_sb[FIRST][:, 0, 0:2], dp_sb[FIRST][:, 2, 0:2]]
-        factors = [last_scaled[:, 3 * P + 4 : 3 * P + 8].rearrange("p (k e) -> p k e", k=2)]
+        row_sums = last_scaled[:, 3 * P + 8 : 3 * P + 8 + TILES]
+        inverses = [last_scaled[:, P : P + 2], last_scaled[:, 3 * P : 3 * P + 2], dp_sb[FIRST][:, 0, 0:2], dp_sb[FIRST][:, 2, 0:2]]
+        factors = [last_scaled[:, 2 * P : 2 * P + 4].rearrange("p (k e) -> p k e", k=2)]
         factors = factors + [held([P, 2, 2], F32, f"factors{m}")[:] for m in range(1, PACK)]
         shifts = {n: held([P, 2], F32, f"shifts{n}")[:] for n in (0, 1, 2, 3, 4, 6)}
 
@@ -319,7 +317,7 @@ def tile_attend_ggqa_sm_k_kernel(tc, q1, q2, kT, dp1, dp2, us, ts, w1, w2, offs,
             for u in range(2):
                 nc.tensor.transpose(back[:, block(u)], words[:].rearrange("p a b c -> p (a b c)").bitcast(F32)[:, block(u)], ident[:])
             target = g_woven[SECOND, 1][:, P:, :].rearrange("s i t -> s (i t)").bitcast(F32).rearrange("s (i u) -> s i u", u=2)
-            nc.scalar.copy(target, back.rearrange("s (u i) -> s i u", u=2))
+            nc.vector.tensor_copy(target, back.rearrange("s (u i) -> s i u", u=2))
 
         def weave_centred(columns, source, target):
             ts_lines = ts_slots[:, columns].rearrange("p (c i) -> p c i", i=LINE).unsqueeze(2)
@@ -327,19 +325,23 @@ def tile_attend_ggqa_sm_k_kernel(tc, q1, q2, kT, dp1, dp2, us, ts, w1, w2, offs,
                                     source.rearrange("p t (c i) -> p c t i", i=LINE),
                                     ts_lines.to_broadcast([P, (columns.stop - columns.start) // LINE, PACK, LINE]), ALU.mult)
 
-        def quantise_gradient(h, a):
-            quantise(g_woven[h, a].rearrange("p i t -> p (i t)"), E5M2, g_codes[h][:, half(a)], g_scales[h][:, half(a)])
+        g_codes, g_scales = {}, {}
 
-        def key_gradient_pass(target, j, h, columns, opens):
+        def quantise_gradient(h, a, tag=None):
+            g_codes[h, a] = held([P, HALF], U32, f"g_codes{h}_{a}", tag)[:]
+            g_scales[h, a] = held([P, HALF], U8, f"g_scales{h}_{a}")[:]
+            quantise(g_woven[h, a].rearrange("p i t -> p (i t)"), E5M2, g_codes[h, a], g_scales[h, a])
+
+        def key_gradient_pass(target, j, h, a, opens):
             nc.tensor.matmul_mx(out=target, lhsT=qr_codes[h][j // 2][:, block(j % 2)].bitcast(E4M3),
                                 lhsT_scale=qr_scales[h][j // 2][:, block(j % 2)],
-                                rhs=g_codes[h][:, columns].bitcast(E5M2), rhs_scale=g_scales[h][:, columns],
+                                rhs=g_codes[h, a].bitcast(E5M2), rhs_scale=g_scales[h, a],
                                 start=opens, stop=not opens)
 
-        def sums(j, columns, target):
+        def sums(j, a, target):
             opener = FIRST if j == 0 else SECOND
             for h in (opener, 1 - opener):
-                key_gradient_pass(target, j, h, columns, h == opener)
+                key_gradient_pass(target, j, h, a, h == opener)
             return target
 
         def vector_scatter(j, a, source):
@@ -436,7 +438,6 @@ def tile_attend_ggqa_sm_k_kernel(tc, q1, q2, kT, dp1, dp2, us, ts, w1, w2, offs,
         last_turned = held([P, 2, P, 2], BF16, "last_turned")
         last_block_round(banks[6], last_turned)
         return_gradient(1, banks[2], nc.scalar.copy)
-        last_block_return(last_turned, banks[4][:, half(0)])
         for t in range(1, PACK):
             centre(t, half(0), centred[:, t, :])
         g_woven[SECOND, 0] = behind_return[:, 2 * R :].rearrange("s (i t) -> s i t", t=PACK)
@@ -444,28 +445,25 @@ def tile_attend_ggqa_sm_k_kernel(tc, q1, q2, kT, dp1, dp2, us, ts, w1, w2, offs,
         quantise_queries_along_r(SECOND, 0)
         quantise_gradient(FIRST, 0)
         quantise_gradient(SECOND, 0)
-        scalar_scatter(0, 0, sums(0, half(0), banks[1][:, half(0)]))
+        scalar_scatter(0, 0, sums(0, 0, banks[1][:, half(0)]))
         centred = held([P, PACK, P], F32, "centred1", "g_woven0_0")
         for t in range(PACK):
             centre(t, block(2), centred[:, t, :])
-        scalar_scatter(1, 0, sums(1, half(0), banks[1][:, half(1)]))
-        quantise_gradient(FIRST, 1)
-        key_gradient_pass(banks[3][:, half(0)], 0, FIRST, half(1), True)
+        scalar_scatter(1, 0, sums(1, 0, banks[1][:, half(1)]))
         weave_centred(block(2), centred[:], g_woven[SECOND, 1][:, :P, :])
+        last_block_return(last_turned, banks[4][:, half(0)])
+        quantise_gradient(FIRST, 1, "last_turned")
+        key_gradient_pass(banks[3][:, half(0)], 0, FIRST, 1, True)
         quantise_gradient(SECOND, 1)
-        key_gradient_pass(banks[3][:, half(0)], 0, SECOND, half(1), False)
-        weave_turned_words(1, banks[0], nc.vector.tensor_copy, "g_woven0_1")
+        key_gradient_pass(banks[3][:, half(0)], 0, SECOND, 1, False)
+        weave_turned_words(1, banks[0], nc.vector.tensor_copy, "g_woven1_1")
         last_sums = held([P, HALF], F32, "dk0_1")
         nc.vector.tensor_copy(last_sums[:], banks[3][:, half(0)])
         quantise_queries_along_r(SECOND, 1)
         nc.vector.tensor_copy(windows[0][:].indirect(half_lists[1]), last_sums[:])
         nc.sync.dma_start(out_planes[0], windows[0][:])
-        scalar_scatter(1, 1, sums(1, half(1), banks[4][:, half(0)]))
-        nc.sync.dma_start(out_planes[1], windows[1][:])
-        vector_scatter(2, 1, sums(2, half(1), banks[5][:, half(0)]))
-        vector_scatter(2, 0, sums(2, half(0), banks[3][:, half(1)]))
-        nc.sync.dma_start(out_planes[2], windows[2][:])
-        last = sums(3, slice(0, SLOTS), banks[4][:])
-        for a in range(2):
-            scalar_scatter(3, a, last[:, half(a)])
-        nc.sync.dma_start(out_planes[3], windows[3][:])
+        for j in range(2, PACK):
+            scalar_scatter(j, 0, sums(j, 0, banks[5 + j % 2][:, half(0)]))
+        for j in range(1, PACK):
+            vector_scatter(j, 1, sums(j, 1, (banks[3][:, half(1)], banks[4][:, half(0)], banks[7][:, half(0)])[j - 1]))
+            nc.sync.dma_start(out_planes[j], windows[j][:])

@@ -445,11 +445,13 @@ def tile_attend_ggqa_sm_k_kernel(tc, q1, q2, kT, dp1, dp2, us, ts, w1, w2, offs,
         quantise_queries_along_r(SECOND, 0)
         quantise_gradient(FIRST, 0)
         quantise_gradient(SECOND, 0)
-        scalar_scatter(0, 0, sums(0, 0, banks[1][:, half(0)]))
+        early_sums = [held([P, HALF], F32, f"dk{j}_0") for j in range(2)]
+        for j in range(2):
+            nc.scalar.copy(early_sums[j][:], sums(j, 0, banks[1][:, half(j)]))
+            nc.scalar.activation(windows[j][:].indirect(half_lists[0]), early_sums[j][:], ACT.Copy)
         centred = held([P, PACK, P], F32, "centred1", "g_woven0_0")
         for t in range(PACK):
             centre(t, block(2), centred[:, t, :])
-        scalar_scatter(1, 0, sums(1, 0, banks[1][:, half(1)]))
         weave_centred(block(2), centred[:], g_woven[SECOND, 1][:, :P, :])
         last_block_return(last_turned, banks[4][:, half(0)])
         quantise_gradient(FIRST, 1, "last_turned")
@@ -457,13 +459,15 @@ def tile_attend_ggqa_sm_k_kernel(tc, q1, q2, kT, dp1, dp2, us, ts, w1, w2, offs,
         quantise_gradient(SECOND, 1)
         key_gradient_pass(banks[3][:, half(0)], 0, SECOND, 1, False)
         weave_turned_words(1, banks[0], nc.vector.tensor_copy, "g_woven1_1")
-        last_sums = held([P, HALF], F32, "dk0_1")
-        nc.vector.tensor_copy(last_sums[:], banks[3][:, half(0)])
+        late_sums = [held([P, HALF], F32, f"dk{j}_1") for j in range(2)]
+        nc.vector.tensor_copy(late_sums[0][:], banks[3][:, half(0)])
         quantise_queries_along_r(SECOND, 1)
-        nc.vector.tensor_copy(windows[0][:].indirect(half_lists[1]), last_sums[:])
-        nc.sync.dma_start(out_planes[0], windows[0][:])
+        nc.vector.tensor_copy(late_sums[1][:], sums(1, 1, banks[5][:, half(0)]))
+        for j in range(2):
+            nc.vector.tensor_copy(windows[j][:].indirect(half_lists[1]), late_sums[j][:])
+            nc.sync.dma_start(out_planes[j], windows[j][:])
         for j in range(2, PACK):
-            scalar_scatter(j, 0, sums(j, 0, banks[5 + j % 2][:, half(0)]))
-        for j in range(1, PACK):
-            vector_scatter(j, 1, sums(j, 1, (banks[3][:, half(1)], banks[4][:, half(0)], banks[7][:, half(0)])[j - 1]))
+            scalar_scatter(j, 0, sums(j, 0, banks[(1, 6)[j - 2]][:, half(0)]))
+        for j in range(2, PACK):
+            vector_scatter(j, 1, sums(j, 1, banks[(4, 7)[j - 2]][:, half(0)]))
             nc.sync.dma_start(out_planes[j], windows[j][:])

@@ -135,8 +135,8 @@ def tile_attend_ggqa_sm_k_kernel(tc, q1, q2, kT, dp1, dp2, us, ts, w1, w2, offs,
                 for u in range(2):
                     nc.tensor.transpose(quarters(bank)[:, 2 * e + u, :], words[:, u::2], ident[:])
 
-        def weave_turned_words(v, bank, copy, tag):
-            qr_woven[SECOND, v] = held([P, 2 * P * PACK], BF16, f"second_qr_woven{v}", tag)[:]
+        def weave_turned_words(v, bank, copy, target):
+            qr_woven[SECOND, v] = target
             copy(qr_woven[SECOND, v].bitcast(F32).rearrange("s (e p u) -> s e p u", e=2, u=2),
                            bank[:].rearrange("s (e u p) -> s e p u", e=2, u=2))
 
@@ -205,7 +205,8 @@ def tile_attend_ggqa_sm_k_kernel(tc, q1, q2, kT, dp1, dp2, us, ts, w1, w2, offs,
         behind_weave = held([P, 4 * SLOTS], F32, "behind_weave", "second_woven0")
         neg_z = [behind_weave[:, t * SLOTS : (t + 1) * SLOTS] for t in range(2)]
         neg_z = neg_z + [held([P, SLOTS], F32, f"neg_z{n}")[:] for n in range(2, TILES)]
-        exps = [held([P, SLOTS], F32, f"e{n}")[:] for n in range(TILES)]
+        fourth = held([P, HALF + SLOTS], F32, "fourth")
+        exps = [fourth[:, HALF:] if n == PACK - 1 else held([P, SLOTS], F32, f"e{n}")[:] for n in range(TILES)]
         neg_max = [held([P, 1], F32, f"neg_max{n}")[:] for n in range(TILES)]
         second_scaled = held([P, PACK * R], F32, "second_scaled")
         scaled = [[behind_weave[:, 2 * SLOTS + b * HALF : 2 * SLOTS + (b + 1) * HALF] for b in range(PACK)],
@@ -213,11 +214,18 @@ def tile_attend_ggqa_sm_k_kernel(tc, q1, q2, kT, dp1, dp2, us, ts, w1, w2, offs,
         products = [held([P, SLOTS], F32, f"products{n}")[:] for n in range(TILES)]
         totals = held([P, TILES], F32, "totals")
         last_scaled = scaled[SECOND][PACK - 1]
-        row_sums = last_scaled[:, 3 * P + 8 : 3 * P + 8 + TILES]
-        inverses = [last_scaled[:, P : P + 2], last_scaled[:, 3 * P : 3 * P + 2], dp_sb[FIRST][:, 0, 0:2], dp_sb[FIRST][:, 2, 0:2]]
-        factors = [last_scaled[:, 2 * P : 2 * P + 4].rearrange("p (k e) -> p k e", k=2)]
-        factors = factors + [held([P, 2, 2], F32, f"factors{m}")[:] for m in range(1, PACK)]
-        shifts = {n: held([P, 2], F32, f"shifts{n}")[:] for n in (0, 1, 2, 3, 4, 6)}
+        early_row_sums = held([P, 2], F32, "early_row_sums")
+        late_row_sums = last_scaled[:, 3 * P + 8 : 3 * P + 8 + TILES]
+
+        def row_sums(first, count):
+            return (early_row_sums if first < 2 else late_row_sums)[:, first : first + count]
+
+        inverses = [last_scaled[:, 0:2], last_scaled[:, 2 * P : 2 * P + 2], last_scaled[:, 3 * P : 3 * P + 2], dp_sb[FIRST][:, 2, 0:2]]
+        factors = [last_scaled[:, P : P + 4].rearrange("p (k e) -> p k e", k=2)]
+        factors.append(last_scaled[:, 3 * P + 4 : 3 * P + 8].rearrange("p (k e) -> p k e", k=2))
+        factors = factors + [held([P, 2, 2], F32, f"factors{m}")[:] for m in range(2, PACK)]
+        shifts = {n: held([P, 2], F32, f"shifts{n}")[:] for n in (0, 2, 3, 4, 6)}
+        shifts[1] = last_scaled[:, 2 * P + 4 : 2 * P + 6]
 
         def scores(target, stationary, stationary_scales, moving, moving_scales):
             nc.tensor.matmul_mx(out=target, lhsT=stationary.bitcast(E4M3), lhsT_scale=stationary_scales,
@@ -230,12 +238,12 @@ def tile_attend_ggqa_sm_k_kernel(tc, q1, q2, kT, dp1, dp2, us, ts, w1, w2, offs,
         def direct_maximum(t):
             nc.vector.tensor_reduce(neg_max[t], neg_z[t], mybir.AxisListType.X, ALU.min)
 
-        def turned_scores(h, b, target):
-            rows = half(1) if h == FIRST else slice(0, R)
+        def turned_scores(h, u, b, target):
+            rows = half(u)
             scores(target, all_k_codes[:, block(b)], all_k_scales[:, block(b)], qd_codes[h][:, rows], qd_scales[h][:, rows])
 
-        def scale_turned(h, b, target):
-            nc.scalar.activation(scaled[h][b], target, ACT.Copy, scale=ts_cols[:, b : b + 1])
+        def scale_turned(h, u, b, target):
+            nc.scalar.activation(scaled[h][b] if h == FIRST else scaled[h][b][:, half(u)], target, ACT.Copy, scale=ts_cols[:, b : b + 1])
 
         def turned_rows(n, bank):
             h, t = divmod(n, PACK)
@@ -256,10 +264,10 @@ def tile_attend_ggqa_sm_k_kernel(tc, q1, q2, kT, dp1, dp2, us, ts, w1, w2, offs,
         def make_products(n):
             h, t = divmod(n, PACK)
             nc.vector.scalar_tensor_tensor(products[n], exps[n], factors[n // 2][:, 0, n % 2 : n % 2 + 1],
-                                           dp_sb[h][:, t, :], ALU.mult, ALU.mult, accum_out=row_sums[:, n : n + 1])
+                                           dp_sb[h][:, t, :], ALU.mult, ALU.mult, accum_out=row_sums(n, 1))
 
         def make_shifts(first, count):
-            nc.vector.tensor_tensor(shifts[first][:, :count], row_sums[:, first : first + count],
+            nc.vector.tensor_tensor(shifts[first][:, :count], row_sums(first, count),
                                     factors[first // 2][:, 1, first % 2 : first % 2 + count], ALU.mult)
 
         def shift(n):
@@ -270,7 +278,7 @@ def tile_attend_ggqa_sm_k_kernel(tc, q1, q2, kT, dp1, dp2, us, ts, w1, w2, offs,
         final_means = [held([P, HALF], F32, f"final_means{a}")[:] for a in range(2)]
         first_turned = held([P, 2 * R], BF16, "first_turned")
         turned = [first_turned[:, b * R : (b + 1) * R].rearrange("i (u s e) -> i u s e", u=2, e=2) for b in range(2)]
-        turn_banks = (banks[2], banks[3], banks[4], banks[5])
+        turn_banks = banks[4:8]
 
         def mean_term(t, columns, target):
             nc.scalar.activation(target, exps[t][:, columns], ACT.Copy, scale=shift(t))
@@ -355,63 +363,71 @@ def tile_attend_ggqa_sm_k_kernel(tc, q1, q2, kT, dp1, dp2, us, ts, w1, w2, offs,
             nc.scalar.activation(windows[j][:].indirect(half_lists[a]), dk[:], ACT.Copy)
 
         out_planes = out.rearrange("(p j) c -> j p c", j=PACK)
+        def turned_pair(h, u, pair):
+            for b in range(PACK):
+                turned_scores(h, u, b, pair[b // 2][:, half(b % 2)])
+            for b in range(PACK):
+                scale_turned(h, u, b, pair[b // 2][:, half(b % 2)])
+
         direct_rows(0, banks[0])
-        for b in range(PACK):
-            turned_scores(FIRST, b, banks[6 + b // 2][:, half(b % 2)])
-        for b in range(PACK):
-            scale_turned(FIRST, b, banks[6 + b // 2][:, half(b % 2)])
+        turned_pair(FIRST, 1, banks[6:8])
         direct_rows(1, banks[1])
         all_rounded = held([P, PACK, R], BF16, "rounded", "second_woven1")
         rounded = [all_rounded[:, j, :] for j in range(PACK)]
         for v in range(2):
             nc.gpsimd.tensor_scalar(all_rounded[:, 2 * v : 2 * v + 2, :], q_raw[SECOND][:, 2 * v : 2 * v + 2, :], 1.0, 0.0,
                                     ALU.mult, ALU.add)
-        for b in range(PACK):
-            turned_scores(SECOND, b, banks[2 + b][:])
-            scale_turned(SECOND, b, banks[2 + b][:])
+        turned_pair(SECOND, 0, banks[2:4])
         for t in range(2):
             direct_maximum(t)
-        for n, bank in zip(range(2, TILES), (banks[0], banks[1], banks[6], banks[7], banks[0], banks[1])):
-            turned_rows(n, bank)
-        for n in range(TILES):
+        for n in range(2, PACK):
+            turned_rows(n, banks[n - 2])
+        for n in range(2):
             exponentials(n)
-        turn_rounded_queries(rounded, 0, banks[6])
-        weave_turned_words(0, banks[6], nc.scalar.copy, None)
+        turned_pair(SECOND, 1, banks[6:8])
+        turned_rows(4, banks[4])
         make_inverses(0)
+        turned_rows(5, banks[5])
+        for v in range(2):
+            turn_rounded_queries(rounded, v, banks[2 + v])
         make_factors(0)
-        make_inverses(1)
         make_products(0)
-        make_factors(1)
         make_products(1)
-        make_inverses(2)
+        turned_rows(6, banks[0])
         make_shifts(0, 1)
+        exponentials(2)
+        exponentials(3)
+        make_inverses(1)
+        turned_rows(7, banks[1])
+        make_factors(1)
+        make_shifts(1, 1)
+        for n in range(PACK, TILES):
+            exponentials(n)
+        make_inverses(2)
         make_products(2)
         make_factors(2)
-        make_shifts(1, 1)
         make_products(3)
         make_inverses(3)
         make_shifts(2, 1)
         make_products(4)
         make_shifts(3, 1)
         make_factors(3)
-        turn_rounded_queries(rounded, 1, banks[0])
         for t in range(PACK - 1):
             mean_term(t, slice(0, SLOTS), means[t])
         for a in range(2):
             mean_term(PACK - 1, half(a), final_means[a])
+        weave_turned_words(0, banks[2], nc.scalar.copy, fourth[:, :SLOTS].bitcast(BF16))
         early, late = range(2), range(2, PACK)
-        for t in range(2):
-            turn_term(t, True, range(PACK))
-        turn_term(2, True, early)
-        turn_term(0, False, early)
+        for opens in (True, False):
+            for t in range(2):
+                turn_term(t, opens, range(PACK))
+        for t in range(2, PACK):
+            turn_term(t, True, early)
         turn_term(2, True, late)
-        turn_term(3, True, early)
-        turn_term(1, False, early)
-        turn_term(0, False, late)
         for t in range(2, PACK):
             turn_term(t, False, early)
         turn_term(3, True, late)
-        for t in range(1, PACK):
+        for t in range(2, PACK):
             turn_term(t, False, late)
         make_products(5)
         make_products(6)
@@ -422,22 +438,22 @@ def tile_attend_ggqa_sm_k_kernel(tc, q1, q2, kT, dp1, dp2, us, ts, w1, w2, offs,
         centred = held([P, PACK, HALF], F32, "centred0")
         centre(0, half(0), centred[:, 0, :])
         make_shifts(6, 2)
-        turn_back(0, banks[7])
-        return_gradient(0, banks[7], nc.scalar.copy)
+        turn_back(0, banks[0])
+        return_gradient(0, banks[0], nc.scalar.copy)
         last_means = held([P, PACK, P], F32, "last_means", "final_means0")
         for opens in (True, False):
             for t in range(PACK):
-                last_block_term(t, opens, banks[6], last_means)
+                last_block_term(t, opens, banks[2], last_means)
         behind_return = held([P, 4 * R], BF16, "behind_return", "first_turned")
         for b in range(2, PACK):
             turned.append(behind_return[:, (b - 2) * R : (b - 1) * R].rearrange("i (u s e) -> i u s e", u=2, e=2))
             round_turned(b)
         g_woven[SECOND, 1] = held([P, HALF, PACK], BF16, "g_woven1_1")[:]
         g_woven[FIRST, 1] = held([P, HALF, PACK], BF16, "g_woven0_1")[:]
-        turn_back(1, banks[2])
+        turn_back(1, banks[1])
         last_turned = held([P, 2, P, 2], BF16, "last_turned")
-        last_block_round(banks[6], last_turned)
-        return_gradient(1, banks[2], nc.scalar.copy)
+        last_block_round(banks[2], last_turned)
+        return_gradient(1, banks[1], nc.scalar.copy)
         for t in range(1, PACK):
             centre(t, half(0), centred[:, t, :])
         g_woven[SECOND, 0] = behind_return[:, 2 * R :].rearrange("s (i t) -> s i t", t=PACK)
@@ -447,27 +463,28 @@ def tile_attend_ggqa_sm_k_kernel(tc, q1, q2, kT, dp1, dp2, us, ts, w1, w2, offs,
         quantise_gradient(SECOND, 0)
         early_sums = [held([P, HALF], F32, f"dk{j}_0") for j in range(2)]
         for j in range(2):
-            nc.scalar.copy(early_sums[j][:], sums(j, 0, banks[1][:, half(j)]))
+            nc.scalar.copy(early_sums[j][:], sums(j, 0, banks[4][:, half(j)]))
             nc.scalar.activation(windows[j][:].indirect(half_lists[0]), early_sums[j][:], ACT.Copy)
         centred = held([P, PACK, P], F32, "centred1", "g_woven0_0")
         for t in range(PACK):
             centre(t, block(2), centred[:, t, :])
         weave_centred(block(2), centred[:], g_woven[SECOND, 1][:, :P, :])
-        last_block_return(last_turned, banks[4][:, half(0)])
+        last_block_return(last_turned, banks[5][:, half(0)])
         quantise_gradient(FIRST, 1, "last_turned")
-        key_gradient_pass(banks[3][:, half(0)], 0, FIRST, 1, True)
+        key_gradient_pass(banks[6][:, half(0)], 0, FIRST, 1, True)
         quantise_gradient(SECOND, 1)
-        key_gradient_pass(banks[3][:, half(0)], 0, SECOND, 1, False)
-        weave_turned_words(1, banks[0], nc.vector.tensor_copy, "g_woven1_1")
+        key_gradient_pass(banks[6][:, half(0)], 0, SECOND, 1, False)
+        weave_turned_words(1, banks[3], nc.vector.tensor_copy,
+                           held([P, 2 * P * PACK], BF16, "second_qr_woven1", "g_woven1_1")[:])
         late_sums = [held([P, HALF], F32, f"dk{j}_1") for j in range(2)]
-        nc.vector.tensor_copy(late_sums[0][:], banks[3][:, half(0)])
+        nc.vector.tensor_copy(late_sums[0][:], banks[6][:, half(0)])
         quantise_queries_along_r(SECOND, 1)
-        nc.vector.tensor_copy(late_sums[1][:], sums(1, 1, banks[5][:, half(0)]))
+        nc.vector.tensor_copy(late_sums[1][:], sums(1, 1, banks[7][:, half(0)]))
         for j in range(2):
             nc.vector.tensor_copy(windows[j][:].indirect(half_lists[1]), late_sums[j][:])
             nc.sync.dma_start(out_planes[j], windows[j][:])
         for j in range(2, PACK):
-            scalar_scatter(j, 0, sums(j, 0, banks[(1, 6)[j - 2]][:, half(0)]))
+            scalar_scatter(j, 0, sums(j, 0, banks[(4, 2)[j - 2]][:, half(0)]))
         for j in range(2, PACK):
-            vector_scatter(j, 1, sums(j, 1, banks[(4, 7)[j - 2]][:, half(0)]))
+            vector_scatter(j, 1, sums(j, 1, banks[j - 2][:, half(0)]))
             nc.sync.dma_start(out_planes[j], windows[j][:])

@@ -109,7 +109,7 @@ def tile_attend_ggqa_sm_k_kernel(tc, q1, q2, kT, dp1, dp2, us, ts, w1, w2, offs,
         qd_scales = [held([P, R], U8, f"qd_scales{h}") for h in range(HEADS)]
         qr_woven = {(FIRST, v): held([P, 2 * P * PACK], BF16, f"qr_woven{v}")[:] for v in range(2)}
         qr_codes = [[held([P, 2 * P], U32, "qr_codes0_0")[:]],
-                    [held([P, 2 * P], U32, f"qr_codes1_{v}")[:] for v in range(2)]]
+                    [held([P, 2 * P], U32, "qr_codes1_0")[:]]]
         qr_scales = [[held([P, 2 * P], U8, f"qr_scales{h}_{v}") for v in range(2)] for h in range(HEADS)]
 
         def weave_queries(h, u, copy, rows=slice(0, P)):
@@ -214,15 +214,15 @@ def tile_attend_ggqa_sm_k_kernel(tc, q1, q2, kT, dp1, dp2, us, ts, w1, w2, offs,
         products = [held([P, SLOTS], F32, f"products{n}")[:] for n in range(TILES)]
         totals = held([P, TILES], F32, "totals")
         last_scaled = scaled[SECOND][PACK - 1]
-        early_row_sums = held([P, 2], F32, "early_row_sums")
+        early_row_sums = last_scaled[:, P : P + 2]
         late_row_sums = last_scaled[:, 3 * P + 8 : 3 * P + 8 + TILES]
 
         def row_sums(first, count):
             return (early_row_sums if first < 2 else late_row_sums)[:, first : first + count]
 
-        inverses = [last_scaled[:, 0:2], last_scaled[:, 2 * P : 2 * P + 2], last_scaled[:, 3 * P : 3 * P + 2], dp_sb[FIRST][:, 2, 0:2]]
-        factors = [last_scaled[:, P : P + 4].rearrange("p (k e) -> p k e", k=2)]
-        factors.append(last_scaled[:, 3 * P + 4 : 3 * P + 8].rearrange("p (k e) -> p k e", k=2))
+        inverses = [scaled[FIRST][PACK - 1][:, P : P + 2], dp_sb[FIRST][:, 0, 0:2], last_scaled[:, 3 * P : 3 * P + 2], dp_sb[FIRST][:, 2, 0:2]]
+        factors = [last_scaled[:, 0:4].rearrange("p (k e) -> p k e", k=2)]
+        factors.append(last_scaled[:, 2 * P : 2 * P + 4].rearrange("p (k e) -> p k e", k=2))
         factors = factors + [held([P, 2, 2], F32, f"factors{m}")[:] for m in range(2, PACK)]
         shifts = {n: held([P, 2], F32, f"shifts{n}")[:] for n in (0, 2, 3, 4, 6)}
         shifts[1] = last_scaled[:, 2 * P + 4 : 2 * P + 6]
@@ -385,22 +385,22 @@ def tile_attend_ggqa_sm_k_kernel(tc, q1, q2, kT, dp1, dp2, us, ts, w1, w2, offs,
         for n in range(2):
             exponentials(n)
         turned_pair(SECOND, 1, banks[6:8])
-        turned_rows(4, banks[4])
         make_inverses(0)
+        turned_rows(4, banks[4])
+        make_factors(0)
         turned_rows(5, banks[5])
         for v in range(2):
             turn_rounded_queries(rounded, v, banks[2 + v])
-        make_factors(0)
-        make_products(0)
-        make_products(1)
-        turned_rows(6, banks[0])
-        make_shifts(0, 1)
         exponentials(2)
         exponentials(3)
+        make_products(0)
+        make_products(1)
         make_inverses(1)
-        turned_rows(7, banks[1])
+        make_shifts(0, 1)
+        turned_rows(6, banks[0])
         make_factors(1)
         make_shifts(1, 1)
+        turned_rows(7, banks[1])
         for n in range(PACK, TILES):
             exponentials(n)
         make_inverses(2)
@@ -435,8 +435,9 @@ def tile_attend_ggqa_sm_k_kernel(tc, q1, q2, kT, dp1, dp2, us, ts, w1, w2, offs,
         make_products(7)
         for b in range(2):
             round_turned(b)
-        centred = held([P, PACK, HALF], F32, "centred0")
-        centre(0, half(0), centred[:, 0, :])
+        direct = slice(0, HALF + P)
+        centred = held([P, PACK, HALF + P], F32, "centred")
+        centre(0, direct, centred[:, 0, :])
         make_shifts(6, 2)
         turn_back(0, banks[0])
         return_gradient(0, banks[0], nc.scalar.copy)
@@ -448,16 +449,15 @@ def tile_attend_ggqa_sm_k_kernel(tc, q1, q2, kT, dp1, dp2, us, ts, w1, w2, offs,
         for b in range(2, PACK):
             turned.append(behind_return[:, (b - 2) * R : (b - 1) * R].rearrange("i (u s e) -> i u s e", u=2, e=2))
             round_turned(b)
-        g_woven[SECOND, 1] = held([P, HALF, PACK], BF16, "g_woven1_1")[:]
         g_woven[FIRST, 1] = held([P, HALF, PACK], BF16, "g_woven0_1")[:]
         turn_back(1, banks[1])
         last_turned = held([P, 2, P, 2], BF16, "last_turned")
         last_block_round(banks[2], last_turned)
         return_gradient(1, banks[1], nc.scalar.copy)
         for t in range(1, PACK):
-            centre(t, half(0), centred[:, t, :])
+            centre(t, direct, centred[:, t, :])
         g_woven[SECOND, 0] = behind_return[:, 2 * R :].rearrange("s (i t) -> s i t", t=PACK)
-        weave_centred(half(0), centred[:], g_woven[SECOND, 0])
+        weave_centred(half(0), centred[:, :, :HALF], g_woven[SECOND, 0])
         quantise_queries_along_r(SECOND, 0)
         quantise_gradient(FIRST, 0)
         quantise_gradient(SECOND, 0)
@@ -465,26 +465,25 @@ def tile_attend_ggqa_sm_k_kernel(tc, q1, q2, kT, dp1, dp2, us, ts, w1, w2, offs,
         for j in range(2):
             nc.scalar.copy(early_sums[j][:], sums(j, 0, banks[4][:, half(j)]))
             nc.scalar.activation(windows[j][:].indirect(half_lists[0]), early_sums[j][:], ACT.Copy)
-        centred = held([P, PACK, P], F32, "centred1", "g_woven0_0")
-        for t in range(PACK):
-            centre(t, block(2), centred[:, t, :])
-        weave_centred(block(2), centred[:], g_woven[SECOND, 1][:, :P, :])
+        g_woven[SECOND, 1] = held([P, HALF, PACK], BF16, "g_woven1_1", "g_woven0_0")[:]
+        weave_centred(block(2), centred[:, :, HALF:], g_woven[SECOND, 1][:, :P, :])
+        weave_turned_words(1, banks[3], nc.vector.tensor_copy,
+                           held([P, 2 * P * PACK], BF16, "second_qr_woven1", "first_turned")[:])
         last_block_return(last_turned, banks[5][:, half(0)])
         quantise_gradient(FIRST, 1, "last_turned")
         key_gradient_pass(banks[6][:, half(0)], 0, FIRST, 1, True)
         quantise_gradient(SECOND, 1)
         key_gradient_pass(banks[6][:, half(0)], 0, SECOND, 1, False)
-        weave_turned_words(1, banks[3], nc.vector.tensor_copy,
-                           held([P, 2 * P * PACK], BF16, "second_qr_woven1", "g_woven1_1")[:])
+        qr_codes[SECOND].append(held([P, 2 * P], U32, "qr_codes1_1", "g_woven0_1")[:])
+        quantise_queries_along_r(SECOND, 1)
         late_sums = [held([P, HALF], F32, f"dk{j}_1") for j in range(2)]
         nc.vector.tensor_copy(late_sums[0][:], banks[6][:, half(0)])
-        quantise_queries_along_r(SECOND, 1)
         nc.vector.tensor_copy(late_sums[1][:], sums(1, 1, banks[7][:, half(0)]))
         for j in range(2):
             nc.vector.tensor_copy(windows[j][:].indirect(half_lists[1]), late_sums[j][:])
             nc.sync.dma_start(out_planes[j], windows[j][:])
         for j in range(2, PACK):
-            scalar_scatter(j, 0, sums(j, 0, banks[(4, 2)[j - 2]][:, half(0)]))
+            scalar_scatter(j, 0, sums(j, 0, banks[4 + j][:, half(1)]))
         for j in range(2, PACK):
             vector_scatter(j, 1, sums(j, 1, banks[j - 2][:, half(0)]))
             nc.sync.dma_start(out_planes[j], windows[j][:])

@@ -57,7 +57,7 @@ def tile_attend_ggqa_sm_k_kernel(tc, q1, q2, kT, dp1, dp2, us, ts, w1, w2, offs,
 
         q_raw = [held([P, PACK, R], F32, "q_raw0")]
         dp_sb = []
-        k_planes = [held([P, TOKENS], F32, f"k_plane{j}") for j in range(PACK - 1)]
+        k_planes = [held([P, TOKENS], F32, f"k_plane{j}") for j in range(2)]
         us_sb = held([P, PACK], F32, "us_sb")
         w_sb = [held([P, PACK], F32, f"w_sb{h}") for h in range(HEADS)]
         ts_window = held([P, TOKENS], F32, "ts_window")
@@ -70,7 +70,7 @@ def tile_attend_ggqa_sm_k_kernel(tc, q1, q2, kT, dp1, dp2, us, ts, w1, w2, offs,
         nc.sync.dma_start(q_raw[FIRST][:], q1.rearrange("(p j) r -> p j r", j=PACK))
         nc.sync.dma_start(offsets[:], offs)
         k_hbm = kT.rearrange("(p j) t -> j p t", j=PACK)
-        for j in range(PACK - 1):
+        for j in range(2):
             nc.sync.dma_start(k_planes[j][:], k_hbm[j])
         nc.scalar.dma_start(us_sb[:], us.rearrange("(s t) o -> s (t o)", t=PACK))
         for h, w in enumerate((w1, w2)):
@@ -79,13 +79,13 @@ def tile_attend_ggqa_sm_k_kernel(tc, q1, q2, kT, dp1, dp2, us, ts, w1, w2, offs,
 
         windows = {}
 
-        def zero_window(j, engine, tag=None):
+        def zero_window(j, tag=None):
             windows[j] = held([P, TOKENS], F32, f"window{j}", tag)
             for columns in (slice(0, TOKENS // 2), slice(TOKENS // 2, TOKENS)):
-                engine.memset(windows[j][:, columns].bitcast(I32), 0)
+                nc.gpsimd.memset(windows[j][:, columns].bitcast(I32), 0)
 
-        for j in range(PACK):
-            zero_window(j, nc.gpsimd if j < 2 else nc.vector)
+        for j in range(2):
+            zero_window(j)
 
         for g in range(RUN // PACK):
             bank = quarters(spread_banks[g])
@@ -144,8 +144,10 @@ def tile_attend_ggqa_sm_k_kernel(tc, q1, q2, kT, dp1, dp2, us, ts, w1, w2, offs,
             quantise(qr_woven[h, v], E4M3, qr_codes[h][v], qr_scales[h][v][:])
 
         for u in range(2):
-            weave_queries(FIRST, u, nc.scalar.copy)
+            weave_queries(FIRST, u, (nc.vector.tensor_copy, nc.scalar.copy)[u])
             quantise_queries_along_d(FIRST, u)
+        k_planes.append(held([P, TOKENS], F32, "k_plane2", "q_raw0"))
+        nc.sync.dma_start(k_planes[2][:], k_hbm[2])
         for v in range(2):
             turn_queries(FIRST, v, banks[4 + v])
             weave_turned_queries(FIRST, v, banks[4 + v])
@@ -156,7 +158,7 @@ def tile_attend_ggqa_sm_k_kernel(tc, q1, q2, kT, dp1, dp2, us, ts, w1, w2, offs,
         ts_cols = held([P, PACK], F32, "ts_cols")
         nc.scalar.copy(ts_cols[:], ts_turned[:, :, 0])
 
-        k_pair = held([P, 2, SLOTS], BF16, "k_pair", "ts_window")
+        k_rows = []
         both_woven = held([P, 2, HALF, PACK], BF16, "k_woven", "ts_runs")
         k_woven = [both_woven[:, a] for a in range(2)]
         all_k_codes = held([P, SLOTS], U32, "k_codes")
@@ -166,21 +168,22 @@ def tile_attend_ggqa_sm_k_kernel(tc, q1, q2, kT, dp1, dp2, us, ts, w1, w2, offs,
         half_lists = [offsets[:, a * HALF // 16 : (a + 1) * HALF // 16] for a in range(2)]
         for j in range(PACK):
             if j < 2:
-                nc.vector.tensor_copy(k_pair[:, j, :], k_planes[j][:].indirect(offsets[:]))
+                k_rows.append(held([P, SLOTS], BF16, f"k_row{j}", ("ts_window", "qr_woven0")[j]))
+                nc.vector.tensor_copy(k_rows[j][:], k_planes[j][:].indirect(offsets[:]))
             else:
                 for a in range(2):
                     nc.vector.tensor_copy(k_woven[a][:, :, j], k_planes[j][:].indirect(half_lists[a]))
             if j == 0:
                 k_planes.append(held([P, TOKENS], F32, "k_plane3", "k_plane0"))
                 nc.sync.dma_start(k_planes[-1][:], k_hbm[PACK - 1])
+                quantise_queries_along_r(FIRST, 0)
             if j == 1:
                 q_raw.append(held([P, PACK, R], F32, "q_raw1", "k_plane1"))
                 nc.sync.dma_start(q_raw[SECOND][:], q2.rearrange("(p j) r -> p j r", j=PACK))
-                quantise_queries_along_r(FIRST, 0)
                 for place in range(2):
-                    nc.scalar.copy(both_woven[:, :, :, place].rearrange("p a i -> p (a i)"), k_pair[:, place, :])
+                    nc.scalar.copy(both_woven[:, :, :, place].rearrange("p a i -> p (a i)"), k_rows[place][:])
             if j == 2:
-                qr_codes[FIRST].append(held([P, 2 * P], U32, "qr_codes0_1", "k_plane2")[:])
+                qr_codes[FIRST].append(held([P, 2 * P], U32, "qr_codes0_1")[:])
                 quantise_queries_along_r(FIRST, 1)
             if j >= 2:
                 dp_sb.append(held([P, PACK, SLOTS], F32, f"dp_sb{j - 2}", "qr_woven1" if j == 2 else "k_plane0"))
@@ -377,6 +380,7 @@ def tile_attend_ggqa_sm_k_kernel(tc, q1, q2, kT, dp1, dp2, us, ts, w1, w2, offs,
         for v in range(2):
             nc.gpsimd.tensor_scalar(all_rounded[:, 2 * v : 2 * v + 2, :], q_raw[SECOND][:, 2 * v : 2 * v + 2, :], 1.0, 0.0,
                                     ALU.mult, ALU.add)
+        zero_window(PACK - 1, "k_plane1")
         turned_pair(SECOND, 0, banks[2:4])
         for t in range(2):
             direct_maximum(t)
@@ -393,6 +397,7 @@ def tile_attend_ggqa_sm_k_kernel(tc, q1, q2, kT, dp1, dp2, us, ts, w1, w2, offs,
             turn_rounded_queries(rounded, v, banks[2 + v])
         exponentials(2)
         exponentials(3)
+        zero_window(2, "second_woven0")
         make_products(0)
         make_products(1)
         make_inverses(1)

@@ -97,7 +97,7 @@ def tile_attend_ggqa_sm_k_kernel(tc, q1, q2, kT, dp1, dp2, us, ts, w1, w2, offs,
                  bank.rearrange("m c p -> m p c"))
 
         ts_slots = held([P, SLOTS], F32, "ts_slots")
-        nc.vector.tensor_copy(ts_slots[:], ts_window[:].indirect(offsets[:]))
+        nc.scalar.activation(ts_slots[:], ts_window[:].indirect(offsets[:]), ACT.Copy)
 
         def quantise(source, fmt, codes, scales):
             nc.vector.quantize_mx(out=codes.bitcast(fmt), scales=scales, in_=source)
@@ -161,18 +161,19 @@ def tile_attend_ggqa_sm_k_kernel(tc, q1, q2, kT, dp1, dp2, us, ts, w1, w2, offs,
         k_rows = []
         both_woven = held([P, 2, HALF, PACK], BF16, "k_woven", "ts_runs")
         k_woven = [both_woven[:, a] for a in range(2)]
-        all_k_codes = held([P, SLOTS], U32, "k_codes")
-        all_k_scales = held([P, SLOTS], U8, "k_scales")
-        k_codes = [all_k_codes[:, a * HALF : (a + 1) * HALF] for a in range(2)]
-        k_scales = [all_k_scales[:, a * HALF : (a + 1) * HALF] for a in range(2)]
         half_lists = [offsets[:, a * HALF // 16 : (a + 1) * HALF // 16] for a in range(2)]
         for j in range(PACK):
             if j < 2:
                 k_rows.append(held([P, SLOTS], BF16, f"k_row{j}", ("ts_window", "qr_woven0")[j]))
                 nc.vector.tensor_copy(k_rows[j][:], k_planes[j][:].indirect(offsets[:]))
-            else:
+            elif j == 2:
                 for a in range(2):
                     nc.vector.tensor_copy(k_woven[a][:, :, j], k_planes[j][:].indirect(half_lists[a]))
+            else:
+                last_half = held([P, HALF], BF16, "last_half")
+                nc.vector.tensor_copy(k_woven[0][:, :, j], k_planes[j][:].indirect(half_lists[0]))
+                nc.scalar.activation(last_half[:], k_planes[j][:].indirect(half_lists[1]), ACT.Copy)
+                nc.vector.tensor_copy(k_woven[1][:, :, j], last_half[:])
             if j == 0:
                 k_planes.append(held([P, TOKENS], F32, "k_plane3", "k_plane0"))
                 nc.sync.dma_start(k_planes[-1][:], k_hbm[PACK - 1])
@@ -186,10 +187,12 @@ def tile_attend_ggqa_sm_k_kernel(tc, q1, q2, kT, dp1, dp2, us, ts, w1, w2, offs,
                 qr_codes[FIRST].append(held([P, 2 * P], U32, "qr_codes0_1")[:])
                 quantise_queries_along_r(FIRST, 1)
             if j >= 2:
-                dp_sb.append(held([P, PACK, SLOTS], F32, f"dp_sb{j - 2}", "qr_woven1" if j == 2 else "k_plane0"))
+                dp_sb.append(held([P, PACK, SLOTS], F32, f"dp_sb{j - 2}", f"qr_woven{3 - j}"))
                 nc.sync.dma_start(dp_sb[-1][:], (dp1, dp2)[j - 2].rearrange("(s t) i -> s t i", t=PACK))
+        all_k_codes = held([P, SLOTS], U32, "k_codes", "k_plane0")
+        all_k_scales = held([P, SLOTS], U8, "k_scales")
         for a in range(2):
-            quantise(k_woven[a].rearrange("p i j -> p (i j)"), E4M3, k_codes[a], k_scales[a])
+            quantise(k_woven[a].rearrange("p i j -> p (i j)"), E4M3, all_k_codes[:, half(a)], all_k_scales[:, half(a)])
 
         neg_us = held([P, PACK], F32, "neg_us")
         nc.gpsimd.tensor_scalar(neg_us[:], us_sb[:], -1.0, 0.0, ALU.mult, ALU.add)

@@ -200,6 +200,9 @@ def tile_attend_ggqa_sm_k_kernel(tc, q1, q2, kT, dp1, dp2, us, ts, w1, w2, offs,
         for h in range(HEADS):
             nc.gpsimd.tensor_tensor(numerators[:, 0, PACK * h : PACK * (h + 1)], w_sb[h][:], us_sb[:], ALU.mult)
         nc.gpsimd.memset(numerators[:, 1, :], -1.0)
+        side_by_side = held([P, 2, 4], F32, "side_by_side", "ts_window")
+        nc.vector.memset(side_by_side[:, :, 3], -1.0)
+        nc.vector.tensor_tensor(side_by_side[:, :, 0], w_sb[FIRST][:, 2:4], us_sb[:, 2:4], ALU.mult)
 
 
         weave_queries(SECOND, 0, nc.vector.tensor_copy)
@@ -224,14 +227,15 @@ def tile_attend_ggqa_sm_k_kernel(tc, q1, q2, kT, dp1, dp2, us, ts, w1, w2, offs,
         late_row_sums = last_scaled[:, 3 * P + 8 : 3 * P + 8 + TILES]
 
         def row_sums(first, count):
+            if first in (2, 3):
+                return side_by_side[:, first - 2, 2:3]
             return (early_row_sums if first < 2 else late_row_sums)[:, first : first + count]
 
-        inverses = [scaled[FIRST][PACK - 1][:, P : P + 2], dp_sb[FIRST][:, 0, 0:2], last_scaled[:, 3 * P : 3 * P + 2], dp_sb[FIRST][:, 2, 0:2]]
+        inverses = [scaled[FIRST][PACK - 1][:, P : P + 2], side_by_side[:, :, 1], last_scaled[:, 3 * P : 3 * P + 2], dp_sb[FIRST][:, 2, 0:2]]
         factors = [last_scaled[:, 0:4].rearrange("p (k e) -> p k e", k=2)]
         factors.append(last_scaled[:, 2 * P : 2 * P + 4].rearrange("p (k e) -> p k e", k=2))
         factors = factors + [held([P, 2, 2], F32, f"factors{m}")[:] for m in range(2, PACK)]
-        shifts = {n: held([P, 2], F32, f"shifts{n}")[:] for n in (0, 2, 3, 4, 6)}
-        shifts[1] = last_scaled[:, 2 * P + 4 : 2 * P + 6]
+        shifts = {n: held([P, 2], F32, f"shifts{n}")[:] for n in (2, 3, 4, 6)}
 
         def scores(target, stationary, stationary_scales, moving, moving_scales):
             nc.tensor.matmul_mx(out=target, lhsT=stationary.bitcast(E4M3), lhsT_scale=stationary_scales,
@@ -264,6 +268,9 @@ def tile_attend_ggqa_sm_k_kernel(tc, q1, q2, kT, dp1, dp2, us, ts, w1, w2, offs,
             nc.vector.reciprocal(inverses[m], totals[:, 2 * m : 2 * m + 2])
 
         def make_factors(m):
+            if m == 1:
+                nc.vector.tensor_reduce(factors[m][:, 0, :], side_by_side[:, :, 0:2], mybir.AxisListType.X, ALU.mult)
+                return
             nc.vector.tensor_tensor(factors[m], numerators[:, :, 2 * m : 2 * m + 2],
                                     inverses[m].unsqueeze(1).to_broadcast([P, 2, 2]), ALU.mult)
 
@@ -273,6 +280,9 @@ def tile_attend_ggqa_sm_k_kernel(tc, q1, q2, kT, dp1, dp2, us, ts, w1, w2, offs,
                                            dp_sb[h][:, t, :], ALU.mult, ALU.mult, accum_out=row_sums(n, 1))
 
         def make_shifts(first, count):
+            if first in (2, 3):
+                nc.vector.tensor_reduce(shifts[first][:, :1], side_by_side[:, first - 2, 1:4], mybir.AxisListType.X, ALU.mult)
+                return
             nc.vector.tensor_tensor(shifts[first][:, :count], row_sums(first, count),
                                     factors[first // 2][:, 1, first % 2 : first % 2 + count], ALU.mult)
 
@@ -288,6 +298,9 @@ def tile_attend_ggqa_sm_k_kernel(tc, q1, q2, kT, dp1, dp2, us, ts, w1, w2, offs,
 
         def mean_term(t, columns, target):
             nc.scalar.activation(target, exps[t][:, columns], ACT.Copy, scale=shift(t))
+
+        def early_mean_term(t):
+            nc.gpsimd.tensor_scalar(means[t], exps[t], row_sums(t, 1), factors[0][:, 1, t : t + 1], ALU.mult, ALU.mult)
 
         def turn_term(t, opens, blocks):
             for b in blocks:
@@ -327,9 +340,11 @@ def tile_attend_ggqa_sm_k_kernel(tc, q1, q2, kT, dp1, dp2, us, ts, w1, w2, offs,
             nc.scalar.activation(words[:], quarters(bank).rearrange("i (u e) s -> i u s e", e=2), ACT.Copy,
                                  scale=ts_cols[:, PACK - 1 : PACK])
 
-        def last_block_return(words, back):
+        def last_block_back(words, back):
             for u in range(2):
                 nc.tensor.transpose(back[:, block(u)], words[:].rearrange("p a b c -> p (a b c)").bitcast(F32)[:, block(u)], ident[:])
+
+        def last_block_return(back):
             target = g_woven[SECOND, 1][:, P:, :].rearrange("s i t -> s (i t)").bitcast(F32).rearrange("s (i u) -> s i u", u=2)
             nc.vector.tensor_copy(target, back.rearrange("s (u i) -> s i u", u=2))
 
@@ -375,9 +390,9 @@ def tile_attend_ggqa_sm_k_kernel(tc, q1, q2, kT, dp1, dp2, us, ts, w1, w2, offs,
             for b in range(PACK):
                 scale_turned(h, u, b, pair[b // 2][:, half(b % 2)])
 
-        direct_rows(0, banks[0])
+        for t in range(2):
+            direct_rows(t, banks[t])
         turned_pair(FIRST, 1, banks[6:8])
-        direct_rows(1, banks[1])
         all_rounded = held([P, PACK, R], BF16, "rounded", "second_woven1")
         rounded = [all_rounded[:, j, :] for j in range(PACK)]
         for v in range(2):
@@ -400,17 +415,17 @@ def tile_attend_ggqa_sm_k_kernel(tc, q1, q2, kT, dp1, dp2, us, ts, w1, w2, offs,
             turn_rounded_queries(rounded, v, banks[2 + v])
         exponentials(2)
         exponentials(3)
-        zero_window(2, "second_woven0")
         make_products(0)
         make_products(1)
         make_inverses(1)
-        make_shifts(0, 1)
+        early_mean_term(0)
+        early_mean_term(1)
         turned_rows(6, banks[0])
         make_factors(1)
-        make_shifts(1, 1)
         turned_rows(7, banks[1])
         for n in range(PACK, TILES):
             exponentials(n)
+        zero_window(2, "neg_z7")
         make_inverses(2)
         make_products(2)
         make_factors(2)
@@ -420,8 +435,8 @@ def tile_attend_ggqa_sm_k_kernel(tc, q1, q2, kT, dp1, dp2, us, ts, w1, w2, offs,
         make_products(4)
         make_shifts(3, 1)
         make_factors(3)
-        for t in range(PACK - 1):
-            mean_term(t, slice(0, SLOTS), means[t])
+        weave_turned_words(1, banks[3], nc.scalar.copy, held([P, 2 * P * PACK], BF16, "second_qr_woven1", "neg_z6")[:])
+        mean_term(2, slice(0, SLOTS), means[2])
         for a in range(2):
             mean_term(PACK - 1, half(a), final_means[a])
         weave_turned_words(0, banks[2], nc.scalar.copy, fourth[:, :SLOTS].bitcast(BF16))
@@ -443,9 +458,8 @@ def tile_attend_ggqa_sm_k_kernel(tc, q1, q2, kT, dp1, dp2, us, ts, w1, w2, offs,
         make_products(7)
         for b in range(2):
             round_turned(b)
-        direct = slice(0, HALF + P)
-        centred = held([P, PACK, HALF + P], F32, "centred")
-        centre(0, direct, centred[:, 0, :])
+        centred = held([P, PACK, HALF], F32, "centred")
+        centre(0, half(0), centred[:, 0, :])
         make_shifts(6, 2)
         turn_back(0, banks[0])
         return_gradient(0, banks[0], nc.scalar.copy)
@@ -461,24 +475,27 @@ def tile_attend_ggqa_sm_k_kernel(tc, q1, q2, kT, dp1, dp2, us, ts, w1, w2, offs,
         turn_back(1, banks[1])
         last_turned = held([P, 2, P, 2], BF16, "last_turned")
         last_block_round(banks[2], last_turned)
+        last_block_back(last_turned, banks[3][:, half(0)])
         return_gradient(1, banks[1], nc.scalar.copy)
         for t in range(1, PACK):
-            centre(t, direct, centred[:, t, :])
+            centre(t, half(0), centred[:, t, :])
         g_woven[SECOND, 0] = behind_return[:, 2 * R :].rearrange("s (i t) -> s i t", t=PACK)
-        weave_centred(half(0), centred[:, :, :HALF], g_woven[SECOND, 0])
+        weave_centred(half(0), centred[:], g_woven[SECOND, 0])
         quantise_queries_along_r(SECOND, 0)
         quantise_gradient(FIRST, 0)
         quantise_gradient(SECOND, 0)
+        g_woven[SECOND, 1] = held([P, HALF, PACK], BF16, "g_woven1_1", "last_turned")[:]
+        later_centred = held([P, PACK, P], F32, "later_centred", "g_woven0_0")[:]
         early_sums = [held([P, HALF], F32, f"dk{j}_0") for j in range(2)]
-        for j in range(2):
-            nc.scalar.copy(early_sums[j][:], sums(j, 0, banks[4][:, half(j)]))
-            nc.scalar.activation(windows[j][:].indirect(half_lists[0]), early_sums[j][:], ACT.Copy)
-        g_woven[SECOND, 1] = held([P, HALF, PACK], BF16, "g_woven1_1", "g_woven0_0")[:]
-        weave_centred(block(2), centred[:, :, HALF:], g_woven[SECOND, 1][:, :P, :])
-        weave_turned_words(1, banks[3], nc.vector.tensor_copy,
-                           held([P, 2 * P * PACK], BF16, "second_qr_woven1", "first_turned")[:])
-        last_block_return(last_turned, banks[5][:, half(0)])
-        quantise_gradient(FIRST, 1, "last_turned")
+        nc.scalar.copy(early_sums[0][:], sums(0, 0, banks[7][:, half(1)]))
+        nc.scalar.activation(windows[0][:].indirect(half_lists[0]), early_sums[0][:], ACT.Copy)
+        nc.scalar.copy(early_sums[1][:], sums(1, 0, banks[1][:, half(0)]))
+        nc.scalar.activation(windows[1][:].indirect(half_lists[0]), early_sums[1][:], ACT.Copy)
+        for t in range(PACK):
+            centre(t, block(2), later_centred[:, t, :])
+        last_block_return(banks[3][:, half(0)])
+        weave_centred(block(2), later_centred, g_woven[SECOND, 1][:, :P, :])
+        quantise_gradient(FIRST, 1, "first_turned")
         key_gradient_pass(banks[6][:, half(0)], 0, FIRST, 1, True)
         quantise_gradient(SECOND, 1)
         key_gradient_pass(banks[6][:, half(0)], 0, SECOND, 1, False)
@@ -493,5 +510,5 @@ def tile_attend_ggqa_sm_k_kernel(tc, q1, q2, kT, dp1, dp2, us, ts, w1, w2, offs,
         for j in range(2, PACK):
             scalar_scatter(j, 0, sums(j, 0, banks[4 + j][:, half(1)]))
         for j in range(2, PACK):
-            vector_scatter(j, 1, sums(j, 1, banks[j - 2][:, half(0)]))
+            vector_scatter(j, 1, sums(j, 1, banks[2 + j][:, half(0)]))
             nc.sync.dma_start(out_planes[j], windows[j][:])

@@ -346,7 +346,7 @@ def tile_attend_ggqa_sm_k_kernel(tc, q1, q2, kT, dp1, dp2, us, ts, w1, w2, offs,
 
         def last_block_return(back):
             target = g_woven[SECOND, 1][:, P:, :].rearrange("s i t -> s (i t)").bitcast(F32).rearrange("s (i u) -> s i u", u=2)
-            nc.vector.tensor_copy(target, back.rearrange("s (u i) -> s i u", u=2))
+            nc.scalar.copy(target, back.rearrange("s (u i) -> s i u", u=2))
 
         def weave_centred(columns, source, target):
             ts_lines = ts_slots[:, columns].rearrange("p (c i) -> p c i", i=LINE).unsqueeze(2)
@@ -486,21 +486,23 @@ def tile_attend_ggqa_sm_k_kernel(tc, q1, q2, kT, dp1, dp2, us, ts, w1, w2, offs,
         quantise_gradient(SECOND, 0)
         g_woven[SECOND, 1] = held([P, HALF, PACK], BF16, "g_woven1_1", "last_turned")[:]
         later_centred = held([P, PACK, P], F32, "later_centred", "g_woven0_0")[:]
-        early_sums = [held([P, HALF], F32, f"dk{j}_0") for j in range(2)]
+        last_block_return(banks[3][:, half(0)])
+        early_sums = [held([P, HALF], F32, "dk0_0")]
         nc.scalar.copy(early_sums[0][:], sums(0, 0, banks[7][:, half(1)]))
         nc.scalar.activation(windows[0][:].indirect(half_lists[0]), early_sums[0][:], ACT.Copy)
-        nc.scalar.copy(early_sums[1][:], sums(1, 0, banks[1][:, half(0)]))
-        nc.scalar.activation(windows[1][:].indirect(half_lists[0]), early_sums[1][:], ACT.Copy)
+        sums(1, 0, banks[2][:, half(0)])
         for t in range(PACK):
             centre(t, block(2), later_centred[:, t, :])
-        last_block_return(banks[3][:, half(0)])
-        weave_centred(block(2), later_centred, g_woven[SECOND, 1][:, :P, :])
         quantise_gradient(FIRST, 1, "first_turned")
         key_gradient_pass(banks[6][:, half(0)], 0, FIRST, 1, True)
+        weave_centred(block(2), later_centred, g_woven[SECOND, 1][:, :P, :])
         quantise_gradient(SECOND, 1)
         key_gradient_pass(banks[6][:, half(0)], 0, SECOND, 1, False)
         qr_codes[SECOND].append(held([P, 2 * P], U32, "qr_codes1_1", "g_woven0_1")[:])
         quantise_queries_along_r(SECOND, 1)
+        early_sums.append(held([P, HALF], F32, "dk1_0", "last_turned"))
+        nc.vector.tensor_copy(early_sums[1][:], banks[2][:, half(0)])
+        nc.scalar.activation(windows[1][:].indirect(half_lists[0]), early_sums[1][:], ACT.Copy)
         late_sums = [held([P, HALF], F32, f"dk{j}_1") for j in range(2)]
         nc.vector.tensor_copy(late_sums[0][:], banks[6][:, half(0)])
         nc.vector.tensor_copy(late_sums[1][:], sums(1, 1, banks[7][:, half(0)]))

@@ -76,7 +76,6 @@ def tile_attend_ggqa_sm_k_kernel(tc, q1, q2, kT, dp1, dp2, us, ts, w1, w2, offs,
         for h, w in enumerate((w1, w2)):
             nc.scalar.dma_start(w_sb[h][:], w.rearrange("(s t) o -> s (t o)", t=PACK))
 
-
         windows = {}
 
         def zero_window(j, tag=None):
@@ -106,7 +105,9 @@ def tile_attend_ggqa_sm_k_kernel(tc, q1, q2, kT, dp1, dp2, us, ts, w1, w2, offs,
         q_woven = [[first_woven[:, u] for u in range(2)],
                    [held([P, 2, P, PACK], BF16, f"second_woven{u}")[:] for u in range(2)]]
         qd_codes = [held([P, R], U32, f"qd_codes{h}") for h in range(HEADS)]
-        qd_scales = [held([P, R], U8, f"qd_scales{h}") for h in range(HEADS)]
+        first_qd_scales = held([P, R], U8, "first_qd_scales")
+        qd_scales = {(FIRST, u): first_qd_scales[:, half(u)] for u in range(2)}
+        qd_scales[SECOND, 0] = held([P, HALF], U8, "second_qd_scales0")[:]
         qr_woven = {(FIRST, v): held([P, 2 * P * PACK], BF16, f"qr_woven{v}")[:] for v in range(2)}
         qr_codes = [[held([P, 2 * P], U32, "qr_codes0_0")[:]],
                     [held([P, 2 * P], U32, "qr_codes1_0")[:]]]
@@ -118,7 +119,7 @@ def tile_attend_ggqa_sm_k_kernel(tc, q1, q2, kT, dp1, dp2, us, ts, w1, w2, offs,
 
         def quantise_queries_along_d(h, u):
             quantise(q_woven[h][u].rearrange("p e s j -> p (e s j)"), E4M3,
-                     qd_codes[h][:, 2 * P * u : 2 * P * (u + 1)], qd_scales[h][:, 2 * P * u : 2 * P * (u + 1)])
+                     qd_codes[h][:, half(u)], qd_scales[h, u])
 
         def turn_queries(h, v, bank):
             for t in range(PACK):
@@ -138,7 +139,7 @@ def tile_attend_ggqa_sm_k_kernel(tc, q1, q2, kT, dp1, dp2, us, ts, w1, w2, offs,
         def weave_turned_words(v, bank, copy, target):
             qr_woven[SECOND, v] = target
             copy(qr_woven[SECOND, v].bitcast(F32).rearrange("s (e p u) -> s e p u", e=2, u=2),
-                           bank[:].rearrange("s (e u p) -> s e p u", e=2, u=2))
+                 bank[:].rearrange("s (e u p) -> s e p u", e=2, u=2))
 
         def quantise_queries_along_r(h, v):
             quantise(qr_woven[h, v], E4M3, qr_codes[h][v], qr_scales[h][v][:])
@@ -196,29 +197,29 @@ def tile_attend_ggqa_sm_k_kernel(tc, q1, q2, kT, dp1, dp2, us, ts, w1, w2, offs,
 
         neg_us = held([P, PACK], F32, "neg_us")
         nc.gpsimd.tensor_scalar(neg_us[:], us_sb[:], -1.0, 0.0, ALU.mult, ALU.add)
+        direct_neg_us = held([P, 2], F32, "direct_neg_us")
+        nc.gpsimd.tensor_scalar(direct_neg_us[:], us_sb[:, :2], -1.0, 0.0, ALU.mult, ALU.add)
         numerators = held([P, 2, TILES], F32, "numerators")
         for h in range(HEADS):
             nc.gpsimd.tensor_tensor(numerators[:, 0, PACK * h : PACK * (h + 1)], w_sb[h][:], us_sb[:], ALU.mult)
         nc.gpsimd.memset(numerators[:, 1, :], -1.0)
         side_by_side = held([P, 2, 4], F32, "side_by_side", "ts_window")
-        nc.vector.memset(side_by_side[:, :, 3], -1.0)
+        nc.vector.memset(side_by_side[:, :, 2], -1.0)
         nc.vector.tensor_tensor(side_by_side[:, :, 0], w_sb[FIRST][:, 2:4], us_sb[:, 2:4], ALU.mult)
 
-
         weave_queries(SECOND, 0, nc.vector.tensor_copy)
-        weave_queries(SECOND, 1, nc.vector.tensor_copy, slice(0, P // 2))
-        weave_queries(SECOND, 1, nc.scalar.copy, slice(P // 2, P))
-        for u in range(2):
-            quantise_queries_along_d(SECOND, u)
+        weave_queries(SECOND, 1, nc.vector.tensor_copy, slice(0, P // 4))
+        quantise_queries_along_d(SECOND, 0)
 
         behind_weave = held([P, 4 * SLOTS], F32, "behind_weave", "second_woven0")
+        first_scaled = held([P, 2, HALF], F32, "first_scaled")
         neg_z = [behind_weave[:, t * SLOTS : (t + 1) * SLOTS] for t in range(2)]
         neg_z = neg_z + [held([P, SLOTS], F32, f"neg_z{n}")[:] for n in range(2, TILES)]
         fourth = held([P, HALF + SLOTS], F32, "fourth")
         exps = [fourth[:, HALF:] if n == PACK - 1 else held([P, SLOTS], F32, f"e{n}")[:] for n in range(TILES)]
         neg_max = [held([P, 1], F32, f"neg_max{n}")[:] for n in range(TILES)]
         second_scaled = held([P, PACK * R], F32, "second_scaled")
-        scaled = [[behind_weave[:, 2 * SLOTS + b * HALF : 2 * SLOTS + (b + 1) * HALF] for b in range(PACK)],
+        scaled = [[first_scaled[:, b, :] for b in range(2)] + [behind_weave[:, 3 * SLOTS + b * HALF : 3 * SLOTS + (b + 1) * HALF] for b in range(2)],
                   [second_scaled[:, b * R : (b + 1) * R] for b in range(PACK)]]
         products = [held([P, SLOTS], F32, f"products{n}")[:] for n in range(TILES)]
         totals = held([P, TILES], F32, "totals")
@@ -226,12 +227,14 @@ def tile_attend_ggqa_sm_k_kernel(tc, q1, q2, kT, dp1, dp2, us, ts, w1, w2, offs,
         early_row_sums = last_scaled[:, P : P + 2]
         late_row_sums = last_scaled[:, 3 * P + 8 : 3 * P + 8 + TILES]
 
+        middle_row_sums = [held([P, 1], F32, f"row_sum{n}") for n in (2, 3)]
+
         def row_sums(first, count):
             if first in (2, 3):
-                return side_by_side[:, first - 2, 2:3]
+                return middle_row_sums[first - 2][:]
             return (early_row_sums if first < 2 else late_row_sums)[:, first : first + count]
 
-        inverses = [scaled[FIRST][PACK - 1][:, P : P + 2], side_by_side[:, :, 1], last_scaled[:, 3 * P : 3 * P + 2], dp_sb[FIRST][:, 2, 0:2]]
+        inverses = [scaled[FIRST][PACK - 1][:, P : P + 2], side_by_side[:, :, 1::2], last_scaled[:, 3 * P : 3 * P + 2], dp_sb[FIRST][:, 2, 0:2]]
         factors = [last_scaled[:, 0:4].rearrange("p (k e) -> p k e", k=2)]
         factors.append(last_scaled[:, 2 * P : 2 * P + 4].rearrange("p (k e) -> p k e", k=2))
         factors = factors + [held([P, 2, 2], F32, f"factors{m}")[:] for m in range(2, PACK)]
@@ -242,15 +245,15 @@ def tile_attend_ggqa_sm_k_kernel(tc, q1, q2, kT, dp1, dp2, us, ts, w1, w2, offs,
                                 rhs=moving.bitcast(E4M3), rhs_scale=moving_scales, start=True, stop=True)
 
         def direct_rows(t, bank):
-            scores(bank[:], qd_codes[FIRST][:, block(t)], qd_scales[FIRST][:, block(t)], all_k_codes[:], all_k_scales[:])
-            nc.vector.scalar_tensor_tensor(neg_z[t], bank[:], neg_us[:, t : t + 1], ts_slots[:], ALU.mult, ALU.mult)
+            scores(bank[:], qd_codes[FIRST][:, block(t)], first_qd_scales[:, block(t)], all_k_codes[:], all_k_scales[:])
+            nc.vector.scalar_tensor_tensor(neg_z[t], bank[:], direct_neg_us[:, t : t + 1], ts_slots[:], ALU.mult, ALU.mult)
 
         def direct_maximum(t):
             nc.vector.tensor_reduce(neg_max[t], neg_z[t], mybir.AxisListType.X, ALU.min)
 
         def turned_scores(h, u, b, target):
             rows = half(u)
-            scores(target, all_k_codes[:, block(b)], all_k_scales[:, block(b)], qd_codes[h][:, rows], qd_scales[h][:, rows])
+            scores(target, all_k_codes[:, block(b)], all_k_scales[:, block(b)], qd_codes[h][:, rows], qd_scales[h, u])
 
         def scale_turned(h, u, b, target):
             nc.scalar.activation(scaled[h][b] if h == FIRST else scaled[h][b][:, half(u)], target, ACT.Copy, scale=ts_cols[:, b : b + 1])
@@ -265,11 +268,13 @@ def tile_attend_ggqa_sm_k_kernel(tc, q1, q2, kT, dp1, dp2, us, ts, w1, w2, offs,
             nc.scalar.activation(exps[n], neg_z[n], ACT.Exp, bias=neg_max[n], scale=-1.0, accum_out=totals[:, n : n + 1])
 
         def make_inverses(m):
-            nc.vector.reciprocal(inverses[m], totals[:, 2 * m : 2 * m + 2])
+            pair = totals[:, 2 * m : 2 * m + 2]
+            nc.vector.reciprocal(inverses[m], pair.unsqueeze(2).to_broadcast([P, 2, 2]) if m == 1 else pair)
 
         def make_factors(m):
             if m == 1:
-                nc.vector.tensor_reduce(factors[m][:, 0, :], side_by_side[:, :, 0:2], mybir.AxisListType.X, ALU.mult)
+                nc.vector.tensor_reduce(factors[m].rearrange("p k e -> p e k"), side_by_side[:].rearrange("p e (k f) -> p e k f", f=2),
+                                        mybir.AxisListType.X, ALU.mult)
                 return
             nc.vector.tensor_tensor(factors[m], numerators[:, :, 2 * m : 2 * m + 2],
                                     inverses[m].unsqueeze(1).to_broadcast([P, 2, 2]), ALU.mult)
@@ -281,7 +286,7 @@ def tile_attend_ggqa_sm_k_kernel(tc, q1, q2, kT, dp1, dp2, us, ts, w1, w2, offs,
 
         def make_shifts(first, count):
             if first in (2, 3):
-                nc.vector.tensor_reduce(shifts[first][:, :1], side_by_side[:, first - 2, 1:4], mybir.AxisListType.X, ALU.mult)
+                nc.scalar.activation(shifts[first][:, :1], row_sums(first, 1), ACT.Copy, scale=factors[1][:, 1, first - 2 : first - 1])
                 return
             nc.vector.tensor_tensor(shifts[first][:, :count], row_sums(first, count),
                                     factors[first // 2][:, 1, first % 2 : first % 2 + count], ALU.mult)
@@ -384,6 +389,7 @@ def tile_attend_ggqa_sm_k_kernel(tc, q1, q2, kT, dp1, dp2, us, ts, w1, w2, offs,
             nc.scalar.activation(windows[j][:].indirect(half_lists[a]), dk[:], ACT.Copy)
 
         out_planes = out.rearrange("(p j) c -> j p c", j=PACK)
+
         def turned_pair(h, u, pair):
             for b in range(PACK):
                 turned_scores(h, u, b, pair[b // 2][:, half(b % 2)])
@@ -393,15 +399,21 @@ def tile_attend_ggqa_sm_k_kernel(tc, q1, q2, kT, dp1, dp2, us, ts, w1, w2, offs,
         for t in range(2):
             direct_rows(t, banks[t])
         turned_pair(FIRST, 1, banks[6:8])
-        all_rounded = held([P, PACK, R], BF16, "rounded", "second_woven1")
-        rounded = [all_rounded[:, j, :] for j in range(PACK)]
-        for v in range(2):
-            nc.gpsimd.tensor_scalar(all_rounded[:, 2 * v : 2 * v + 2, :], q_raw[SECOND][:, 2 * v : 2 * v + 2, :], 1.0, 0.0,
-                                    ALU.mult, ALU.add)
-        zero_window(PACK - 1, "k_plane1")
+        rounded = []
+
+        def round_queries(v, target):
+            nc.gpsimd.tensor_scalar(target, q_raw[SECOND][:, 2 * v : 2 * v + 2, :], 1.0, 0.0, ALU.mult, ALU.add)
+            rounded.extend(target[:, e, :] for e in range(2))
+
+        weave_queries(SECOND, 1, nc.scalar.copy, slice(P // 4, P))
+        round_queries(0, behind_weave[:, 2 * SLOTS : 3 * SLOTS].bitcast(BF16).rearrange("p (e r) -> p e r", e=2))
         turned_pair(SECOND, 0, banks[2:4])
-        for t in range(2):
-            direct_maximum(t)
+        direct_maximum(0)
+        qd_scales[SECOND, 1] = held([P, HALF], U8, "second_qd_scales1", "direct_neg_us")[:]
+        quantise_queries_along_d(SECOND, 1)
+        direct_maximum(1)
+        round_queries(1, held([P, 2, R], BF16, "rounded", "second_woven1")[:])
+        zero_window(PACK - 1, "k_plane1")
         for n in range(2, PACK):
             turned_rows(n, banks[n - 2])
         for n in range(2):
@@ -431,11 +443,12 @@ def tile_attend_ggqa_sm_k_kernel(tc, q1, q2, kT, dp1, dp2, us, ts, w1, w2, offs,
         make_factors(2)
         make_products(3)
         make_inverses(3)
-        make_shifts(2, 1)
         make_products(4)
-        make_shifts(3, 1)
         make_factors(3)
+
+        make_shifts(2, 1)
         weave_turned_words(1, banks[3], nc.scalar.copy, held([P, 2 * P * PACK], BF16, "second_qr_woven1", "neg_z6")[:])
+        make_shifts(3, 1)
         mean_term(2, slice(0, SLOTS), means[2])
         for a in range(2):
             mean_term(PACK - 1, half(a), final_means[a])
@@ -487,6 +500,7 @@ def tile_attend_ggqa_sm_k_kernel(tc, q1, q2, kT, dp1, dp2, us, ts, w1, w2, offs,
         g_woven[SECOND, 1] = held([P, HALF, PACK], BF16, "g_woven1_1", "last_turned")[:]
         later_centred = held([P, PACK, P], F32, "later_centred", "g_woven0_0")[:]
         last_block_return(banks[3][:, half(0)])
+
         early_sums = [held([P, HALF], F32, "dk0_0")]
         nc.scalar.copy(early_sums[0][:], sums(0, 0, banks[7][:, half(1)]))
         nc.scalar.activation(windows[0][:].indirect(half_lists[0]), early_sums[0][:], ACT.Copy)

from contextlib import ExitStack

import concourse.mybir as mybir
from concourse.masks import make_identity

F32 = mybir.dt.float32
BF16 = mybir.dt.bfloat16
I32 = mybir.dt.int32
U32 = mybir.dt.uint32
U16 = mybir.dt.uint16
U8 = mybir.dt.uint8
E4M3 = mybir.dt.float8_e4m3fn_x4
E5M2 = mybir.dt.float8_e5m2_x4
ALU = mybir.AluOpType
ACT = mybir.ActivationFunctionType

P = 128
PACK = 4
D = 512
R = 512
SLOTS = 512
TOKENS = 2048
HEADS = 2
HALF = SLOTS // 2
RUN = TOKENS // P
LINE = 4
FIRST, SECOND = 0, 1
TILES = HEADS * PACK
FLOPS = 4 * 2 * D * R * SLOTS


def tile_attend_ggqa_sm_k_kernel(tc, q1, q2, kT, dp1, dp2, us, ts, w1, w2, offs, out):
    nc = tc.nc
    with ExitStack() as ctx:
        keep = ctx.enter_context(tc.tile_pool(name="keep", bufs=1))
        psum = ctx.enter_context(tc.psum_pool(name="psum", bufs=1))

        def held(shape, dtype, name, tag=None):
            return keep.tile(shape, dtype, name=name, tag=tag or name, align_bytes=64)

        spread_banks = [psum.tile([P, SLOTS], F32, name=f"spread{n}", tag=f"bank{n}") for n in range(RUN // PACK)]
        banks = [psum.tile([P, SLOTS], F32, name=f"bank{n}", tag=f"bank{n}") for n in range(8)]

        def half(a):
            return slice(a * HALF, (a + 1) * HALF)

        def block(b):
            return slice(b * P, (b + 1) * P)

        def quarters(bank):
            return bank[:].rearrange("p (c i) -> p c i", c=PACK)

        def halves(bank):
            return bank[:].rearrange("p (c i) -> p c i", c=2)

        offsets = keep.tile([P, SLOTS // 16], U16, name="offsets")

        q_raw = [held([P, PACK, R], F32, "q_raw0")]
        dp_sb = []
        k_planes = [held([P, TOKENS], F32, f"k_plane{j}") for j in range(2)]
        us_sb = held([P, PACK], F32, "us_sb")
        w_sb = [held([P, PACK], F32, f"w_sb{h}") for h in range(HEADS)]
        ts_window = held([P, TOKENS], F32, "ts_window")
        ident = held([P, P], F32, "ident")

        make_identity(nc, ident[:])

        ts_runs = held([P, RUN], F32, "ts_runs")
        nc.sync.dma_start(ts_runs[:], ts[0:1, :].rearrange("o (p c) -> p (o c)", c=RUN))
        nc.sync.dma_start(q_raw[FIRST][:], q1.rearrange("(p j) r -> p j r", j=PACK))
        nc.sync.dma_start(offsets[:], offs)
        k_hbm = kT.rearrange("(p j) t -> j p t", j=PACK)
        for j in range(2):
            nc.sync.dma_start(k_planes[j][:], k_hbm[j])
        nc.scalar.dma_start(us_sb[:], us.rearrange("(s t) o -> s (t o)", t=PACK))
        for h, w in enumerate((w1, w2)):
            nc.scalar.dma_start(w_sb[h][:], w.rearrange("(s t) o -> s (t o)", t=PACK))

        windows = {}

        def zero_window(j, tag=None):
            windows[j] = held([P, TOKENS], F32, f"window{j}", tag)
            for columns in (slice(0, TOKENS // 2), slice(TOKENS // 2, TOKENS)):
                nc.gpsimd.memset(windows[j][:, columns].bitcast(I32), 0)

        for j in range(2):
            zero_window(j)

        for g in range(RUN // PACK):
            bank = quarters(spread_banks[g])
            for c in range(PACK):
                column = ts_runs[:, PACK * g + c : PACK * g + c + 1]
                nc.tensor.transpose(bank[:, c, :], column.to_broadcast([P, P]), ident[:])
            copy = nc.scalar.copy if g % 2 == 0 else nc.vector.tensor_copy
            copy(ts_window[:].rearrange("m (p c) -> m p c", c=RUN)[:, :, PACK * g : PACK * (g + 1)],
                 bank.rearrange("m c p -> m p c"))

        ts_slots = held([P, SLOTS], F32, "ts_slots")
        nc.scalar.activation(ts_slots[:], ts_window[:].indirect(offsets[:]), ACT.Copy)

        def quantise(source, fmt, codes, scales):
            nc.vector.quantize_mx(out=codes.bitcast(fmt), scales=scales, in_=source)

        first_woven = held([P, 2, 2, P, PACK], BF16, "first_woven", "ts_runs")
        q_woven = [[first_woven[:, u] for u in range(2)],
                   [held([P, 2, P, PACK], BF16, f"second_woven{u}")[:] for u in range(2)]]
        qd_codes = [held([P, R], U32, f"qd_codes{h}") for h in range(HEADS)]
        first_qd_scales = held([P, R], U8, "first_qd_scales")
        qd_scales = {(FIRST, u): first_qd_scales[:, half(u)] for u in range(2)}
        qd_scales[SECOND, 0] = held([P, HALF], U8, "second_qd_scales0")[:]
        qr_woven = {(FIRST, v): held([P, 2 * P * PACK], BF16, f"qr_woven{v}")[:] for v in range(2)}
        qr_codes = [[held([P, 2 * P], U32, "qr_codes0_0")[:]],
                    [held([P, 2 * P], U32, "qr_codes1_0")[:]]]
        qr_scales = [[held([P, 2 * P], U8, f"qr_scales{h}_{v}") for v in range(2)] for h in range(HEADS)]

        def weave_queries(h, u, copy, rows=slice(0, P)):
            copy(q_woven[h][u].rearrange("p e s j -> p s j e")[:, rows],
                 q_raw[h][:].rearrange("p j (s t) -> p s j t", t=PACK)[:, rows, :, 2 * u : 2 * u + 2])

        def quantise_queries_along_d(h, u):
            quantise(q_woven[h][u].rearrange("p e s j -> p (e s j)"), E4M3,
                     qd_codes[h][:, half(u)], qd_scales[h, u])

        def turn_queries(h, v, bank):
            for t in range(PACK):
                words = q_woven[h][t // 2].rearrange("p e s j -> p (e s j)").bitcast(F32)
                nc.tensor.transpose(quarters(bank)[:, t, :], words[:, 2 * P * (t % 2) + v : 2 * P * (t % 2 + 1) : 2], ident[:])

        def weave_turned_queries(h, v, bank):
            nc.scalar.copy(qr_woven[h, v].rearrange("s (e p t) -> s e p t", e=2, t=PACK),
                           bank[:].bitcast(BF16).rearrange("s (t p e) -> s e p t", t=PACK, e=2))

        def turn_rounded_queries(rounded, v, bank):
            for e in range(2):
                words = rounded[2 * v + e].bitcast(F32)
                for u in range(2):
                    nc.tensor.transpose(quarters(bank)[:, 2 * e + u, :], words[:, u::2], ident[:])

        def weave_turned_words(v, bank, copy, target):
            qr_woven[SECOND, v] = target
            copy(qr_woven[SECOND, v].bitcast(F32).rearrange("s (e p u) -> s e p u", e=2, u=2),
                 bank[:].rearrange("s (e u p) -> s e p u", e=2, u=2))

        def quantise_queries_along_r(h, v):
            quantise(qr_woven[h, v], E4M3, qr_codes[h][v], qr_scales[h][v][:])

        for u in range(2):
            weave_queries(FIRST, u, (nc.vector.tensor_copy, nc.scalar.copy)[u])
            quantise_queries_along_d(FIRST, u)
        k_planes.append(held([P, TOKENS], F32, "k_plane2", "q_raw0"))
        nc.sync.dma_start(k_planes[2][:], k_hbm[2])
        for v in range(2):
            turn_queries(FIRST, v, banks[4 + v])
            weave_turned_queries(FIRST, v, banks[4 + v])

        ts_turned = quarters(banks[4])
        for b in range(PACK):
            nc.tensor.transpose(ts_turned[:, b, :], ts_slots[:, b * P : (b + 1) * P], ident[:])
        ts_cols = held([P, PACK], F32, "ts_cols")
        nc.scalar.copy(ts_cols[:], ts_turned[:, :, 0])

        k_rows = []
        both_woven = held([P, 2, HALF, PACK], BF16, "k_woven", "ts_runs")
        k_woven = [both_woven[:, a] for a in range(2)]
        half_lists = [offsets[:, a * HALF // 16 : (a + 1) * HALF // 16] for a in range(2)]
        for j in range(PACK):
            if j < 2:
                k_rows.append(held([P, SLOTS], BF16, f"k_row{j}", ("ts_window", "qr_woven0")[j]))
                nc.vector.tensor_copy(k_rows[j][:], k_planes[j][:].indirect(offsets[:]))
            elif j == 2:
                for a in range(2):
                    nc.vector.tensor_copy(k_woven[a][:, :, j], k_planes[j][:].indirect(half_lists[a]))
            else:
                last_half = held([P, HALF], BF16, "last_half")
                nc.vector.tensor_copy(k_woven[0][:, :, j], k_planes[j][:].indirect(half_lists[0]))
                nc.scalar.activation(last_half[:], k_planes[j][:].indirect(half_lists[1]), ACT.Copy)
                nc.vector.tensor_copy(k_woven[1][:, :, j], last_half[:])
            if j == 0:
                k_planes.append(held([P, TOKENS], F32, "k_plane3", "k_plane0"))
                nc.sync.dma_start(k_planes[-1][:], k_hbm[PACK - 1])
                quantise_queries_along_r(FIRST, 0)
            if j == 1:
                q_raw.append(held([P, PACK, R], F32, "q_raw1", "k_plane1"))
                nc.sync.dma_start(q_raw[SECOND][:], q2.rearrange("(p j) r -> p j r", j=PACK))
                for place in range(2):
                    nc.scalar.copy(both_woven[:, :, :, place].rearrange("p a i -> p (a i)"), k_rows[place][:])
            if j == 2:
                qr_codes[FIRST].append(held([P, 2 * P], U32, "qr_codes0_1")[:])
                quantise_queries_along_r(FIRST, 1)
            if j >= 2:
                dp_sb.append(held([P, PACK, SLOTS], F32, f"dp_sb{j - 2}", f"qr_woven{3 - j}"))
                nc.sync.dma_start(dp_sb[-1][:], (dp1, dp2)[j - 2].rearrange("(s t) i -> s t i", t=PACK))
        all_k_codes = held([P, SLOTS], U32, "k_codes", "k_plane0")
        all_k_scales = held([P, SLOTS], U8, "k_scales")
        for a in range(2):
            quantise(k_woven[a].rearrange("p i j -> p (i j)"), E4M3, all_k_codes[:, half(a)], all_k_scales[:, half(a)])

        neg_us = held([P, PACK], F32, "neg_us")
        nc.gpsimd.tensor_scalar(neg_us[:], us_sb[:], -1.0, 0.0, ALU.mult, ALU.add)
        direct_neg_us = held([P, 2], F32, "direct_neg_us")
        nc.gpsimd.tensor_scalar(direct_neg_us[:], us_sb[:, :2], -1.0, 0.0, ALU.mult, ALU.add)
        numerators = held([P, 2, TILES], F32, "numerators")
        for h in range(HEADS):
            nc.gpsimd.tensor_tensor(numerators[:, 0, PACK * h : PACK * (h + 1)], w_sb[h][:], us_sb[:], ALU.mult)
        nc.gpsimd.memset(numerators[:, 1, :], -1.0)
        side_by_side = held([P, 2, 4], F32, "side_by_side", "ts_window")
        nc.vector.memset(side_by_side[:, :, 2], -1.0)
        nc.vector.tensor_tensor(side_by_side[:, :, 0], w_sb[FIRST][:, 2:4], us_sb[:, 2:4], ALU.mult)

        weave_queries(SECOND, 0, nc.vector.tensor_copy)
        weave_queries(SECOND, 1, nc.vector.tensor_copy, slice(0, P // 4))
        quantise_queries_along_d(SECOND, 0)

        behind_weave = held([P, 4 * SLOTS], F32, "behind_weave", "second_woven0")
        first_scaled = held([P, 2, HALF], F32, "first_scaled")
        neg_z = [behind_weave[:, t * SLOTS : (t + 1) * SLOTS] for t in range(2)]
        neg_z = neg_z + [held([P, SLOTS], F32, f"neg_z{n}")[:] for n in range(2, TILES)]
        fourth = held([P, HALF + SLOTS], F32, "fourth")
        exps = [fourth[:, HALF:] if n == PACK - 1 else held([P, SLOTS], F32, f"e{n}")[:] for n in range(TILES)]
        neg_max = [held([P, 1], F32, f"neg_max{n}")[:] for n in range(TILES)]
        second_scaled = held([P, PACK * R], F32, "second_scaled")
        scaled = [[first_scaled[:, b, :] for b in range(2)] + [behind_weave[:, 3 * SLOTS + b * HALF : 3 * SLOTS + (b + 1) * HALF] for b in range(2)],
                  [second_scaled[:, b * R : (b + 1) * R] for b in range(PACK)]]
        products = [held([P, SLOTS], F32, f"products{n}")[:] for n in range(TILES)]
        totals = held([P, TILES], F32, "totals")
        last_scaled = scaled[SECOND][PACK - 1]
        early_row_sums = last_scaled[:, P : P + 2]
        late_row_sums = last_scaled[:, 3 * P + 8 : 3 * P + 8 + TILES]

        middle_row_sums = [held([P, 1], F32, f"row_sum{n}") for n in (2, 3)]

        def row_sums(first, count):
            if first in (2, 3):
                return middle_row_sums[first - 2][:]
            return (early_row_sums if first < 2 else late_row_sums)[:, first : first + count]

        inverses = [scaled[FIRST][PACK - 1][:, P : P + 2], side_by_side[:, :, 1::2], last_scaled[:, 3 * P : 3 * P + 2], dp_sb[FIRST][:, 2, 0:2]]
        factors = [last_scaled[:, 0:4].rearrange("p (k e) -> p k e", k=2)]
        factors.append(last_scaled[:, 2 * P : 2 * P + 4].rearrange("p (k e) -> p k e", k=2))
        factors = factors + [held([P, 2, 2], F32, f"factors{m}")[:] for m in range(2, PACK)]
        shifts = {n: held([P, 2], F32, f"shifts{n}")[:] for n in (2, 3, 4, 6)}

        def scores(target, stationary, stationary_scales, moving, moving_scales):
            nc.tensor.matmul_mx(out=target, lhsT=stationary.bitcast(E4M3), lhsT_scale=stationary_scales,
                                rhs=moving.bitcast(E4M3), rhs_scale=moving_scales, start=True, stop=True)

        def direct_rows(t, bank):
            scores(bank[:], qd_codes[FIRST][:, block(t)], first_qd_scales[:, block(t)], all_k_codes[:], all_k_scales[:])
            nc.vector.scalar_tensor_tensor(neg_z[t], bank[:], direct_neg_us[:, t : t + 1], ts_slots[:], ALU.mult, ALU.mult)

        def direct_maximum(t):
            nc.vector.tensor_reduce(neg_max[t], neg_z[t], mybir.AxisListType.X, ALU.min)

        def turned_scores(h, u, b, target):
            rows = half(u)
            scores(target, all_k_codes[:, block(b)], all_k_scales[:, block(b)], qd_codes[h][:, rows], qd_scales[h, u])

        def scale_turned(h, u, b, target):
            nc.scalar.activation(scaled[h][b] if h == FIRST else scaled[h][b][:, half(u)], target, ACT.Copy, scale=ts_cols[:, b : b + 1])

        def turned_rows(n, bank):
            h, t = divmod(n, PACK)
            for b in range(PACK):
                nc.tensor.transpose(bank[:, block(b)], scaled[h][b][:, block(t - 2 * (1 - h))], ident[:])
            nc.vector.tensor_scalar(neg_z[n], bank[:], neg_us[:, t : t + 1], None, ALU.mult, ALU.min, accum_out=neg_max[n])

        def exponentials(n):
            nc.scalar.activation(exps[n], neg_z[n], ACT.Exp, bias=neg_max[n], scale=-1.0, accum_out=totals[:, n : n + 1])

        def make_inverses(m):
            pair = totals[:, 2 * m : 2 * m + 2]
            nc.vector.reciprocal(inverses[m], pair.unsqueeze(2).to_broadcast([P, 2, 2]) if m == 1 else pair)

        def make_factors(m):
            if m == 1:
                nc.vector.tensor_reduce(factors[m].rearrange("p k e -> p e k"), side_by_side[:].rearrange("p e (k f) -> p e k f", f=2),
                                        mybir.AxisListType.X, ALU.mult)
                return
            nc.vector.tensor_tensor(factors[m], numerators[:, :, 2 * m : 2 * m + 2],
                                    inverses[m].unsqueeze(1).to_broadcast([P, 2, 2]), ALU.mult)

        def make_products(n):
            h, t = divmod(n, PACK)
            nc.vector.scalar_tensor_tensor(products[n], exps[n], factors[n // 2][:, 0, n % 2 : n % 2 + 1],
                                           dp_sb[h][:, t, :], ALU.mult, ALU.mult, accum_out=row_sums(n, 1))

        def make_shifts(first, count):
            if first in (2, 3):
                nc.scalar.activation(shifts[first][:, :1], row_sums(first, 1), ACT.Copy, scale=factors[1][:, 1, first - 2 : first - 1])
                return
            nc.vector.tensor_tensor(shifts[first][:, :count], row_sums(first, count),
                                    factors[first // 2][:, 1, first % 2 : first % 2 + count], ALU.mult)

        def shift(n):
            return shifts[n][:, 0:1] if n in shifts else shifts[n - 1][:, 1:2]

        g_woven = {(FIRST, 0): held([P, HALF, PACK], BF16, "g_woven0_0")[:]}
        means = [held([P, SLOTS], F32, f"means{t}")[:] for t in range(PACK - 1)]
        final_means = [held([P, HALF], F32, f"final_means{a}")[:] for a in range(2)]
        first_turned = held([P, 2 * R], BF16, "first_turned")
        turned = [first_turned[:, b * R : (b + 1) * R].rearrange("i (u s e) -> i u s e", u=2, e=2) for b in range(2)]
        turn_banks = banks[4:8]

        def mean_term(t, columns, target):
            nc.scalar.activation(target, exps[t][:, columns], ACT.Copy, scale=shift(t))

        def early_mean_term(t):
            nc.gpsimd.tensor_scalar(means[t], exps[t], row_sums(t, 1), factors[0][:, 1, t : t + 1], ALU.mult, ALU.mult)

        def turn_term(t, opens, blocks):
            for b in blocks:
                mean = means[t][:, block(b)] if t < PACK - 1 else final_means[b // 2][:, block(b % 2)]
                term = products[t][:, block(b)] if opens else mean
                nc.tensor.matmul(quarters(turn_banks[b])[:, t, :], term, ident[:],
                                 start=opens and t == 0, stop=not opens and t == PACK - 1, is_transpose=True)

        def round_turned(b):
            nc.scalar.activation(turned[b], quarters(turn_banks[b]).rearrange("i (u e) s -> i u s e", e=2), ACT.Copy,
                                 scale=ts_cols[:, b : b + 1])

        def turn_back(a, bank):
            for c in range(2):
                words = turned[2 * a + c].rearrange("p a b c -> p (a b c)").bitcast(F32)
                for u in range(2):
                    nc.tensor.transpose(halves(bank)[:, u, block(c)], words[:, block(u)], ident[:])

        def return_gradient(a, bank, copy):
            target = g_woven[FIRST, a].rearrange("s i t -> s (i t)").bitcast(F32).rearrange("s (i u) -> s i u", u=2)
            copy(target, halves(bank).rearrange("s u i -> s i u"))

        def centre(t, columns, target):
            n = PACK + t
            nc.vector.scalar_tensor_tensor(target, exps[n][:, columns], shift(n), products[n][:, columns], ALU.mult, ALU.add)

        def last_block_term(t, opens, bank, last_means):
            n = PACK + t
            term = products[n][:, block(PACK - 1)]
            if not opens:
                term = last_means[:, t, :]
                nc.scalar.activation(term, exps[n][:, block(PACK - 1)], ACT.Copy, scale=shift(n))
            nc.tensor.matmul(quarters(bank)[:, t, :], term, ident[:], start=opens and t == 0,
                             stop=not opens and t == PACK - 1, is_transpose=True)

        def last_block_round(bank, words):
            nc.scalar.activation(words[:], quarters(bank).rearrange("i (u e) s -> i u s e", e=2), ACT.Copy,
                                 scale=ts_cols[:, PACK - 1 : PACK])

        def last_block_back(words, back):
            for u in range(2):
                nc.tensor.transpose(back[:, block(u)], words[:].rearrange("p a b c -> p (a b c)").bitcast(F32)[:, block(u)], ident[:])

        def last_block_return(back):
            target = g_woven[SECOND, 1][:, P:, :].rearrange("s i t -> s (i t)").bitcast(F32).rearrange("s (i u) -> s i u", u=2)
            nc.scalar.copy(target, back.rearrange("s (u i) -> s i u", u=2))

        def weave_centred(columns, source, target):
            ts_lines = ts_slots[:, columns].rearrange("p (c i) -> p c i", i=LINE).unsqueeze(2)
            nc.vector.tensor_tensor(target.rearrange("p (c i) t -> p c t i", i=LINE),
                                    source.rearrange("p t (c i) -> p c t i", i=LINE),
                                    ts_lines.to_broadcast([P, (columns.stop - columns.start) // LINE, PACK, LINE]), ALU.mult)

        g_codes, g_scales = {}, {}

        def quantise_gradient(h, a, tag=None):
            g_codes[h, a] = held([P, HALF], U32, f"g_codes{h}_{a}", tag)[:]
            g_scales[h, a] = held([P, HALF], U8, f"g_scales{h}_{a}")[:]
            quantise(g_woven[h, a].rearrange("p i t -> p (i t)"), E5M2, g_codes[h, a], g_scales[h, a])

        def key_gradient_pass(target, j, h, a, opens):
            nc.tensor.matmul_mx(out=target, lhsT=qr_codes[h][j // 2][:, block(j % 2)].bitcast(E4M3),
                                lhsT_scale=qr_scales[h][j // 2][:, block(j % 2)],
                                rhs=g_codes[h, a].bitcast(E5M2), rhs_scale=g_scales[h, a],
                                start=opens, stop=not opens)

        def sums(j, a, target):
            opener = FIRST if j == 0 else SECOND
            for h in (opener, 1 - opener):
                key_gradient_pass(target, j, h, a, h == opener)
            return target

        def vector_scatter(j, a, source):
            dk = held([P, HALF], F32, f"dk{j}_{a}")
            nc.vector.tensor_copy(dk[:], source)
            nc.vector.tensor_copy(windows[j][:].indirect(half_lists[a]), dk[:])

        def scalar_scatter(j, a, source):
            dk = held([P, HALF], F32, f"dk{j}_{a}")
            nc.scalar.copy(dk[:], source)
            nc.scalar.activation(windows[j][:].indirect(half_lists[a]), dk[:], ACT.Copy)

        out_planes = out.rearrange("(p j) c -> j p c", j=PACK)

        def turned_pair(h, u, pair):
            for b in range(PACK):
                turned_scores(h, u, b, pair[b // 2][:, half(b % 2)])
            for b in range(PACK):
                scale_turned(h, u, b, pair[b // 2][:, half(b % 2)])

        for t in range(2):
            direct_rows(t, banks[t])
        turned_pair(FIRST, 1, banks[6:8])
        rounded = []

        def round_queries(v, target):
            nc.gpsimd.tensor_scalar(target, q_raw[SECOND][:, 2 * v : 2 * v + 2, :], 1.0, 0.0, ALU.mult, ALU.add)
            rounded.extend(target[:, e, :] for e in range(2))

        weave_queries(SECOND, 1, nc.scalar.copy, slice(P // 4, P))
        round_queries(0, behind_weave[:, 2 * SLOTS : 3 * SLOTS].bitcast(BF16).rearrange("p (e r) -> p e r", e=2))
        turned_pair(SECOND, 0, banks[2:4])
        direct_maximum(0)
        qd_scales[SECOND, 1] = held([P, HALF], U8, "second_qd_scales1", "direct_neg_us")[:]
        quantise_queries_along_d(SECOND, 1)
        direct_maximum(1)
        round_queries(1, held([P, 2, R], BF16, "rounded", "second_woven1")[:])
        zero_window(PACK - 1, "k_plane1")
        for n in range(2, PACK):
            turned_rows(n, banks[n - 2])
        for n in range(2):
            exponentials(n)
        turned_pair(SECOND, 1, banks[6:8])
        make_inverses(0)
        turned_rows(4, banks[4])
        make_factors(0)
        turned_rows(5, banks[5])
        for v in range(2):
            turn_rounded_queries(rounded, v, banks[2 + v])
        exponentials(2)
        exponentials(3)
        make_products(0)
        make_products(1)
        make_inverses(1)
        early_mean_term(0)
        early_mean_term(1)
        turned_rows(6, banks[0])
        make_factors(1)
        turned_rows(7, banks[1])
        for n in range(PACK, TILES):
            exponentials(n)
        zero_window(2, "neg_z7")
        make_inverses(2)
        make_products(2)
        make_factors(2)
        make_products(3)
        make_inverses(3)
        make_products(4)
        make_factors(3)

        make_shifts(2, 1)
        weave_turned_words(1, banks[3], nc.scalar.copy, held([P, 2 * P * PACK], BF16, "second_qr_woven1", "neg_z6")[:])
        make_shifts(3, 1)
        mean_term(2, slice(0, SLOTS), means[2])
        for a in range(2):
            mean_term(PACK - 1, half(a), final_means[a])
        weave_turned_words(0, banks[2], nc.scalar.copy, fourth[:, :SLOTS].bitcast(BF16))
        early, late = range(2), range(2, PACK)
        for opens in (True, False):
            for t in range(2):
                turn_term(t, opens, range(PACK))
        for t in range(2, PACK):
            turn_term(t, True, early)
        turn_term(2, True, late)
        for t in range(2, PACK):
            turn_term(t, False, early)
        turn_term(3, True, late)
        for t in range(2, PACK):
            turn_term(t, False, late)
        make_products(5)
        make_products(6)
        make_shifts(4, 2)
        make_products(7)
        for b in range(2):
            round_turned(b)
        centred = held([P, PACK, HALF], F32, "centred")
        centre(0, half(0), centred[:, 0, :])
        make_shifts(6, 2)
        turn_back(0, banks[0])
        return_gradient(0, banks[0], nc.scalar.copy)
        last_means = held([P, PACK, P], F32, "last_means", "final_means0")
        for opens in (True, False):
            for t in range(PACK):
                last_block_term(t, opens, banks[2], last_means)
        behind_return = held([P, 4 * R], BF16, "behind_return", "first_turned")
        for b in range(2, PACK):
            turned.append(behind_return[:, (b - 2) * R : (b - 1) * R].rearrange("i (u s e) -> i u s e", u=2, e=2))
            round_turned(b)
        g_woven[FIRST, 1] = held([P, HALF, PACK], BF16, "g_woven0_1")[:]
        turn_back(1, banks[1])
        last_turned = held([P, 2, P, 2], BF16, "last_turned")
        last_block_round(banks[2], last_turned)
        last_block_back(last_turned, banks[3][:, half(0)])
        return_gradient(1, banks[1], nc.scalar.copy)
        for t in range(1, PACK):
            centre(t, half(0), centred[:, t, :])
        g_woven[SECOND, 0] = behind_return[:, 2 * R :].rearrange("s (i t) -> s i t", t=PACK)
        weave_centred(half(0), centred[:], g_woven[SECOND, 0])
        quantise_queries_along_r(SECOND, 0)
        quantise_gradient(FIRST, 0)
        quantise_gradient(SECOND, 0)
        g_woven[SECOND, 1] = held([P, HALF, PACK], BF16, "g_woven1_1", "last_turned")[:]
        later_centred = held([P, PACK, P], F32, "later_centred", "g_woven0_0")[:]
        last_block_return(banks[3][:, half(0)])

        early_sums = [held([P, HALF], F32, "dk0_0")]
        nc.scalar.copy(early_sums[0][:], sums(0, 0, banks[7][:, half(1)]))
        nc.scalar.activation(windows[0][:].indirect(half_lists[0]), early_sums[0][:], ACT.Copy)
        sums(1, 0, banks[2][:, half(0)])
        for t in range(PACK):
            centre(t, block(2), later_centred[:, t, :])
        quantise_gradient(FIRST, 1, "first_turned")
        key_gradient_pass(banks[6][:, half(0)], 0, FIRST, 1, True)
        weave_centred(block(2), later_centred, g_woven[SECOND, 1][:, :P, :])
        quantise_gradient(SECOND, 1)
        key_gradient_pass(banks[6][:, half(0)], 0, SECOND, 1, False)
        qr_codes[SECOND].append(held([P, 2 * P], U32, "qr_codes1_1", "g_woven0_1")[:])
        quantise_queries_along_r(SECOND, 1)
        early_sums.append(held([P, HALF], F32, "dk1_0", "last_turned"))
        nc.vector.tensor_copy(early_sums[1][:], banks[2][:, half(0)])
        nc.scalar.activation(windows[1][:].indirect(half_lists[0]), early_sums[1][:], ACT.Copy)
        late_sums = [held([P, HALF], F32, f"dk{j}_1") for j in range(2)]
        nc.vector.tensor_copy(late_sums[0][:], banks[6][:, half(0)])
        nc.vector.tensor_copy(late_sums[1][:], sums(1, 1, banks[7][:, half(0)]))
        for j in range(2):
            nc.vector.tensor_copy(windows[j][:].indirect(half_lists[1]), late_sums[j][:])
            nc.sync.dma_start(out_planes[j], windows[j][:])
        for j in range(2, PACK):
            scalar_scatter(j, 0, sums(j, 0, banks[4 + j][:, half(1)]))
        for j in range(2, PACK):
            vector_scatter(j, 1, sums(j, 1, banks[2 + j][:, half(0)]))
            nc.sync.dma_start(out_planes[j], windows[j][:])
